import numpy as np
import ml_dtypes


def mxq(x, axis, fmt="e4m3"):
    dtype, down = {"e4m3": (ml_dtypes.float8_e4m3fn, 7), "e5m2": (ml_dtypes.float8_e5m2, 14)}[fmt]
    v = np.moveaxis(np.asarray(x, np.float32).astype(ml_dtypes.bfloat16).astype(np.float64), axis, -1)
    blocks = v.reshape(v.shape[:-1] + (-1, 32))
    amax = np.abs(blocks).max(-1, keepdims=True)
    byte = np.maximum(np.where(amax > 0, np.frexp(amax)[1] - 1 + 127, 0) - down, 1)
    scale = np.exp2(byte - 127.0)
    codes = (blocks / scale).astype(np.float32).astype(dtype).astype(np.float64)
    return np.moveaxis((codes * scale).reshape(v.shape), -1, axis)


WIDE = False


def mx_kscale(k):
    if not WIDE:
        return np.ones(k)
    levels = np.array([24, -24, 12, -12, 0])
    if k % 512:
        return np.exp2(np.random.permutation(np.resize(levels, k // 32))).repeat(32)
    a = np.empty((k // 512, 16))
    for p in range(k // 512):
        a[p, :8] = np.random.permutation(np.resize(levels, 8))
        for g in range(8):
            far = levels[np.abs(levels - a[p, g]) >= 10]
            a[p, g + 8] = far[np.random.randint(len(far))]
    return np.exp2(a.ravel()).repeat(32)


def f64(x):
    return np.asarray(x).astype(np.float64)


def striped(idx):
    return np.tile(idx.reshape(-1, 16).T, (8, 1)).astype(np.uint16)


def unstriped(offs):
    return offs[:16].T.reshape(-1).astype(np.int64)


E2M1 = np.array([0.0, 0.5, 1.0, 1.5, 2.0, 3.0, 4.0, 6.0, -0.0, -0.5, -1.0, -1.5, -2.0, -3.0, -4.0, -6.0])


def pack_weight(w, fmt):
    k, n = w.shape
    w = f64(np.asarray(w, np.float32).astype(ml_dtypes.bfloat16)).reshape(k // 32, 32, n)
    amax = np.abs(w).max(1)
    if fmt == "e4m3":
        byte = np.frexp(amax)[1] - 1 + 127 - 7
    else:
        mant, ex = np.frexp(amax / 6.0)
        byte = np.where(mant > 0.5, ex, ex - 1) + 127
    byte = np.clip(np.where(amax > 0, byte, 1), 1, 254)
    scaled = (w * np.exp2(127.0 - byte)[:, None, :]).reshape(k, n).astype(np.float32)
    by_word = np.ascontiguousarray(scaled.reshape(k // 512, 128, 4, n).transpose(0, 1, 3, 2))
    if fmt == "e4m3":
        words = by_word.astype(ml_dtypes.float8_e4m3fn).view(np.uint8)
    else:
        c = by_word.astype(ml_dtypes.float4_e2m1fn).view(np.uint8) & 0xF
        words = (c[..., 0::2] | (c[..., 1::2] << 4)).reshape(k // 512, 128, 2 * n)
    return np.ascontiguousarray(words), np.ascontiguousarray(byte.astype(np.uint8).reshape(k // 512, 16, n))


def unpack_weight(words, scales, fmt):
    g, _, n = scales.shape
    words = np.ascontiguousarray(words).reshape(g, 128, n, -1)
    if fmt == "e4m3":
        vals = words.view(ml_dtypes.float8_e4m3fn).astype(np.float64)
    else:
        nib = np.empty((g, 128, n, 4), np.uint8)
        nib[..., 0::2] = words & 0xF
        nib[..., 1::2] = words >> 4
        vals = E2M1[nib]
    vals = vals * np.repeat(np.exp2(scales.astype(np.float64) - 127.0), 8, axis=1)[..., None]
    return vals.transpose(0, 1, 3, 2).reshape(g * 512, n)


def pack_table4(v):
    words, scales = pack_weight(v, "e2m1")
    g, t = words.shape[0] // 2, v.shape[1]
    return np.ascontiguousarray(words.reshape(g, 2, 128, t, 2).transpose(0, 2, 3, 1, 4).reshape(g, 128, t, 4)), scales


def unpack_table4(words, scales):
    g, _, t, _ = words.shape
    return unpack_weight(words.reshape(g, 128, t, 2, 2).transpose(0, 3, 1, 2, 4).reshape(2 * g, 128, 2 * t), scales, "e2m1")


K, F, N, T, J = 1024, 512, 256, 4096, 2048


def setup_inputs():
    n = np.random.standard_normal
    s = mx_kscale(K)[:, None]
    u = mx_kscale(F)[:, None]
    p_tab = pack_table4(n((K, T)) * s)
    p_co = pack_weight(n((K, F)) / np.sqrt(K) / s, "e2m1")
    p_si = pack_weight(n((K, F)) / np.sqrt(K) / s, "e2m1")
    p_fb = pack_weight(np.abs(n((F, N))) / F / u, "e2m1")
    return {
        "tab_words": p_tab[0],
        "tab_scales": p_tab[1],
        "co_words": p_co[0],
        "co_scales": p_co[1],
        "si_words": p_si[0],
        "si_scales": p_si[1],
        "gn": (np.random.uniform(0.5, 2.0, F) * u[:, 0]).astype(np.float32),
        "fb_words": p_fb[0],
        "fb_scales": p_fb[1],
        "ts": np.tile(np.exp(0.5 * n(T)), (128, 1)).astype(np.float32),
        "offs": striped(np.random.permutation(T)[:J]),
    }


def reference(tab_words, tab_scales, co_words, co_scales, si_words, si_scales, gn, fb_words, fb_scales, ts, offs):
    idx = unstriped(offs)
    tab_ = unpack_table4(tab_words, tab_scales)[:, idx]
    co_ = unpack_weight(co_words, co_scales, "e2m1")
    si_ = unpack_weight(si_words, si_scales, "e2m1")
    re = co_.T @ tab_
    im = si_.T @ tab_
    h = f64(gn)[:, None] * ((re) ** 2 + (im) ** 2)
    h_ = mxq(h, 0, "e4m3")
    fb_ = unpack_weight(fb_words, fb_scales, "e2m1")
    y = fb_.T @ h_
    return y * f64(ts)[0, idx][None, :]

@@ -1,0 +1,253 @@
+from contextlib import ExitStack
+
+import concourse.mybir as mybir
+from concourse.masks import make_identity
+
+K, F, N, T, J = 1024, 512, 256, 4096, 2048
+FLOPS = 2 * J * (2 * K * F + F * N)
+
+F32 = mybir.dt.float32
+BF16 = mybir.dt.bfloat16
+I32 = mybir.dt.int32
+U32 = mybir.dt.uint32
+U16 = mybir.dt.uint16
+U8 = mybir.dt.uint8
+FP8X4 = mybir.dt.float8_e4m3fn_x4
+FP4X4 = mybir.dt.float4_e2m1fn_x4
+ALU = mybir.AluOpType
+ACT = mybir.ActivationFunctionType
+
+P = 128
+PACK = 4
+PASSES = K // (P * PACK)
+GROUP = 16
+CHUNK = 512
+SCALE_CHUNK = 1024
+BLOCKS = [(0, 512), (512, 512), (1024, 512), (1536, 256), (1792, 256)]
+PIECE = 256
+SUM_PIECE = 128
+SIGN_COLS = 128
+BANK = 512
+SHIFT = 16
+SHIFTED = P - SHIFT
+TINY = 2.0**-110
+
+
+def tile_list_meltab_gain_kernel(
+    tc, tab_words, tab_scales, co_words, co_scales, si_words, si_scales, gn, fb_words, fb_scales, ts, offs, out
+):
+    nc = tc.nc
+    with ExitStack() as ctx:
+        keep = ctx.enter_context(tc.tile_pool(name="keep", bufs=1))
+        work = ctx.enter_context(tc.tile_pool(name="work", bufs=2))
+        dft_psum = ctx.enter_context(tc.psum_pool(name="dft_psum", bufs=5))
+        sign_psum = ctx.enter_context(tc.psum_pool(name="sign_psum", bufs=1))
+        mel_psum = ctx.enter_context(tc.psum_pool(name="mel_psum", bufs=2))
+
+        offsets = keep.tile([P, J // GROUP], U16, name="offsets")
+        nc.sync.dma_start(offsets[:], offs)
+
+        def listed(j0, width):
+            return offsets[:, j0 // GROUP : (j0 + width) // GROUP]
+
+        gain = keep.tile([P, PACK], F32, name="gain")
+        nc.sync.dma_start(gain[:], gn.rearrange("(p t) -> p t", t=PACK))
+
+        scale_table = keep.tile([P, T // 4], I32, name="scale_table", tag="then_filters", align_bytes=64)
+        nc.vector.memset(scale_table[:], 0)
+        w_scales_raw = keep.tile([P, 2, PASSES, F // 4], I32, name="w_scales_raw", tag="then_levels", align_bytes=64)
+        nc.vector.memset(w_scales_raw[:], 0)
+        scale_pass1 = keep.tile([P, J // 4], I32, name="scale_pass1", align_bytes=64)
+        nc.vector.memset(scale_pass1[:], 0)
+
+        for r in range(4):
+            nc.sync.dma_start(
+                scale_table[r:P:SHIFT, :], tab_scales[:, r:16:4, :].rearrange("a q t -> q a t").bitcast(I32)
+            )
+        w_words_raw = keep.tile([P, 2, PASSES, F // 2], I32, name="w_words_raw", align_bytes=64)
+        for part, words in enumerate((co_words, si_words)):
+            nc.scalar.dma_start(w_words_raw[:, part], words.rearrange("a p b -> p a b").bitcast(I32))
+        gain_neg = keep.tile([P, PACK], F32, name="gain_neg", tag="then_words", align_bytes=64)
+        nc.vector.tensor_scalar(gain_neg[:], gain[:], -1.0, TINY, ALU.mult, ALU.max)
+        gain_pos = keep.tile([P, PACK], F32, name="gain_pos")
+        nc.vector.tensor_tensor(gain_pos[:], gain_neg[:], gain[:], ALU.max)
+        word_table = keep.tile([P, T], I32, name="word_table", tag="then_words", align_bytes=64)
+        nc.sync.dma_start(word_table[:], tab_words[0].rearrange("p t b -> p (t b)").bitcast(I32))
+        for part, (scales, queue) in enumerate(((co_scales, nc.scalar), (si_scales, nc.gpsimd))):
+            for q in range(4):
+                queue.dma_start(
+                    w_scales_raw[32 * q : 32 * q + 4, part],
+                    scales[:, 4 * q : 4 * q + 4, :].rearrange("a r f -> r a f").bitcast(I32),
+                )
+
+        gain_sign = keep.tile([P, PACK], F32, name="gain_sign")
+        nc.scalar.activation(gain_sign[:], gain[:], ACT.Sign)
+        root0 = keep.tile([P, PACK], F32, name="root0")
+        nc.scalar.activation(root0[:], gain_pos[:], ACT.Sqrt)
+        root0_inv = keep.tile([P, PACK], F32, name="root0_inv")
+        nc.vector.reciprocal(root0_inv[:], root0[:])
+        quot = keep.tile([P, PACK], F32, name="quot")
+        nc.gpsimd.tensor_tensor(quot[:], gain_pos[:], root0_inv[:], ALU.mult)
+        root_sum = keep.tile([P, PACK], F32, name="root_sum")
+        nc.gpsimd.tensor_tensor(root_sum[:], quot[:], root0[:], ALU.add)
+        root = keep.tile([P, PACK], F32, name="root")
+        nc.gpsimd.tensor_scalar(root[:], root_sum[:], 0.5, None, ALU.mult)
+        sign_rows = keep.tile([P, SIGN_COLS // PACK, PACK], BF16, name="sign_rows")
+        nc.scalar.copy(sign_rows[:], gain_sign[:].unsqueeze(1).to_broadcast([P, SIGN_COLS // PACK, PACK]))
+        identity = keep.tile([P, P], BF16, name="identity")
+        make_identity(nc, identity[:])
+        flipped_bank = mel_psum.tile([P, P], BF16, name="flipped_bank", tag="mel_bank")
+        nc.tensor.transpose(flipped_bank[:], sign_rows[:].rearrange("p c t -> p (c t)"), identity[:])
+        flipped = keep.tile([P, P], BF16, name="flipped")
+        nc.scalar.copy(flipped[:], flipped_bank[:])
+        signs = sign_psum.tile([P, SIGN_COLS], BF16, name="signs")
+        nc.tensor.transpose(signs[:], flipped[:], identity[:])
+
+        w_words = keep.tile([P, 2, PASSES, 2 * F], U8, name="w_words", align_bytes=64)
+        w_scales = keep.tile([P, 2, PASSES, F], U8, name="w_scales", align_bytes=64)
+        for part in range(2):
+            nc.vector.tensor_copy(
+                w_words[:, part].bitcast(U16).rearrange("p a (t m) -> p a t m", t=PACK),
+                w_words_raw[:, part].bitcast(U16).rearrange("p a (m t) -> p a t m", t=PACK),
+            )
+
+        scale_pass0 = {}
+
+        def gather_scales(j0):
+            picked = keep.tile([P, SCALE_CHUNK], U8, name="picked_scales%d" % j0, align_bytes=64)
+            nc.vector.tensor_copy(picked[:], scale_table[:].bitcast(U8).indirect(listed(j0, SCALE_CHUNK)))
+            nc.scalar.dma_start(
+                scale_pass1[0:SHIFTED, j0 // 4 : (j0 + SCALE_CHUNK) // 4], picked[SHIFT:P, :].bitcast(I32)
+            )
+            scale_pass0[j0] = picked
+
+        frames = {}
+
+        def gather_words(j0):
+            picked = work.tile([P, CHUNK], U32, name="picked_words")
+            nc.vector.tensor_copy(picked[:], word_table[:].bitcast(U32).indirect(listed(j0, CHUNK)))
+            parted = keep.tile([P, PASSES, 2 * CHUNK], U8, name="frames%d" % j0, align_bytes=64)
+            nc.vector.tensor_copy(
+                parted[:].bitcast(U16), picked[:].bitcast(U16).rearrange("p (n a) -> p a n", a=PASSES)
+            )
+            frames[j0] = parted
+
+        picked_levels = {}
+
+        def gather_levels(j0):
+            picked = keep.tile([P, CHUNK], F32, name="picked_levels%d" % j0)
+            nc.vector.tensor_copy(picked[:], levels[:].indirect(listed(j0, CHUNK)))
+            picked_levels[j0] = picked
+
+        def transform(j0, width):
+            c0 = j0 % CHUNK
+            s0 = j0 % SCALE_CHUNK
+            words = frames[j0 - c0]
+            planes = (
+                scale_pass0[j0 - s0][:, s0 : s0 + width],
+                scale_pass1[:].bitcast(U8)[:, j0 : j0 + width],
+            )
+            squares = work.tile([P, 2, PACK, width], F32, name="squares", bufs=3)
+            per_bank = BANK // width
+            for t in range(PACK):
+                for part in range(2):
+                    if part % per_bank == 0:
+                        bank = dft_psum.tile([P, per_bank, width], F32, name="dft_bank")
+                    for a in range(PASSES):
+                        nc.tensor.matmul_mx(
+                            out=bank[:, part % per_bank, :],
+                            lhsT=w_words[:, part, a, 2 * P * t : 2 * P * (t + 1)].bitcast(FP4X4),
+                            lhsT_scale=w_scales[:, part, a, P * t : P * (t + 1)],
+                            rhs=words[:, a, 2 * c0 : 2 * (c0 + width)].bitcast(FP4X4),
+                            rhs_scale=planes[a],
+                            start=(a == 0),
+                            stop=(a == PASSES - 1),
+                        )
+                    if part % per_bank == per_bank - 1:
+                        nc.scalar.activation(
+                            squares[:, part + 1 - per_bank : part + 1, t, :], bank[:], ACT.Square,
+                            scale=root[:, t : t + 1],
+                        )
+            return squares
+
+        def filter_bank(j0, width, squares):
+            pieces = range(0, width, PIECE)
+            power = work.tile([P, width * PACK], BF16, name="power", align_bytes=64)
+            signed = work.tile([P, width * PACK], BF16, name="signed", align_bytes=64)
+            codes = work.tile([P, width], U32, name="codes", align_bytes=64)
+            scales = work.tile([P, width], U8, name="scales", align_bytes=64)
+            adder = nc.vector if j0 + width == J else nc.gpsimd
+            for n0 in range(0, width, SUM_PIECE):
+                adder.tensor_tensor(
+                    power[:, PACK * n0 : PACK * (n0 + SUM_PIECE)].rearrange("p (c i t) -> p c t i", i=2, t=PACK),
+                    squares[:, 0, :, n0 : n0 + SUM_PIECE].rearrange("p t (c i) -> p c t i", i=2),
+                    squares[:, 1, :, n0 : n0 + SUM_PIECE].rearrange("p t (c i) -> p c t i", i=2),
+                    ALU.add,
+                )
+            for n0 in pieces:
+                cols = slice(PACK * n0, PACK * (n0 + PIECE))
+                nc.vector.tensor_tensor(
+                    signed[:, cols].rearrange("p (r c) -> p r c", c=SIGN_COLS),
+                    power[:, cols].rearrange("p (r c) -> p r c", c=SIGN_COLS),
+                    signs[:].unsqueeze(1).to_broadcast([P, PIECE * PACK // SIGN_COLS, SIGN_COLS]),
+                    ALU.mult,
+                )
+            for n0 in pieces:
+                nc.vector.quantize_mx(
+                    out=codes[:, n0 : n0 + PIECE].bitcast(FP8X4),
+                    scales=scales[:, n0 : n0 + PIECE],
+                    in_=signed[:, PACK * n0 : PACK * (n0 + PIECE)],
+                )
+            c0 = j0 % CHUNK
+            level = picked_levels[j0 - c0][:, c0 : c0 + width]
+            result = work.tile([P, N // P, width], F32, name="result", bufs=3)
+            per_bank = BANK // width
+            for half in range(N // P):
+                if half % per_bank == 0:
+                    bank = mel_psum.tile([P, per_bank, width], F32, name="mel_bank", tag="mel_bank")
+                nc.tensor.matmul_mx(
+                    out=bank[:, half % per_bank, :],
+                    lhsT=fb_codes.bitcast(U8)[:, 2 * P * half : 2 * P * (half + 1)].bitcast(FP4X4),
+                    lhsT_scale=fb_scale.bitcast(U8)[:, P * half : P * (half + 1)],
+                    rhs=codes[:].bitcast(FP8X4),
+                    rhs_scale=scales[:],
+                    start=True,
+                    stop=True,
+                )
+                if half % per_bank == per_bank - 1:
+                    nc.vector.tensor_tensor(
+                        result[:, half + 1 - per_bank : half + 1, :],
+                        bank[:],
+                        level.unsqueeze(1).to_broadcast([P, per_bank, width]),
+                        ALU.mult,
+                    )
+            nc.sync.dma_start(out[:, j0 : j0 + width].rearrange("(h p) j -> p h j", p=P), result[:])
+
+        gather_scales(0)
+        for part in range(2):
+            nc.vector.tensor_copy(
+                w_scales[:, part].rearrange("p a (t m) -> p a t m", t=PACK),
+                w_scales_raw[:, part].bitcast(U8).rearrange("p a (m t) -> p a t m", t=PACK),
+            )
+        levels = keep.tile([P, T], F32, name="levels", tag="then_levels", align_bytes=64)
+        nc.sync.dma_start(levels[:], ts)
+        gather_words(0)
+        gather_scales(SCALE_CHUNK)
+        filters = keep.tile([P, N // 2 + N // 4], I32, name="filters", tag="then_filters", align_bytes=64)
+        fb_codes, fb_scale = filters[:, 0 : N // 2], filters[:, N // 2 :]
+        nc.gpsimd.memset(fb_scale, 0)
+        nc.sync.dma_start(fb_codes, fb_words[0].bitcast(I32))
+        for q in range(4):
+            nc.sync.dma_start(fb_scale[32 * q : 32 * q + 4, :], fb_scales[0, 4 * q : 4 * q + 4, :].bitcast(I32))
+        gather_words(CHUNK)
+        pending = None
+        for j0, width in BLOCKS:
+            squares = transform(j0, width)
+            if j0 % CHUNK == 0:
+                if j0 + 2 * CHUNK < J:
+                    gather_words(j0 + 2 * CHUNK)
+                gather_levels(j0)
+            if pending is not None:
+                filter_bank(*pending)
+            pending = (j0, width, squares)
+        filter_bank(*pending)

@@ -24,9 +24,13 @@ GROUP = 16
 CHUNK = 512
 SCALE_CHUNK = 1024
 BLOCKS = [(0, 512), (512, 512), (1024, 512), (1536, 256), (1792, 256)]
-PIECE = 256
-SUM_PIECE = 128
+TURNED_UNTIL = 1536
 SIGN_COLS = 128
+ORDER = [
+    ("transform", 0), ("transform", 1), ("quantize", 0), ("filter", 0), ("transform", 2), ("quantize", 1),
+    ("transform", 3), ("filter", 1), ("quantize", 2), ("transform", 4), ("filter", 2), ("quantize", 3),
+    ("filter", 3), ("quantize", 4), ("filter", 4),
+]
 BANK = 512
 SHIFT = 16
 SHIFTED = P - SHIFT
@@ -40,9 +44,8 @@ def tile_list_meltab_gain_kernel(
     with ExitStack() as ctx:
         keep = ctx.enter_context(tc.tile_pool(name="keep", bufs=1))
         work = ctx.enter_context(tc.tile_pool(name="work", bufs=2))
-        dft_psum = ctx.enter_context(tc.psum_pool(name="dft_psum", bufs=5))
-        sign_psum = ctx.enter_context(tc.psum_pool(name="sign_psum", bufs=1))
-        mel_psum = ctx.enter_context(tc.psum_pool(name="mel_psum", bufs=2))
+        dft_psum = ctx.enter_context(tc.psum_pool(name="dft_psum", bufs=4))
+        mel_psum = ctx.enter_context(tc.psum_pool(name="mel_psum", bufs=4))
 
         offsets = keep.tile([P, J // GROUP], U16, name="offsets")
         nc.sync.dma_start(offsets[:], offs)
@@ -53,9 +56,9 @@ def tile_list_meltab_gain_kernel(
         gain = keep.tile([P, PACK], F32, name="gain")
         nc.sync.dma_start(gain[:], gn.rearrange("(p t) -> p t", t=PACK))
 
-        scale_table = keep.tile([P, T // 4], I32, name="scale_table", tag="then_filters", align_bytes=64)
+        scale_table = keep.tile([P, T // 4], I32, name="scale_table", tag="then_levels", align_bytes=64)
         nc.vector.memset(scale_table[:], 0)
-        w_scales_raw = keep.tile([P, 2, PASSES, F // 4], I32, name="w_scales_raw", tag="then_levels", align_bytes=64)
+        w_scales_raw = keep.tile([P, 2, PASSES, F // 4], I32, name="w_scales_raw", tag="then_filters", align_bytes=64)
         nc.vector.memset(w_scales_raw[:], 0)
         scale_pass1 = keep.tile([P, J // 4], I32, name="scale_pass1", align_bytes=64)
         nc.vector.memset(scale_pass1[:], 0)
@@ -66,20 +69,19 @@ def tile_list_meltab_gain_kernel(
             )
         w_words_raw = keep.tile([P, 2, PASSES, F // 2], I32, name="w_words_raw", align_bytes=64)
         for part, words in enumerate((co_words, si_words)):
-            nc.scalar.dma_start(w_words_raw[:, part], words.rearrange("a p b -> p a b").bitcast(I32))
+            nc.sync.dma_start(w_words_raw[:, part], words.rearrange("a p b -> p a b").bitcast(I32))
+        for part, scales in enumerate((co_scales, si_scales)):
+            for q in range(4):
+                nc.sync.dma_start(
+                    w_scales_raw[32 * q : 32 * q + 4, part],
+                    scales[:, 4 * q : 4 * q + 4, :].rearrange("a r f -> r a f").bitcast(I32),
+                )
         gain_neg = keep.tile([P, PACK], F32, name="gain_neg", tag="then_words", align_bytes=64)
         nc.vector.tensor_scalar(gain_neg[:], gain[:], -1.0, TINY, ALU.mult, ALU.max)
         gain_pos = keep.tile([P, PACK], F32, name="gain_pos")
         nc.vector.tensor_tensor(gain_pos[:], gain_neg[:], gain[:], ALU.max)
         word_table = keep.tile([P, T], I32, name="word_table", tag="then_words", align_bytes=64)
         nc.sync.dma_start(word_table[:], tab_words[0].rearrange("p t b -> p (t b)").bitcast(I32))
-        for part, (scales, queue) in enumerate(((co_scales, nc.scalar), (si_scales, nc.gpsimd))):
-            for q in range(4):
-                queue.dma_start(
-                    w_scales_raw[32 * q : 32 * q + 4, part],
-                    scales[:, 4 * q : 4 * q + 4, :].rearrange("a r f -> r a f").bitcast(I32),
-                )
-
         gain_sign = keep.tile([P, PACK], F32, name="gain_sign")
         nc.scalar.activation(gain_sign[:], gain[:], ACT.Sign)
         root0 = keep.tile([P, PACK], F32, name="root0")
@@ -92,16 +94,11 @@ def tile_list_meltab_gain_kernel(
         nc.gpsimd.tensor_tensor(root_sum[:], quot[:], root0[:], ALU.add)
         root = keep.tile([P, PACK], F32, name="root")
         nc.gpsimd.tensor_scalar(root[:], root_sum[:], 0.5, None, ALU.mult)
-        sign_rows = keep.tile([P, SIGN_COLS // PACK, PACK], BF16, name="sign_rows")
-        nc.scalar.copy(sign_rows[:], gain_sign[:].unsqueeze(1).to_broadcast([P, SIGN_COLS // PACK, PACK]))
-        identity = keep.tile([P, P], BF16, name="identity")
+        signs = keep.tile([P, SIGN_COLS // PACK, PACK], BF16, name="signs")
+        nc.scalar.copy(signs[:], gain_sign[:].unsqueeze(1).to_broadcast([P, SIGN_COLS // PACK, PACK]))
+
+        identity = keep.tile([P, P], F32, name="identity")
         make_identity(nc, identity[:])
-        flipped_bank = mel_psum.tile([P, P], BF16, name="flipped_bank", tag="mel_bank")
-        nc.tensor.transpose(flipped_bank[:], sign_rows[:].rearrange("p c t -> p (c t)"), identity[:])
-        flipped = keep.tile([P, P], BF16, name="flipped")
-        nc.scalar.copy(flipped[:], flipped_bank[:])
-        signs = sign_psum.tile([P, SIGN_COLS], BF16, name="signs")
-        nc.tensor.transpose(signs[:], flipped[:], identity[:])
 
         w_words = keep.tile([P, 2, PASSES, 2 * F], U8, name="w_words", align_bytes=64)
         w_scales = keep.tile([P, 2, PASSES, F], U8, name="w_scales", align_bytes=64)
@@ -133,11 +130,19 @@ def tile_list_meltab_gain_kernel(
             frames[j0] = parted
 
         picked_levels = {}
+        level_columns = {}
 
         def gather_levels(j0):
             picked = keep.tile([P, CHUNK], F32, name="picked_levels%d" % j0)
             nc.vector.tensor_copy(picked[:], levels[:].indirect(listed(j0, CHUNK)))
             picked_levels[j0] = picked
+            if j0 < TURNED_UNTIL:
+                bank = mel_psum.tile([P, CHUNK // P, P], F32, name="level_bank", tag="mel_bank")
+                for i in range(CHUNK // P):
+                    nc.tensor.transpose(bank[:, i, :], picked[:, P * i : P * (i + 1)], identity[:])
+                column = keep.tile([P, CHUNK // P], F32, name="level_columns%d" % j0)
+                nc.scalar.copy(column[:], bank[:, :, 0])
+                level_columns[j0] = column
 
         def transform(j0, width):
             c0 = j0 % CHUNK
@@ -170,43 +175,49 @@ def tile_list_meltab_gain_kernel(
                         )
             return squares
 
-        def filter_bank(j0, width, squares):
-            pieces = range(0, width, PIECE)
+        def quantize_power(width, squares):
+            piece = width // 2
+            pieces = (0, piece)
             power = work.tile([P, width * PACK], BF16, name="power", align_bytes=64)
             signed = work.tile([P, width * PACK], BF16, name="signed", align_bytes=64)
-            codes = work.tile([P, width], U32, name="codes", align_bytes=64)
-            scales = work.tile([P, width], U8, name="scales", align_bytes=64)
-            adder = nc.vector if j0 + width == J else nc.gpsimd
-            for n0 in range(0, width, SUM_PIECE):
-                adder.tensor_tensor(
-                    power[:, PACK * n0 : PACK * (n0 + SUM_PIECE)].rearrange("p (c i t) -> p c t i", i=2, t=PACK),
-                    squares[:, 0, :, n0 : n0 + SUM_PIECE].rearrange("p t (c i) -> p c t i", i=2),
-                    squares[:, 1, :, n0 : n0 + SUM_PIECE].rearrange("p t (c i) -> p c t i", i=2),
+            codes = work.tile([P, width], U32, name="codes", align_bytes=64, bufs=3)
+            scales = work.tile([P, width], U8, name="scales", align_bytes=64, bufs=3)
+            for n0 in pieces:
+                nc.vector.tensor_tensor(
+                    power[:, PACK * n0 : PACK * (n0 + piece)].rearrange("p (c i t) -> p c t i", i=2, t=PACK),
+                    squares[:, 0, :, n0 : n0 + piece].rearrange("p t (c i) -> p c t i", i=2),
+                    squares[:, 1, :, n0 : n0 + piece].rearrange("p t (c i) -> p c t i", i=2),
                     ALU.add,
                 )
             for n0 in pieces:
-                cols = slice(PACK * n0, PACK * (n0 + PIECE))
+                cols = slice(PACK * n0, PACK * (n0 + piece))
                 nc.vector.tensor_tensor(
                     signed[:, cols].rearrange("p (r c) -> p r c", c=SIGN_COLS),
                     power[:, cols].rearrange("p (r c) -> p r c", c=SIGN_COLS),
-                    signs[:].unsqueeze(1).to_broadcast([P, PIECE * PACK // SIGN_COLS, SIGN_COLS]),
+                    signs[:].rearrange("p c t -> p (c t)").unsqueeze(1).to_broadcast(
+                        [P, piece * PACK // SIGN_COLS, SIGN_COLS]
+                    ),
                     ALU.mult,
                 )
             for n0 in pieces:
                 nc.vector.quantize_mx(
-                    out=codes[:, n0 : n0 + PIECE].bitcast(FP8X4),
-                    scales=scales[:, n0 : n0 + PIECE],
-                    in_=signed[:, PACK * n0 : PACK * (n0 + PIECE)],
+                    out=codes[:, n0 : n0 + piece].bitcast(FP8X4),
+                    scales=scales[:, n0 : n0 + piece],
+                    in_=signed[:, PACK * n0 : PACK * (n0 + piece)],
                 )
+            return codes, scales
+
+        def store(j0, width, result):
+            nc.sync.dma_start(out[:, j0 : j0 + width].rearrange("(h p) j -> p h j", p=P), result[:])
+
+        def filter_bank(j0, width, codes, scales):
             c0 = j0 % CHUNK
             level = picked_levels[j0 - c0][:, c0 : c0 + width]
             result = work.tile([P, N // P, width], F32, name="result", bufs=3)
-            per_bank = BANK // width
+            bank = mel_psum.tile([P, N // P, width], F32, name="mel_bank", tag="mel_bank")
             for half in range(N // P):
-                if half % per_bank == 0:
-                    bank = mel_psum.tile([P, per_bank, width], F32, name="mel_bank", tag="mel_bank")
                 nc.tensor.matmul_mx(
-                    out=bank[:, half % per_bank, :],
+                    out=bank[:, half, :],
                     lhsT=fb_codes.bitcast(U8)[:, 2 * P * half : 2 * P * (half + 1)].bitcast(FP4X4),
                     lhsT_scale=fb_scale.bitcast(U8)[:, P * half : P * (half + 1)],
                     rhs=codes[:].bitcast(FP8X4),
@@ -214,14 +225,41 @@ def tile_list_meltab_gain_kernel(
                     start=True,
                     stop=True,
                 )
-                if half % per_bank == per_bank - 1:
-                    nc.vector.tensor_tensor(
-                        result[:, half + 1 - per_bank : half + 1, :],
-                        bank[:],
-                        level.unsqueeze(1).to_broadcast([P, per_bank, width]),
-                        ALU.mult,
+            nc.vector.tensor_tensor(
+                result[:], bank[:], level.unsqueeze(1).to_broadcast([P, N // P, width]), ALU.mult
+            )
+            store(j0, width, result)
+
+        def filter_bank_turned(j0, width, codes, scales):
+            for n0 in range(0, width, 2 * P):
+                by_frame = work.tile([P, 2, N], F32, name="by_frame", bufs=3)
+                bank = mel_psum.tile([P, 2, N], F32, name="frame_bank", tag="mel_bank")
+                for i in range(2):
+                    cols = slice(n0 + P * i, n0 + P * (i + 1))
+                    nc.tensor.matmul_mx(
+                        out=bank[:, i, :],
+                        lhsT=codes[:, cols].bitcast(FP8X4),
+                        lhsT_scale=scales[:, cols],
+                        rhs=fb_codes.bitcast(U8).bitcast(FP4X4),
+                        rhs_scale=fb_scale.bitcast(U8),
+                        start=True,
+                        stop=True,
                     )
-            nc.sync.dma_start(out[:, j0 : j0 + width].rearrange("(h p) j -> p h j", p=P), result[:])
+                for i in range(2):
+                    tile_in_chunk = n0 // P + i
+                    nc.scalar.activation(
+                        by_frame[:, i, :], bank[:, i, :], ACT.Copy,
+                        scale=level_columns[j0][:, tile_in_chunk : tile_in_chunk + 1],
+                    )
+                turned = mel_psum.tile([P, N // P, 2 * P], F32, name="turned_bank", tag="mel_bank")
+                for i in range(2):
+                    for half in range(N // P):
+                        nc.tensor.transpose(
+                            turned[:, half, P * i : P * (i + 1)], by_frame[:, i, P * half : P * (half + 1)], identity[:]
+                        )
+                result = work.tile([P, N // P, 2 * P], F32, name="result", bufs=3)
+                nc.scalar.copy(result[:], turned[:])
+                store(j0 + n0, 2 * P, result)
 
         gather_scales(0)
         for part in range(2):
@@ -229,25 +267,28 @@ def tile_list_meltab_gain_kernel(
                 w_scales[:, part].rearrange("p a (t m) -> p a t m", t=PACK),
                 w_scales_raw[:, part].bitcast(U8).rearrange("p a (m t) -> p a t m", t=PACK),
             )
-        levels = keep.tile([P, T], F32, name="levels", tag="then_levels", align_bytes=64)
-        nc.sync.dma_start(levels[:], ts)
-        gather_words(0)
         gather_scales(SCALE_CHUNK)
+        gather_words(0)
+        levels = keep.tile([P, T], F32, name="levels", tag="then_levels", align_bytes=64)
         filters = keep.tile([P, N // 2 + N // 4], I32, name="filters", tag="then_filters", align_bytes=64)
         fb_codes, fb_scale = filters[:, 0 : N // 2], filters[:, N // 2 :]
         nc.gpsimd.memset(fb_scale, 0)
         nc.sync.dma_start(fb_codes, fb_words[0].bitcast(I32))
         for q in range(4):
             nc.sync.dma_start(fb_scale[32 * q : 32 * q + 4, :], fb_scales[0, 4 * q : 4 * q + 4, :].bitcast(I32))
+        nc.sync.dma_start(levels[:], ts)
         gather_words(CHUNK)
-        pending = None
-        for j0, width in BLOCKS:
-            squares = transform(j0, width)
-            if j0 % CHUNK == 0:
-                if j0 + 2 * CHUNK < J:
-                    gather_words(j0 + 2 * CHUNK)
-                gather_levels(j0)
-            if pending is not None:
-                filter_bank(*pending)
-            pending = (j0, width, squares)
-        filter_bank(*pending)
+        squares = {}
+        quantized = {}
+        for step, b in ORDER:
+            j0, width = BLOCKS[b]
+            if step == "transform":
+                squares[b] = transform(j0, width)
+                if j0 % CHUNK == 0:
+                    if j0 + 2 * CHUNK < J:
+                        gather_words(j0 + 2 * CHUNK)
+                    gather_levels(j0)
+            elif step == "quantize":
+                quantized[b] = quantize_power(width, squares[b])
+            else:
+                (filter_bank_turned if j0 < TURNED_UNTIL else filter_bank)(j0, width, *quantized[b])

@@ -24,11 +24,11 @@ GROUP = 16
 CHUNK = 512
 SCALE_CHUNK = 1024
 BLOCKS = [(0, 512), (512, 512), (1024, 512), (1536, 256), (1792, 256)]
-TURNED_UNTIL = 1536
+TURNED_UNTIL = 1024
 SIGN_COLS = 128
 ORDER = [
-    ("transform", 0), ("transform", 1), ("quantize", 0), ("filter", 0), ("transform", 2), ("quantize", 1),
-    ("transform", 3), ("filter", 1), ("quantize", 2), ("transform", 4), ("filter", 2), ("quantize", 3),
+    ("transform", 0), ("transform", 1), ("quantize", 0), ("transform", 2), ("filter", 0), ("quantize", 1),
+    ("transform", 3), ("quantize", 2), ("transform", 4), ("filter", 1), ("filter", 2), ("quantize", 3),
     ("filter", 3), ("quantize", 4), ("filter", 4),
 ]
 BANK = 512
@@ -56,10 +56,18 @@ def tile_list_meltab_gain_kernel(
         gain = keep.tile([P, PACK], F32, name="gain")
         nc.sync.dma_start(gain[:], gn.rearrange("(p t) -> p t", t=PACK))
 
-        scale_table = keep.tile([P, T // 4], I32, name="scale_table", tag="then_levels", align_bytes=64)
+        scale_table = keep.tile([P, T // 4], I32, name="scale_table", tag="then_filters", align_bytes=64)
         nc.vector.memset(scale_table[:], 0)
-        w_scales_raw = keep.tile([P, 2, PASSES, F // 4], I32, name="w_scales_raw", tag="then_filters", align_bytes=64)
-        nc.vector.memset(w_scales_raw[:], 0)
+
+        def load_weight_scales(scales):
+            raw = keep.tile([P, PASSES, F // 4], I32, name="w_scales_raw", tag="then_levels", align_bytes=64)
+            nc.vector.memset(raw[:], 0)
+            for q in range(4):
+                nc.sync.dma_start(
+                    raw[32 * q : 32 * q + 4], scales[:, 4 * q : 4 * q + 4, :].rearrange("a r f -> r a f").bitcast(I32)
+                )
+            return raw
+
         scale_pass1 = keep.tile([P, J // 4], I32, name="scale_pass1", align_bytes=64)
         nc.vector.memset(scale_pass1[:], 0)
 
@@ -70,12 +78,7 @@ def tile_list_meltab_gain_kernel(
         w_words_raw = keep.tile([P, 2, PASSES, F // 2], I32, name="w_words_raw", align_bytes=64)
         for part, words in enumerate((co_words, si_words)):
             nc.sync.dma_start(w_words_raw[:, part], words.rearrange("a p b -> p a b").bitcast(I32))
-        for part, scales in enumerate((co_scales, si_scales)):
-            for q in range(4):
-                nc.sync.dma_start(
-                    w_scales_raw[32 * q : 32 * q + 4, part],
-                    scales[:, 4 * q : 4 * q + 4, :].rearrange("a r f -> r a f").bitcast(I32),
-                )
+        co_scales_raw = load_weight_scales(co_scales)
         gain_neg = keep.tile([P, PACK], F32, name="gain_neg", tag="then_words", align_bytes=64)
         nc.vector.tensor_scalar(gain_neg[:], gain[:], -1.0, TINY, ALU.mult, ALU.max)
         gain_pos = keep.tile([P, PACK], F32, name="gain_pos")
@@ -121,7 +124,7 @@ def tile_list_meltab_gain_kernel(
         frames = {}
 
         def gather_words(j0):
-            picked = work.tile([P, CHUNK], U32, name="picked_words")
+            picked = work.tile([P, CHUNK], U32, name="picked_words", bufs=1)
             nc.vector.tensor_copy(picked[:], word_table[:].bitcast(U32).indirect(listed(j0, CHUNK)))
             parted = keep.tile([P, PASSES, 2 * CHUNK], U8, name="frames%d" % j0, align_bytes=64)
             nc.vector.tensor_copy(
@@ -154,8 +157,12 @@ def tile_list_meltab_gain_kernel(
             )
             squares = work.tile([P, 2, PACK, width], F32, name="squares", bufs=3)
             per_bank = BANK // width
-            for t in range(PACK):
-                for part in range(2):
+            if per_bank == 1:
+                order = [(t, part) for part in range(2) for t in range(PACK)]
+            else:
+                order = [(t, part) for t in range(PACK) for part in range(2)]
+            for t, part in order:
+                if True:
                     if part % per_bank == 0:
                         bank = dft_psum.tile([P, per_bank, width], F32, name="dft_bank")
                     for a in range(PASSES):
@@ -180,8 +187,8 @@ def tile_list_meltab_gain_kernel(
             pieces = (0, piece)
             power = work.tile([P, width * PACK], BF16, name="power", align_bytes=64)
             signed = work.tile([P, width * PACK], BF16, name="signed", align_bytes=64)
-            codes = work.tile([P, width], U32, name="codes", align_bytes=64, bufs=3)
-            scales = work.tile([P, width], U8, name="scales", align_bytes=64, bufs=3)
+            codes = work.tile([P, width], U32, name="codes", align_bytes=64, bufs=4)
+            scales = work.tile([P, width], U8, name="scales", align_bytes=64, bufs=4)
             for n0 in pieces:
                 nc.vector.tensor_tensor(
                     power[:, PACK * n0 : PACK * (n0 + piece)].rearrange("p (c i t) -> p c t i", i=2, t=PACK),
@@ -214,10 +221,12 @@ def tile_list_meltab_gain_kernel(
             c0 = j0 % CHUNK
             level = picked_levels[j0 - c0][:, c0 : c0 + width]
             result = work.tile([P, N // P, width], F32, name="result", bufs=3)
-            bank = mel_psum.tile([P, N // P, width], F32, name="mel_bank", tag="mel_bank")
+            per_bank = BANK // width
             for half in range(N // P):
+                if half % per_bank == 0:
+                    bank = mel_psum.tile([P, per_bank, width], F32, name="mel_bank", tag="mel_bank")
                 nc.tensor.matmul_mx(
-                    out=bank[:, half, :],
+                    out=bank[:, half % per_bank, :],
                     lhsT=fb_codes.bitcast(U8)[:, 2 * P * half : 2 * P * (half + 1)].bitcast(FP4X4),
                     lhsT_scale=fb_scale.bitcast(U8)[:, P * half : P * (half + 1)],
                     rhs=codes[:].bitcast(FP8X4),
@@ -225,9 +234,13 @@ def tile_list_meltab_gain_kernel(
                     start=True,
                     stop=True,
                 )
-            nc.vector.tensor_tensor(
-                result[:], bank[:], level.unsqueeze(1).to_broadcast([P, N // P, width]), ALU.mult
-            )
+                if half % per_bank == per_bank - 1:
+                    nc.vector.tensor_tensor(
+                        result[:, half + 1 - per_bank : half + 1, :],
+                        bank[:],
+                        level.unsqueeze(1).to_broadcast([P, per_bank, width]),
+                        ALU.mult,
+                    )
             store(j0, width, result)
 
         def filter_bank_turned(j0, width, codes, scales):
@@ -261,21 +274,25 @@ def tile_list_meltab_gain_kernel(
                 nc.scalar.copy(result[:], turned[:])
                 store(j0 + n0, 2 * P, result)
 
-        gather_scales(0)
-        for part in range(2):
+        def order_scales(part, raw):
             nc.vector.tensor_copy(
                 w_scales[:, part].rearrange("p a (t m) -> p a t m", t=PACK),
-                w_scales_raw[:, part].bitcast(U8).rearrange("p a (m t) -> p a t m", t=PACK),
+                raw[:].bitcast(U8).rearrange("p a (m t) -> p a t m", t=PACK),
             )
+
+        gather_scales(0)
+        order_scales(0, co_scales_raw)
+        si_scales_raw = load_weight_scales(si_scales)
         gather_scales(SCALE_CHUNK)
         gather_words(0)
-        levels = keep.tile([P, T], F32, name="levels", tag="then_levels", align_bytes=64)
+        order_scales(1, si_scales_raw)
         filters = keep.tile([P, N // 2 + N // 4], I32, name="filters", tag="then_filters", align_bytes=64)
         fb_codes, fb_scale = filters[:, 0 : N // 2], filters[:, N // 2 :]
         nc.gpsimd.memset(fb_scale, 0)
         nc.sync.dma_start(fb_codes, fb_words[0].bitcast(I32))
         for q in range(4):
             nc.sync.dma_start(fb_scale[32 * q : 32 * q + 4, :], fb_scales[0, 4 * q : 4 * q + 4, :].bitcast(I32))
+        levels = keep.tile([P, T], F32, name="levels", tag="then_levels", align_bytes=64)
         nc.sync.dma_start(levels[:], ts)
         gather_words(CHUNK)
         squares = {}

@@ -24,7 +24,7 @@ GROUP = 16
 CHUNK = 512
 SCALE_CHUNK = 1024
 BLOCKS = [(0, 512), (512, 512), (1024, 512), (1536, 256), (1792, 256)]
-TURNED_UNTIL = 1024
+TURNED_UNTIL = 1536
 SIGN_COLS = 128
 ORDER = [
     ("transform", 0), ("transform", 1), ("quantize", 0), ("transform", 2), ("filter", 0), ("quantize", 1),
@@ -45,7 +45,8 @@ def tile_list_meltab_gain_kernel(
         keep = ctx.enter_context(tc.tile_pool(name="keep", bufs=1))
         work = ctx.enter_context(tc.tile_pool(name="work", bufs=2))
         dft_psum = ctx.enter_context(tc.psum_pool(name="dft_psum", bufs=4))
-        mel_psum = ctx.enter_context(tc.psum_pool(name="mel_psum", bufs=4))
+        mel_psum = ctx.enter_context(tc.psum_pool(name="mel_psum", bufs=1))
+        turn_psum = ctx.enter_context(tc.psum_pool(name="turn_psum", bufs=3))
 
         offsets = keep.tile([P, J // GROUP], U16, name="offsets")
         nc.sync.dma_start(offsets[:], offs)
@@ -140,7 +141,7 @@ def tile_list_meltab_gain_kernel(
             nc.vector.tensor_copy(picked[:], levels[:].indirect(listed(j0, CHUNK)))
             picked_levels[j0] = picked
             if j0 < TURNED_UNTIL:
-                bank = mel_psum.tile([P, CHUNK // P, P], F32, name="level_bank", tag="mel_bank")
+                bank = turn_psum.tile([P, CHUNK // P, P], F32, name="level_bank", tag="turn_bank")
                 for i in range(CHUNK // P):
                     nc.tensor.transpose(bank[:, i, :], picked[:, P * i : P * (i + 1)], identity[:])
                 column = keep.tile([P, CHUNK // P], F32, name="level_columns%d" % j0)
@@ -246,7 +247,7 @@ def tile_list_meltab_gain_kernel(
         def filter_bank_turned(j0, width, codes, scales):
             for n0 in range(0, width, 2 * P):
                 by_frame = work.tile([P, 2, N], F32, name="by_frame", bufs=3)
-                bank = mel_psum.tile([P, 2, N], F32, name="frame_bank", tag="mel_bank")
+                bank = turn_psum.tile([P, 2, N], F32, name="frame_bank", tag="turn_bank")
                 for i in range(2):
                     cols = slice(n0 + P * i, n0 + P * (i + 1))
                     nc.tensor.matmul_mx(
@@ -264,7 +265,7 @@ def tile_list_meltab_gain_kernel(
                         by_frame[:, i, :], bank[:, i, :], ACT.Copy,
                         scale=level_columns[j0][:, tile_in_chunk : tile_in_chunk + 1],
                     )
-                turned = mel_psum.tile([P, N // P, 2 * P], F32, name="turned_bank", tag="mel_bank")
+                turned = turn_psum.tile([P, N // P, 2 * P], F32, name="turned_bank", tag="turn_bank")
                 for i in range(2):
                     for half in range(N // P):
                         nc.tensor.transpose(

@@ -24,11 +24,11 @@ GROUP = 16
 CHUNK = 512
 SCALE_CHUNK = 1024
 BLOCKS = [(0, 512), (512, 512), (1024, 512), (1536, 256), (1792, 256)]
-TURNED_UNTIL = 1536
+TURNED_UNTIL = 1024
 SIGN_COLS = 128
 ORDER = [
     ("transform", 0), ("transform", 1), ("quantize", 0), ("transform", 2), ("filter", 0), ("quantize", 1),
-    ("transform", 3), ("quantize", 2), ("transform", 4), ("filter", 1), ("filter", 2), ("quantize", 3),
+    ("transform", 3), ("quantize", 2), ("transform", 4), ("filter", 2), ("filter", 1), ("quantize", 3),
     ("filter", 3), ("quantize", 4), ("filter", 4),
 ]
 BANK = 512
@@ -45,8 +45,8 @@ def tile_list_meltab_gain_kernel(
         keep = ctx.enter_context(tc.tile_pool(name="keep", bufs=1))
         work = ctx.enter_context(tc.tile_pool(name="work", bufs=2))
         dft_psum = ctx.enter_context(tc.psum_pool(name="dft_psum", bufs=4))
-        mel_psum = ctx.enter_context(tc.psum_pool(name="mel_psum", bufs=1))
-        turn_psum = ctx.enter_context(tc.psum_pool(name="turn_psum", bufs=3))
+        mel_psum = ctx.enter_context(tc.psum_pool(name="mel_psum", bufs=2))
+        turn_psum = ctx.enter_context(tc.psum_pool(name="turn_psum", bufs=2))
 
         offsets = keep.tile([P, J // GROUP], U16, name="offsets")
         nc.sync.dma_start(offsets[:], offs)
@@ -124,14 +124,16 @@ def tile_list_meltab_gain_kernel(
 
         frames = {}
 
-        def gather_words(j0):
-            picked = work.tile([P, CHUNK], U32, name="picked_words", bufs=1)
-            nc.vector.tensor_copy(picked[:], word_table[:].bitcast(U32).indirect(listed(j0, CHUNK)))
-            parted = keep.tile([P, PASSES, 2 * CHUNK], U8, name="frames%d" % j0, align_bytes=64)
-            nc.vector.tensor_copy(
-                parted[:].bitcast(U16), picked[:].bitcast(U16).rearrange("p (n a) -> p a n", a=PASSES)
-            )
-            frames[j0] = parted
+        def gather_words(j0, chunks):
+            picked = work.tile([P, chunks * CHUNK], U32, name="picked_words", bufs=1)
+            nc.vector.tensor_copy(picked[:], word_table[:].bitcast(U32).indirect(listed(j0, chunks * CHUNK)))
+            for c0 in range(0, chunks * CHUNK, CHUNK):
+                parted = keep.tile([P, PASSES, 2 * CHUNK], U8, name="frames%d" % (j0 + c0), align_bytes=64)
+                nc.vector.tensor_copy(
+                    parted[:].bitcast(U16),
+                    picked[:, c0 : c0 + CHUNK].bitcast(U16).rearrange("p (n a) -> p a n", a=PASSES),
+                )
+                frames[j0 + c0] = parted
 
         picked_levels = {}
         level_columns = {}
@@ -192,9 +194,9 @@ def tile_list_meltab_gain_kernel(
             scales = work.tile([P, width], U8, name="scales", align_bytes=64, bufs=4)
             for n0 in pieces:
                 nc.vector.tensor_tensor(
-                    power[:, PACK * n0 : PACK * (n0 + piece)].rearrange("p (c i t) -> p c t i", i=2, t=PACK),
-                    squares[:, 0, :, n0 : n0 + piece].rearrange("p t (c i) -> p c t i", i=2),
-                    squares[:, 1, :, n0 : n0 + piece].rearrange("p t (c i) -> p c t i", i=2),
+                    power[:, PACK * n0 : PACK * (n0 + piece)].rearrange("p (c i t) -> p c t i", i=4, t=PACK),
+                    squares[:, 0, :, n0 : n0 + piece].rearrange("p t (c i) -> p c t i", i=4),
+                    squares[:, 1, :, n0 : n0 + piece].rearrange("p t (c i) -> p c t i", i=4),
                     ALU.add,
                 )
             for n0 in pieces:
@@ -271,7 +273,7 @@ def tile_list_meltab_gain_kernel(
                         nc.tensor.transpose(
                             turned[:, half, P * i : P * (i + 1)], by_frame[:, i, P * half : P * (half + 1)], identity[:]
                         )
-                result = work.tile([P, N // P, 2 * P], F32, name="result", bufs=3)
+                result = work.tile([P, N // P, 2 * P], F32, name="turned_result", bufs=3)
                 nc.scalar.copy(result[:], turned[:])
                 store(j0 + n0, 2 * P, result)
 
@@ -285,7 +287,7 @@ def tile_list_meltab_gain_kernel(
         order_scales(0, co_scales_raw)
         si_scales_raw = load_weight_scales(si_scales)
         gather_scales(SCALE_CHUNK)
-        gather_words(0)
+        gather_words(0, 1)
         order_scales(1, si_scales_raw)
         filters = keep.tile([P, N // 2 + N // 4], I32, name="filters", tag="then_filters", align_bytes=64)
         fb_codes, fb_scale = filters[:, 0 : N // 2], filters[:, N // 2 :]
@@ -295,7 +297,7 @@ def tile_list_meltab_gain_kernel(
             nc.sync.dma_start(fb_scale[32 * q : 32 * q + 4, :], fb_scales[0, 4 * q : 4 * q + 4, :].bitcast(I32))
         levels = keep.tile([P, T], F32, name="levels", tag="then_levels", align_bytes=64)
         nc.sync.dma_start(levels[:], ts)
-        gather_words(CHUNK)
+        gather_words(CHUNK, 2)
         squares = {}
         quantized = {}
         for step, b in ORDER:
@@ -303,8 +305,8 @@ def tile_list_meltab_gain_kernel(
             if step == "transform":
                 squares[b] = transform(j0, width)
                 if j0 % CHUNK == 0:
-                    if j0 + 2 * CHUNK < J:
-                        gather_words(j0 + 2 * CHUNK)
+                    if j0 == 0:
+                        gather_words(3 * CHUNK, 1)
                     gather_levels(j0)
             elif step == "quantize":
                 quantized[b] = quantize_power(width, squares[b])

@@ -1,7 +1,6 @@
 from contextlib import ExitStack
 
 import concourse.mybir as mybir
-from concourse.masks import make_identity
 
 K, F, N, T, J = 1024, 512, 256, 4096, 2048
 FLOPS = 2 * J * (2 * K * F + F * N)
@@ -22,18 +21,14 @@ PACK = 4
 PASSES = K // (P * PACK)
 GROUP = 16
 CHUNK = 512
-SCALE_CHUNK = 1024
-BLOCKS = [(0, 512), (512, 512), (1024, 512), (1536, 256), (1792, 256)]
-TURNED_UNTIL = 1024
-SIGN_COLS = 128
-ORDER = [
-    ("transform", 0), ("transform", 1), ("quantize", 0), ("transform", 2), ("filter", 0), ("quantize", 1),
-    ("transform", 3), ("quantize", 2), ("transform", 4), ("filter", 2), ("filter", 1), ("quantize", 3),
-    ("filter", 3), ("quantize", 4), ("filter", 4),
-]
-BANK = 512
+UNIT = 256
+UNITS = J // UNIT
+SCALE_CHUNKS = [(0, 512), (512, 1536)]
 SHIFT = 16
 SHIFTED = P - SHIFT
+ROUTES = ["S","S","S","S","A","A","A","A"]
+TURNED = []
+SIGN_COLS = 128
 TINY = 2.0**-110
 
 
@@ -43,10 +38,13 @@ def tile_list_meltab_gain_kernel(
     nc = tc.nc
     with ExitStack() as ctx:
         keep = ctx.enter_context(tc.tile_pool(name="keep", bufs=1))
+        staged = ctx.enter_context(tc.tile_pool(name="staged", bufs=1))
+        chain = ctx.enter_context(tc.tile_pool(name="chain", bufs=1))
+        behind = ctx.enter_context(tc.tile_pool(name="behind", bufs=1))
+        early = ctx.enter_context(tc.tile_pool(name="early", bufs=1))
         work = ctx.enter_context(tc.tile_pool(name="work", bufs=2))
-        dft_psum = ctx.enter_context(tc.psum_pool(name="dft_psum", bufs=4))
-        mel_psum = ctx.enter_context(tc.psum_pool(name="mel_psum", bufs=2))
-        turn_psum = ctx.enter_context(tc.psum_pool(name="turn_psum", bufs=2))
+        dft_psum = ctx.enter_context(tc.psum_pool(name="dft_psum", bufs=3))
+        aux_psum = ctx.enter_context(tc.psum_pool(name="aux_psum", bufs=5))
 
         offsets = keep.tile([P, J // GROUP], U16, name="offsets")
         nc.sync.dma_start(offsets[:], offs)
@@ -54,261 +52,307 @@ def tile_list_meltab_gain_kernel(
         def listed(j0, width):
             return offsets[:, j0 // GROUP : (j0 + width) // GROUP]
 
-        gain = keep.tile([P, PACK], F32, name="gain")
-        nc.sync.dma_start(gain[:], gn.rearrange("(p t) -> p t", t=PACK))
+        w_words = []
+        for part, words in enumerate((co_words, si_words)):
+            tile = early.tile([P, PASSES, 2 * F], U8, name="w_words%d" % part, align_bytes=64, offset=4 * F * part)
+            nc.sync.dma_start(tile[:].bitcast(I32), words.rearrange("a p b -> p a b").bitcast(I32))
+            w_words.append(tile)
 
-        scale_table = keep.tile([P, T // 4], I32, name="scale_table", tag="then_filters", align_bytes=64)
+        scale_table = staged.tile([P, T // 4], I32, name="scale_table", offset=0)
         nc.vector.memset(scale_table[:], 0)
-
-        def load_weight_scales(scales):
-            raw = keep.tile([P, PASSES, F // 4], I32, name="w_scales_raw", tag="then_levels", align_bytes=64)
-            nc.vector.memset(raw[:], 0)
-            for q in range(4):
-                nc.sync.dma_start(
-                    raw[32 * q : 32 * q + 4], scales[:, 4 * q : 4 * q + 4, :].rearrange("a r f -> r a f").bitcast(I32)
-                )
-            return raw
-
-        scale_pass1 = keep.tile([P, J // 4], I32, name="scale_pass1", align_bytes=64)
-        nc.vector.memset(scale_pass1[:], 0)
-
         for r in range(4):
             nc.sync.dma_start(
                 scale_table[r:P:SHIFT, :], tab_scales[:, r:16:4, :].rearrange("a q t -> q a t").bitcast(I32)
             )
-        w_words_raw = keep.tile([P, 2, PASSES, F // 2], I32, name="w_words_raw", align_bytes=64)
-        for part, words in enumerate((co_words, si_words)):
-            nc.sync.dma_start(w_words_raw[:, part], words.rearrange("a p b -> p a b").bitcast(I32))
-        co_scales_raw = load_weight_scales(co_scales)
-        gain_neg = keep.tile([P, PACK], F32, name="gain_neg", tag="then_words", align_bytes=64)
-        nc.vector.tensor_scalar(gain_neg[:], gain[:], -1.0, TINY, ALU.mult, ALU.max)
-        gain_pos = keep.tile([P, PACK], F32, name="gain_pos")
-        nc.vector.tensor_tensor(gain_pos[:], gain_neg[:], gain[:], ALU.max)
-        word_table = keep.tile([P, T], I32, name="word_table", tag="then_words", align_bytes=64)
-        nc.sync.dma_start(word_table[:], tab_words[0].rearrange("p t b -> p (t b)").bitcast(I32))
-        gain_sign = keep.tile([P, PACK], F32, name="gain_sign")
-        nc.scalar.activation(gain_sign[:], gain[:], ACT.Sign)
-        root0 = keep.tile([P, PACK], F32, name="root0")
-        nc.scalar.activation(root0[:], gain_pos[:], ACT.Sqrt)
-        root0_inv = keep.tile([P, PACK], F32, name="root0_inv")
-        nc.vector.reciprocal(root0_inv[:], root0[:])
-        quot = keep.tile([P, PACK], F32, name="quot")
-        nc.gpsimd.tensor_tensor(quot[:], gain_pos[:], root0_inv[:], ALU.mult)
-        root_sum = keep.tile([P, PACK], F32, name="root_sum")
-        nc.gpsimd.tensor_tensor(root_sum[:], quot[:], root0[:], ALU.add)
-        root = keep.tile([P, PACK], F32, name="root")
-        nc.gpsimd.tensor_scalar(root[:], root_sum[:], 0.5, None, ALU.mult)
-        signs = keep.tile([P, SIGN_COLS // PACK, PACK], BF16, name="signs")
-        nc.scalar.copy(signs[:], gain_sign[:].unsqueeze(1).to_broadcast([P, SIGN_COLS // PACK, PACK]))
 
+        diagonal = behind.tile([P, P], I32, name="diagonal", offset=4 * T - 2 * P, align_bytes=64)
+        nc.gpsimd.iota(diagonal[:], pattern=[[-1, P]], base=0, channel_multiplier=1)
         identity = keep.tile([P, P], F32, name="identity")
-        make_identity(nc, identity[:])
+        nc.vector.tensor_scalar(identity[:], diagonal[:], 0.0, None, ALU.is_equal)
+        word_table = behind.tile([P, T], I32, name="word_table", offset=0, align_bytes=64)
+        nc.sync.dma_start(word_table[:], tab_words[0].rearrange("p t b -> p (t b)").bitcast(I32))
 
-        w_words = keep.tile([P, 2, PASSES, 2 * F], U8, name="w_words", align_bytes=64)
-        w_scales = keep.tile([P, 2, PASSES, F], U8, name="w_scales", align_bytes=64)
-        for part in range(2):
-            nc.vector.tensor_copy(
-                w_words[:, part].bitcast(U16).rearrange("p a (t m) -> p a t m", t=PACK),
-                w_words_raw[:, part].bitcast(U16).rearrange("p a (m t) -> p a t m", t=PACK),
-            )
+        w_planes = behind.tile([P, 2 * PASSES * F], U8, name="w_planes", offset=4 * T, align_bytes=64)
+        nc.vector.memset(w_planes[:].bitcast(I32), 0)
+        for part, scales in enumerate((co_scales, si_scales)):
+            for q in range(4):
+                nc.sync.dma_start(
+                    w_planes[32 * q : 32 * q + 4, PASSES * F * part : PASSES * F * (part + 1)]
+                    .bitcast(I32)
+                    .rearrange("r (a f) -> r a f", a=PASSES),
+                    scales[:, 4 * q : 4 * q + 4, :].rearrange("a r f -> r a f").bitcast(I32),
+                )
+        w_scales = [
+            w_planes[:, PASSES * F * part : PASSES * F * (part + 1)].rearrange("p (a f) -> p a f", a=PASSES)
+            for part in range(2)
+        ]
+
+        scale_pass1 = keep.tile([P, J // 4], I32, name="scale_pass1", align_bytes=64)
+        nc.vector.memset(scale_pass1[:], 0)
 
         scale_pass0 = {}
 
-        def gather_scales(j0):
-            picked = keep.tile([P, SCALE_CHUNK], U8, name="picked_scales%d" % j0, align_bytes=64)
-            nc.vector.tensor_copy(picked[:], scale_table[:].bitcast(U8).indirect(listed(j0, SCALE_CHUNK)))
-            nc.scalar.dma_start(
-                scale_pass1[0:SHIFTED, j0 // 4 : (j0 + SCALE_CHUNK) // 4], picked[SHIFT:P, :].bitcast(I32)
-            )
-            scale_pass0[j0] = picked
+        def gather_scales(j0, width):
+            picked = keep.tile([P, width], U8, name="picked_scales%d" % j0, align_bytes=64)
+            nc.vector.tensor_copy(picked[:], scale_table[:].bitcast(U8).indirect(listed(j0, width)))
+            (nc.scalar if j0 == 0 else nc.sync).dma_start(scale_pass1[0:SHIFTED, j0 // 4 : (j0 + width) // 4], picked[SHIFT:P, :].bitcast(I32))
+            for j in range(j0, j0 + width, UNIT):
+                scale_pass0[j] = picked[:, j - j0 : j - j0 + UNIT]
 
         frames = {}
 
-        def gather_words(j0, chunks):
-            picked = work.tile([P, chunks * CHUNK], U32, name="picked_words", bufs=1)
-            nc.vector.tensor_copy(picked[:], word_table[:].bitcast(U32).indirect(listed(j0, chunks * CHUNK)))
-            for c0 in range(0, chunks * CHUNK, CHUNK):
-                parted = keep.tile([P, PASSES, 2 * CHUNK], U8, name="frames%d" % (j0 + c0), align_bytes=64)
+        def gather_words(j0):
+            if j0 == 0:
+                picked = chain.tile([P, CHUNK], U32, name="first_words", align_bytes=64, offset=0)
+            else:
+                picked = chain.tile([P, CHUNK], U32, name="picked_words", align_bytes=64, offset=1536)
+            nc.vector.tensor_copy(picked[:], word_table[:].bitcast(U32).indirect(listed(j0, CHUNK)))
+            step = UNIT if j0 == 0 else CHUNK
+            for c0 in range(0, CHUNK, step):
+                parted = keep.tile([P, PASSES, 2 * step], U8, name="frames%d" % (j0 + c0), align_bytes=64)
                 nc.vector.tensor_copy(
                     parted[:].bitcast(U16),
-                    picked[:, c0 : c0 + CHUNK].bitcast(U16).rearrange("p (n a) -> p a n", a=PASSES),
+                    picked[:, c0 : c0 + step].bitcast(U16).rearrange("p (n a) -> p a n", a=PASSES),
                 )
-                frames[j0 + c0] = parted
+                for u0 in range(0, step, UNIT):
+                    frames[j0 + c0 + u0] = parted[:, :, 2 * u0 : 2 * (u0 + UNIT)]
 
         picked_levels = {}
         level_columns = {}
 
         def gather_levels(j0):
-            picked = keep.tile([P, CHUNK], F32, name="picked_levels%d" % j0)
+            picked = work.tile([P, CHUNK], F32, name="picked_levels", bufs=4)
             nc.vector.tensor_copy(picked[:], levels[:].indirect(listed(j0, CHUNK)))
-            picked_levels[j0] = picked
-            if j0 < TURNED_UNTIL:
-                bank = turn_psum.tile([P, CHUNK // P, P], F32, name="level_bank", tag="turn_bank")
-                for i in range(CHUNK // P):
-                    nc.tensor.transpose(bank[:, i, :], picked[:, P * i : P * (i + 1)], identity[:])
-                column = keep.tile([P, CHUNK // P], F32, name="level_columns%d" % j0)
-                nc.scalar.copy(column[:], bank[:, :, 0])
-                level_columns[j0] = column
+            for u0 in range(0, CHUNK, UNIT):
+                picked_levels[j0 + u0] = picked[:, u0 : u0 + UNIT]
+            turned = [u0 for u0 in range(0, CHUNK, UNIT) if (j0 + u0) // UNIT in TURNED]
+            if turned:
+                tiles = len(turned) * UNIT // P
+                bank = aux_psum.tile([P, CHUNK // P, P], F32, name="level_bank", tag="aux")
+                for i in range(tiles):
+                    c0 = turned[0] + P * i
+                    nc.tensor.transpose(bank[:, i, :], picked[:, c0 : c0 + P], identity[:])
+                column = keep.tile([P, tiles], F32, name="level_columns%d" % j0)
+                nc.scalar.copy(column[:], bank[:, 0:tiles, 0])
+                for i in range(tiles):
+                    level_columns[j0 + turned[0] + P * i] = column[:, i : i + 1]
 
-        def transform(j0, width):
-            c0 = j0 % CHUNK
-            s0 = j0 % SCALE_CHUNK
-            words = frames[j0 - c0]
-            planes = (
-                scale_pass0[j0 - s0][:, s0 : s0 + width],
-                scale_pass1[:].bitcast(U8)[:, j0 : j0 + width],
-            )
-            squares = work.tile([P, 2, PACK, width], F32, name="squares", bufs=3)
-            per_bank = BANK // width
-            if per_bank == 1:
-                order = [(t, part) for part in range(2) for t in range(PACK)]
-            else:
-                order = [(t, part) for t in range(PACK) for part in range(2)]
-            for t, part in order:
-                if True:
-                    if part % per_bank == 0:
-                        bank = dft_psum.tile([P, per_bank, width], F32, name="dft_bank")
+        def planes(j0):
+            return scale_pass0[j0], scale_pass1[:].bitcast(U8)[:, j0 : j0 + UNIT]
+
+        squares = {}
+
+        def transform_by_frame(j0, width):
+            for part in range(2):
+                for j in range(j0, j0 + width, P):
+                    c0 = j % UNIT
+                    bank = dft_psum.tile([P, F], F32, name="dft_bank", tag="dft")
                     for a in range(PASSES):
                         nc.tensor.matmul_mx(
-                            out=bank[:, part % per_bank, :],
-                            lhsT=w_words[:, part, a, 2 * P * t : 2 * P * (t + 1)].bitcast(FP4X4),
-                            lhsT_scale=w_scales[:, part, a, P * t : P * (t + 1)],
-                            rhs=words[:, a, 2 * c0 : 2 * (c0 + width)].bitcast(FP4X4),
-                            rhs_scale=planes[a],
+                            out=bank[:],
+                            lhsT=frames[j - c0][:, a, 2 * c0 : 2 * (c0 + P)].bitcast(FP4X4),
+                            lhsT_scale=planes(j - c0)[a][:, c0 : c0 + P],
+                            rhs=w_words[part][:, a, :].bitcast(FP4X4),
+                            rhs_scale=w_scales[part][:, a, :],
                             start=(a == 0),
                             stop=(a == PASSES - 1),
                         )
-                    if part % per_bank == per_bank - 1:
-                        nc.scalar.activation(
-                            squares[:, part + 1 - per_bank : part + 1, t, :], bank[:], ACT.Square,
-                            scale=root[:, t : t + 1],
-                        )
-            return squares
+                    square = work.tile([P, PACK, P], F32, name="square", bufs=14)
+                    nc.scalar.activation(square[:], bank[:].rearrange("p (m t) -> p t m", t=PACK), ACT.Square)
+                    squares[j, part] = square
 
-        def quantize_power(width, squares):
-            piece = width // 2
-            pieces = (0, piece)
-            power = work.tile([P, width * PACK], BF16, name="power", align_bytes=64)
-            signed = work.tile([P, width * PACK], BF16, name="signed", align_bytes=64)
-            codes = work.tile([P, width], U32, name="codes", align_bytes=64, bufs=4)
-            scales = work.tile([P, width], U8, name="scales", align_bytes=64, bufs=4)
-            for n0 in pieces:
-                nc.vector.tensor_tensor(
-                    power[:, PACK * n0 : PACK * (n0 + piece)].rearrange("p (c i t) -> p c t i", i=4, t=PACK),
-                    squares[:, 0, :, n0 : n0 + piece].rearrange("p t (c i) -> p c t i", i=4),
-                    squares[:, 1, :, n0 : n0 + piece].rearrange("p t (c i) -> p c t i", i=4),
-                    ALU.add,
+        def transform_by_frequency(j0):
+            square = work.tile([P, 2, PACK, UNIT], F32, name="squares", bufs=3)
+            for t in range(PACK):
+                bank = dft_psum.tile([P, 2, UNIT], F32, name="dft_bank", tag="dft")
+                for part in range(2):
+                    for a in range(PASSES):
+                        nc.tensor.matmul_mx(
+                            out=bank[:, part, :],
+                            lhsT=dealt_words[part][:, a, 2 * P * t : 2 * P * (t + 1)].bitcast(FP4X4),
+                            lhsT_scale=dealt_scales[part][:, a, P * t : P * (t + 1)],
+                            rhs=frames[j0][:, a, :].bitcast(FP4X4),
+                            rhs_scale=planes(j0)[a],
+                            start=(a == 0),
+                            stop=(a == PASSES - 1),
+                        )
+                nc.scalar.activation(square[:, :, t, :], bank[:], ACT.Square, scale=root[:, t : t + 1])
+            squares[j0] = square
+
+        def add_turned(target, j, t):
+            for part in range(2):
+                nc.tensor.matmul(
+                    target, lhsT=squares[j, part][:, t, :], rhs=identity[:], is_transpose=True,
+                    start=(part == 0), stop=(part == 1),
                 )
-            for n0 in pieces:
-                cols = slice(PACK * n0, PACK * (n0 + piece))
+
+        def power_on_vector(j0, power):
+            for i in range(UNIT // P):
+                bank = aux_psum.tile([P, PACK, P], F32, name="sum_bank", tag="aux")
+                for t in range(PACK):
+                    add_turned(bank[:, t, :], j0 + P * i, t)
                 nc.vector.tensor_tensor(
-                    signed[:, cols].rearrange("p (r c) -> p r c", c=SIGN_COLS),
-                    power[:, cols].rearrange("p (r c) -> p r c", c=SIGN_COLS),
-                    signs[:].rearrange("p c t -> p (c t)").unsqueeze(1).to_broadcast(
-                        [P, piece * PACK // SIGN_COLS, SIGN_COLS]
-                    ),
+                    power[:, PACK * P * i : PACK * P * (i + 1)].rearrange("p (j t) -> p j t", t=PACK),
+                    bank[:].rearrange("p t j -> p j t"),
+                    gain[:].unsqueeze(1).to_broadcast([P, P, PACK]),
                     ALU.mult,
                 )
-            for n0 in pieces:
-                nc.vector.quantize_mx(
-                    out=codes[:, n0 : n0 + piece].bitcast(FP8X4),
-                    scales=scales[:, n0 : n0 + piece],
-                    in_=signed[:, PACK * n0 : PACK * (n0 + piece)],
-                )
+
+        def power_on_scalar(j0, power):
+            rows = work.tile([P, PACK, UNIT], BF16, name="rows")
+            for t0 in range(0, PACK, 2):
+                bank = aux_psum.tile([P, 2, UNIT], F32, name="sum_bank", tag="aux")
+                for e in range(2):
+                    for i in range(UNIT // P):
+                        add_turned(bank[:, e, P * i : P * (i + 1)], j0 + P * i, t0 + e)
+                for e in range(2):
+                    nc.scalar.activation(
+                        rows[:, t0 + e, :], bank[:, e, :], ACT.Copy, scale=gain[:, t0 + e : t0 + e + 1]
+                    )
+            nc.vector.tensor_copy(
+                power[:].rearrange("p (c i t) -> p c t i", i=4, t=PACK),
+                rows[:].rearrange("p t (c i) -> p c t i", i=4),
+            )
+
+        def power_by_frequency(j0, power):
+            unsigned = work.tile([P, UNIT * PACK], BF16, name="unsigned", align_bytes=64)
+            nc.vector.tensor_tensor(
+                unsigned[:].rearrange("p (c i t) -> p c t i", i=4, t=PACK),
+                squares[j0][:, 0].rearrange("p t (c i) -> p c t i", i=4),
+                squares[j0][:, 1].rearrange("p t (c i) -> p c t i", i=4),
+                ALU.add,
+            )
+            nc.vector.tensor_tensor(
+                power[:].rearrange("p (r c) -> p r c", c=SIGN_COLS),
+                unsigned[:].rearrange("p (r c) -> p r c", c=SIGN_COLS),
+                signs[:].rearrange("p c t -> p (c t)").unsqueeze(1).to_broadcast(
+                    [P, UNIT * PACK // SIGN_COLS, SIGN_COLS]
+                ),
+                ALU.mult,
+            )
+
+        def power_codes(u):
+            power = work.tile([P, UNIT * PACK], BF16, name="power", align_bytes=64)
+            {"A": power_by_frequency, "B": power_on_vector, "S": power_on_scalar}[ROUTES[u]](UNIT * u, power)
+            codes = work.tile([P, UNIT], U32, name="codes", align_bytes=64, bufs=8)
+            scales = work.tile([P, UNIT], U8, name="scales", align_bytes=64, bufs=8)
+            nc.vector.quantize_mx(out=codes[:].bitcast(FP8X4), scales=scales[:], in_=power[:])
             return codes, scales
 
-        def store(j0, width, result):
-            nc.sync.dma_start(out[:, j0 : j0 + width].rearrange("(h p) j -> p h j", p=P), result[:])
+        def store(j0, result):
+            nc.sync.dma_start(out[:, j0 : j0 + UNIT].rearrange("(h p) j -> p h j", p=P), result[:])
 
-        def filter_bank(j0, width, codes, scales):
-            c0 = j0 % CHUNK
-            level = picked_levels[j0 - c0][:, c0 : c0 + width]
-            result = work.tile([P, N // P, width], F32, name="result", bufs=3)
-            per_bank = BANK // width
+        def filter_direct(j0, codes, scales):
+            result = work.tile([P, N // P, UNIT], F32, name="result", bufs=3)
+            bank = aux_psum.tile([P, N // P, UNIT], F32, name="mel_bank", tag="aux")
             for half in range(N // P):
-                if half % per_bank == 0:
-                    bank = mel_psum.tile([P, per_bank, width], F32, name="mel_bank", tag="mel_bank")
                 nc.tensor.matmul_mx(
-                    out=bank[:, half % per_bank, :],
-                    lhsT=fb_codes.bitcast(U8)[:, 2 * P * half : 2 * P * (half + 1)].bitcast(FP4X4),
-                    lhsT_scale=fb_scale.bitcast(U8)[:, P * half : P * (half + 1)],
+                    out=bank[:, half, :],
+                    lhsT=fb_codes[:, 2 * P * half : 2 * P * (half + 1)].bitcast(FP4X4),
+                    lhsT_scale=fb_scale[:, P * half : P * (half + 1)],
                     rhs=codes[:].bitcast(FP8X4),
                     rhs_scale=scales[:],
                     start=True,
                     stop=True,
                 )
-                if half % per_bank == per_bank - 1:
-                    nc.vector.tensor_tensor(
-                        result[:, half + 1 - per_bank : half + 1, :],
-                        bank[:],
-                        level.unsqueeze(1).to_broadcast([P, per_bank, width]),
-                        ALU.mult,
-                    )
-            store(j0, width, result)
-
-        def filter_bank_turned(j0, width, codes, scales):
-            for n0 in range(0, width, 2 * P):
-                by_frame = work.tile([P, 2, N], F32, name="by_frame", bufs=3)
-                bank = turn_psum.tile([P, 2, N], F32, name="frame_bank", tag="turn_bank")
-                for i in range(2):
-                    cols = slice(n0 + P * i, n0 + P * (i + 1))
-                    nc.tensor.matmul_mx(
-                        out=bank[:, i, :],
-                        lhsT=codes[:, cols].bitcast(FP8X4),
-                        lhsT_scale=scales[:, cols],
-                        rhs=fb_codes.bitcast(U8).bitcast(FP4X4),
-                        rhs_scale=fb_scale.bitcast(U8),
-                        start=True,
-                        stop=True,
-                    )
-                for i in range(2):
-                    tile_in_chunk = n0 // P + i
-                    nc.scalar.activation(
-                        by_frame[:, i, :], bank[:, i, :], ACT.Copy,
-                        scale=level_columns[j0][:, tile_in_chunk : tile_in_chunk + 1],
-                    )
-                turned = turn_psum.tile([P, N // P, 2 * P], F32, name="turned_bank", tag="turn_bank")
-                for i in range(2):
-                    for half in range(N // P):
-                        nc.tensor.transpose(
-                            turned[:, half, P * i : P * (i + 1)], by_frame[:, i, P * half : P * (half + 1)], identity[:]
-                        )
-                result = work.tile([P, N // P, 2 * P], F32, name="turned_result", bufs=3)
-                nc.scalar.copy(result[:], turned[:])
-                store(j0 + n0, 2 * P, result)
-
-        def order_scales(part, raw):
-            nc.vector.tensor_copy(
-                w_scales[:, part].rearrange("p a (t m) -> p a t m", t=PACK),
-                raw[:].bitcast(U8).rearrange("p a (m t) -> p a t m", t=PACK),
+            nc.vector.tensor_tensor(
+                result[:], bank[:], picked_levels[j0].unsqueeze(1).to_broadcast([P, N // P, UNIT]), ALU.mult
             )
+            store(j0, result)
 
-        gather_scales(0)
-        order_scales(0, co_scales_raw)
-        si_scales_raw = load_weight_scales(si_scales)
-        gather_scales(SCALE_CHUNK)
-        gather_words(0, 1)
-        order_scales(1, si_scales_raw)
-        filters = keep.tile([P, N // 2 + N // 4], I32, name="filters", tag="then_filters", align_bytes=64)
-        fb_codes, fb_scale = filters[:, 0 : N // 2], filters[:, N // 2 :]
-        nc.gpsimd.memset(fb_scale, 0)
-        nc.sync.dma_start(fb_codes, fb_words[0].bitcast(I32))
-        for q in range(4):
-            nc.sync.dma_start(fb_scale[32 * q : 32 * q + 4, :], fb_scales[0, 4 * q : 4 * q + 4, :].bitcast(I32))
-        levels = keep.tile([P, T], F32, name="levels", tag="then_levels", align_bytes=64)
+        def filter_turned(j0, codes, scales):
+            by_frame = work.tile([P, UNIT // P, N], F32, name="by_frame", bufs=3)
+            bank = aux_psum.tile([P, UNIT // P, N], F32, name="frame_bank", tag="aux")
+            for i in range(UNIT // P):
+                cols = slice(P * i, P * (i + 1))
+                nc.tensor.matmul_mx(
+                    out=bank[:, i, :],
+                    lhsT=codes[:, cols].bitcast(FP8X4),
+                    lhsT_scale=scales[:, cols],
+                    rhs=fb_codes[:].bitcast(FP4X4),
+                    rhs_scale=fb_scale[:],
+                    start=True,
+                    stop=True,
+                )
+            for i in range(UNIT // P):
+                nc.scalar.activation(by_frame[:, i, :], bank[:, i, :], ACT.Copy, scale=level_columns[j0 + P * i])
+            turned = aux_psum.tile([P, N // P, UNIT], F32, name="turned_bank", tag="aux")
+            for i in range(UNIT // P):
+                for half in range(N // P):
+                    nc.tensor.transpose(
+                        turned[:, half, P * i : P * (i + 1)], by_frame[:, i, P * half : P * (half + 1)], identity[:]
+                    )
+            result = work.tile([P, N // P, UNIT], F32, name="turned_result", bufs=3)
+            nc.scalar.copy(result[:], turned[:])
+            store(j0, result)
+
+        for j0, width in SCALE_CHUNKS:
+            gather_scales(j0, width)
+        gather_words(0)
+        gain = staged.tile([P, PACK], F32, name="gain", offset=0)
+        nc.sync.dma_start(gain[:], gn.rearrange("(p t) -> p t", t=PACK))
+        levels = staged.tile([P, T], F32, name="levels", offset=2048)
         nc.sync.dma_start(levels[:], ts)
-        gather_words(CHUNK, 2)
-        squares = {}
+        fb_codes = early.tile([P, 2 * N], U8, name="fb_codes", offset=0, align_bytes=64)
+        nc.sync.dma_start(fb_codes[:].bitcast(I32), fb_words[0].bitcast(I32))
+        fb_scale = staged.tile([P, N], U8, name="fb_scale", offset=256, align_bytes=64)
+        nc.vector.memset(fb_scale[:].bitcast(I32), 0)
+        for q in range(4):
+            nc.sync.dma_start(
+                fb_scale[32 * q : 32 * q + 4, :].bitcast(I32), fb_scales[0, 4 * q : 4 * q + 4, :].bitcast(I32)
+            )
+        gather_words(CHUNK)
+
+        dealt_words, dealt_scales = [], []
+        for part in range(2):
+            tile = keep.tile([P, PASSES, 2 * F], U8, name="dealt_words%d" % part, align_bytes=64)
+            nc.vector.tensor_copy(
+                tile[:].bitcast(U16).rearrange("p a (t m) -> p a t m", t=PACK),
+                w_words[part][:].bitcast(U16).rearrange("p a (m t) -> p a t m", t=PACK),
+            )
+            dealt_words.append(tile)
+            tile = chain.tile(
+                [P, PASSES, F], U8, name="dealt_scales%d" % part, align_bytes=64, offset=3584 * part
+            )
+            nc.vector.tensor_copy(
+                tile[:].rearrange("p a (t m) -> p a t m", t=PACK),
+                w_scales[part].rearrange("p a (m t) -> p a t m", t=PACK),
+            )
+            dealt_scales.append(tile)
+        negated = keep.tile([P, PACK], F32, name="negated")
+        nc.gpsimd.tensor_scalar(negated[:], gain[:], -1.0, TINY, ALU.mult, ALU.max)
+        size = keep.tile([P, PACK], F32, name="size")
+        nc.vector.tensor_tensor(size[:], negated[:], gain[:], ALU.max)
+        half = keep.tile([P, PACK], F32, name="half")
+        nc.gpsimd.memset(half[:], 0.5)
+        guess = keep.tile([P, PACK], F32, name="guess")
+        nc.gpsimd.tensor_tensor(guess[:], size[:], half[:], ALU.pow)
+        inverse = keep.tile([P, PACK], F32, name="inverse")
+        nc.vector.reciprocal(inverse[:], guess[:])
+        quotient = keep.tile([P, PACK], F32, name="quotient")
+        nc.gpsimd.tensor_tensor(quotient[:], size[:], inverse[:], ALU.mult)
+        doubled = keep.tile([P, PACK], F32, name="doubled")
+        nc.gpsimd.tensor_tensor(doubled[:], quotient[:], guess[:], ALU.add)
+        root = keep.tile([P, PACK], F32, name="root")
+        nc.gpsimd.tensor_tensor(root[:], doubled[:], half[:], ALU.mult)
+        signs = keep.tile([P, SIGN_COLS // PACK, PACK], BF16, name="signs")
+        nc.scalar.activation(
+            signs[:], gain[:].unsqueeze(1).to_broadcast([P, SIGN_COLS // PACK, PACK]), ACT.Sign
+        )
+
         quantized = {}
-        for step, b in ORDER:
-            j0, width = BLOCKS[b]
-            if step == "transform":
-                squares[b] = transform(j0, width)
-                if j0 % CHUNK == 0:
-                    if j0 == 0:
-                        gather_words(3 * CHUNK, 1)
-                    gather_levels(j0)
-            elif step == "quantize":
-                quantized[b] = quantize_power(width, squares[b])
-            else:
-                (filter_bank_turned if j0 < TURNED_UNTIL else filter_bank)(j0, width, *quantized[b])
+        transform_by_frame(0, 2 * UNIT)
+        for step in range(1, UNITS + 2):
+            if 2 <= step < UNITS:
+                if ROUTES[step] == "A":
+                    transform_by_frequency(UNIT * step)
+                else:
+                    transform_by_frame(UNIT * step, UNIT)
+            if step in (1, 3):
+                gather_words(CHUNK * (step + 3) // 2)
+            if step <= UNITS:
+                quantized[step - 1] = power_codes(step - 1)
+                if step % 2 == 1:
+                    gather_levels(UNIT * (step - 1))
+            if step >= 2:
+                (filter_turned if step - 2 in TURNED else filter_direct)(UNIT * (step - 2), *quantized[step - 2])

@@ -1,6 +1,7 @@
 from contextlib import ExitStack
 
 import concourse.mybir as mybir
+from concourse.masks import make_identity
 
 K, F, N, T, J = 1024, 512, 256, 4096, 2048
 FLOPS = 2 * J * (2 * K * F + F * N)
@@ -22,12 +23,14 @@ PASSES = K // (P * PACK)
 GROUP = 16
 CHUNK = 512
 UNIT = 256
-UNITS = J // UNIT
 SCALE_CHUNKS = [(0, 512), (512, 1536)]
 SHIFT = 16
 SHIFTED = P - SHIFT
-ROUTES = ["S","S","S","S","A","A","A","A"]
-TURNED = []
+BANKS = 8
+BANK = 512
+BLOCKS = [("frame", 0, 512), ("frequency", 512, 512), ("frequency", 1024, 512), ("frequency", 1536, 256), ("frequency", 1792, 256)]
+TURNED = [0, 1]
+ORDER = [("transform", 0), ("transform", 1), ("add", 0), ("quantize", 1), ("quantize", 0), ("transform", 2), ("transform", 3), ("quantize", 2), ("filter", 1), ("transform", 4), ("filter", 0), ("quantize", 3), ("filter", 2), ("quantize", 4), ("filter", 3), ("filter", 4)]
 SIGN_COLS = 128
 TINY = 2.0**-110
 
@@ -38,13 +41,17 @@ def tile_list_meltab_gain_kernel(
     nc = tc.nc
     with ExitStack() as ctx:
         keep = ctx.enter_context(tc.tile_pool(name="keep", bufs=1))
-        staged = ctx.enter_context(tc.tile_pool(name="staged", bufs=1))
         chain = ctx.enter_context(tc.tile_pool(name="chain", bufs=1))
         behind = ctx.enter_context(tc.tile_pool(name="behind", bufs=1))
-        early = ctx.enter_context(tc.tile_pool(name="early", bufs=1))
         work = ctx.enter_context(tc.tile_pool(name="work", bufs=2))
-        dft_psum = ctx.enter_context(tc.psum_pool(name="dft_psum", bufs=3))
-        aux_psum = ctx.enter_context(tc.psum_pool(name="aux_psum", bufs=5))
+        psum = ctx.enter_context(tc.psum_pool(name="psum", bufs=1))
+        taken = []
+
+        def next_bank(rows):
+            taken.append(rows)
+            return psum.tile(
+                [P, rows, BANK // rows], F32, name="bank%d" % len(taken), offset=4 * BANK * (len(taken) % BANKS)
+            )
 
         offsets = keep.tile([P, J // GROUP], U16, name="offsets")
         nc.sync.dma_start(offsets[:], offs)
@@ -52,23 +59,28 @@ def tile_list_meltab_gain_kernel(
         def listed(j0, width):
             return offsets[:, j0 // GROUP : (j0 + width) // GROUP]
 
+        gain = keep.tile([P, PACK], F32, name="gain")
+        nc.scalar.dma_start(gain[:], gn.rearrange("(p t) -> p t", t=PACK))
+
         w_words = []
         for part, words in enumerate((co_words, si_words)):
-            tile = early.tile([P, PASSES, 2 * F], U8, name="w_words%d" % part, align_bytes=64, offset=4 * F * part)
-            nc.sync.dma_start(tile[:].bitcast(I32), words.rearrange("a p b -> p a b").bitcast(I32))
+            tile = keep.tile([P, PASSES, 2 * F], U8, name="w_words%d" % part, align_bytes=64)
+            nc.scalar.dma_start(tile[:].bitcast(I32), words.rearrange("a p b -> p a b").bitcast(I32))
             w_words.append(tile)
 
-        scale_table = staged.tile([P, T // 4], I32, name="scale_table", offset=0)
+        scale_table = keep.tile([P, T // 4], I32, name="scale_table", align_bytes=64)
         nc.vector.memset(scale_table[:], 0)
         for r in range(4):
-            nc.sync.dma_start(
+            (nc.sync, nc.scalar)[r % 2].dma_start(
                 scale_table[r:P:SHIFT, :], tab_scales[:, r:16:4, :].rearrange("a q t -> q a t").bitcast(I32)
             )
 
-        diagonal = behind.tile([P, P], I32, name="diagonal", offset=4 * T - 2 * P, align_bytes=64)
-        nc.gpsimd.iota(diagonal[:], pattern=[[-1, P]], base=0, channel_multiplier=1)
-        identity = keep.tile([P, P], F32, name="identity")
-        nc.vector.tensor_scalar(identity[:], diagonal[:], 0.0, None, ALU.is_equal)
+        scale_pass1 = {}
+        for j0, width in SCALE_CHUNKS:
+            scale_pass1[j0] = keep.tile([P, width // 4], I32, name="scale_pass1_%d" % j0, align_bytes=64)
+        blank = behind.tile([P, P], I32, name="blank", offset=4 * T - 2 * P, align_bytes=64)
+        nc.vector.memset(blank[:], 0)
+        nc.vector.tensor_copy(scale_pass1[0][:], blank[:])
         word_table = behind.tile([P, T], I32, name="word_table", offset=0, align_bytes=64)
         nc.sync.dma_start(word_table[:], tab_words[0].rearrange("p t b -> p (t b)").bitcast(I32))
 
@@ -87,25 +99,43 @@ def tile_list_meltab_gain_kernel(
             for part in range(2)
         ]
 
-        scale_pass1 = keep.tile([P, J // 4], I32, name="scale_pass1", align_bytes=64)
-        nc.vector.memset(scale_pass1[:], 0)
+        nc.vector.memset(scale_pass1[CHUNK][:], 0)
+        identity = keep.tile([P, P], F32, name="identity")
+        make_identity(nc, identity[:])
+
+        negated = keep.tile([P, PACK], F32, name="negated")
+        nc.vector.tensor_scalar(negated[:], gain[:], -1.0, TINY, ALU.mult, ALU.max)
+        size = keep.tile([P, PACK], F32, name="size")
+        nc.vector.tensor_tensor(size[:], negated[:], gain[:], ALU.max)
+        half_guess = keep.tile([P, PACK], F32, name="half_guess")
+        nc.scalar.activation(half_guess[:], size[:], ACT.Sqrt, scale=0.25)
+        spread = gain[:].unsqueeze(1).to_broadcast([P, SIGN_COLS // PACK, PACK])
+        below = keep.tile([P, SIGN_COLS // PACK, PACK], F32, name="below")
+        nc.vector.tensor_scalar(below[:], spread, 0.0, None, ALU.is_lt)
+        signs = keep.tile([P, SIGN_COLS // PACK, PACK], BF16, name="signs")
+        nc.vector.scalar_tensor_tensor(signs[:], spread, 0.0, below[:], ALU.is_gt, ALU.subtract)
+        inverse = keep.tile([P, PACK], F32, name="inverse")
+        nc.vector.reciprocal(inverse[:], half_guess[:])
+        half_quotient = keep.tile([P, PACK], F32, name="half_quotient")
+        nc.vector.scalar_tensor_tensor(half_quotient[:], size[:], 0.25, inverse[:], ALU.mult, ALU.mult)
+        root = keep.tile([P, PACK], F32, name="root")
+        nc.vector.tensor_tensor(root[:], half_quotient[:], half_guess[:], ALU.add)
 
         scale_pass0 = {}
 
         def gather_scales(j0, width):
             picked = keep.tile([P, width], U8, name="picked_scales%d" % j0, align_bytes=64)
             nc.vector.tensor_copy(picked[:], scale_table[:].bitcast(U8).indirect(listed(j0, width)))
-            (nc.scalar if j0 == 0 else nc.sync).dma_start(scale_pass1[0:SHIFTED, j0 // 4 : (j0 + width) // 4], picked[SHIFT:P, :].bitcast(I32))
-            for j in range(j0, j0 + width, UNIT):
-                scale_pass0[j] = picked[:, j - j0 : j - j0 + UNIT]
+            nc.scalar.dma_start(scale_pass1[j0][0:SHIFTED, :], picked[SHIFT:P, :].bitcast(I32))
+            scale_pass0[j0] = picked
 
         frames = {}
 
         def gather_words(j0):
             if j0 == 0:
-                picked = chain.tile([P, CHUNK], U32, name="first_words", align_bytes=64, offset=0)
+                picked = chain.tile([P, CHUNK], U32, name="first_words", align_bytes=64, offset=16320)
             else:
-                picked = chain.tile([P, CHUNK], U32, name="picked_words", align_bytes=64, offset=1536)
+                picked = chain.tile([P, CHUNK], U32, name="picked_words", align_bytes=64, offset=18176)
             nc.vector.tensor_copy(picked[:], word_table[:].bitcast(U32).indirect(listed(j0, CHUNK)))
             step = UNIT if j0 == 0 else CHUNK
             for c0 in range(0, CHUNK, step):
@@ -114,144 +144,149 @@ def tile_list_meltab_gain_kernel(
                     parted[:].bitcast(U16),
                     picked[:, c0 : c0 + step].bitcast(U16).rearrange("p (n a) -> p a n", a=PASSES),
                 )
-                for u0 in range(0, step, UNIT):
-                    frames[j0 + c0 + u0] = parted[:, :, 2 * u0 : 2 * (u0 + UNIT)]
+                frames[j0 + c0] = parted
+
+        def frame_operand(j0, width, a):
+            first = max(j for j in frames if j <= j0)
+            words = frames[first][:, a, 2 * (j0 - first) : 2 * (j0 - first + width)].bitcast(FP4X4)
+            first = max(j for j in scale_pass0 if j <= j0)
+            plane = (scale_pass0[first][:], scale_pass1[first][:].bitcast(U8))[a]
+            return words, plane[:, j0 - first : j0 - first + width]
 
         picked_levels = {}
         level_columns = {}
 
         def gather_levels(j0):
-            picked = work.tile([P, CHUNK], F32, name="picked_levels", bufs=4)
+            picked = keep.tile([P, CHUNK], F32, name="picked_levels%d" % j0)
             nc.vector.tensor_copy(picked[:], levels[:].indirect(listed(j0, CHUNK)))
             for u0 in range(0, CHUNK, UNIT):
                 picked_levels[j0 + u0] = picked[:, u0 : u0 + UNIT]
-            turned = [u0 for u0 in range(0, CHUNK, UNIT) if (j0 + u0) // UNIT in TURNED]
-            if turned:
-                tiles = len(turned) * UNIT // P
-                bank = aux_psum.tile([P, CHUNK // P, P], F32, name="level_bank", tag="aux")
-                for i in range(tiles):
-                    c0 = turned[0] + P * i
-                    nc.tensor.transpose(bank[:, i, :], picked[:, c0 : c0 + P], identity[:])
-                column = keep.tile([P, tiles], F32, name="level_columns%d" % j0)
-                nc.scalar.copy(column[:], bank[:, 0:tiles, 0])
-                for i in range(tiles):
-                    level_columns[j0 + turned[0] + P * i] = column[:, i : i + 1]
 
-        def planes(j0):
-            return scale_pass0[j0], scale_pass1[:].bitcast(U8)[:, j0 : j0 + UNIT]
+        def turn_levels(units):
+            tiles = [j0 + c0 for j0 in units for c0 in range(0, UNIT, P)]
+            bank = next_bank(BANK // P)
+            for i, j in enumerate(tiles):
+                nc.tensor.transpose(bank[:, i, :], picked_levels[j - j % UNIT][:, j % UNIT : j % UNIT + P], identity[:])
+            column = keep.tile([P, len(tiles)], F32, name="level_columns%d" % units[0])
+            nc.scalar.copy(column[:], bank[:, 0 : len(tiles), 0])
+            for i, j in enumerate(tiles):
+                level_columns[j] = column[:, i : i + 1]
 
         squares = {}
 
         def transform_by_frame(j0, width):
             for part in range(2):
                 for j in range(j0, j0 + width, P):
-                    c0 = j % UNIT
-                    bank = dft_psum.tile([P, F], F32, name="dft_bank", tag="dft")
+                    bank = next_bank(1)
                     for a in range(PASSES):
+                        words, plane = frame_operand(j, P, a)
                         nc.tensor.matmul_mx(
-                            out=bank[:],
-                            lhsT=frames[j - c0][:, a, 2 * c0 : 2 * (c0 + P)].bitcast(FP4X4),
-                            lhsT_scale=planes(j - c0)[a][:, c0 : c0 + P],
+                            out=bank[:, 0, :],
+                            lhsT=words,
+                            lhsT_scale=plane,
                             rhs=w_words[part][:, a, :].bitcast(FP4X4),
                             rhs_scale=w_scales[part][:, a, :],
                             start=(a == 0),
                             stop=(a == PASSES - 1),
                         )
-                    square = work.tile([P, PACK, P], F32, name="square", bufs=14)
-                    nc.scalar.activation(square[:], bank[:].rearrange("p (m t) -> p t m", t=PACK), ACT.Square)
+                    square = keep.tile([P, PACK, P], F32, name="square%d_%d" % (j, part))
+                    nc.scalar.activation(square[:], bank[:, 0, :].rearrange("p (m t) -> p t m", t=PACK), ACT.Square)
                     squares[j, part] = square
 
-        def transform_by_frequency(j0):
-            square = work.tile([P, 2, PACK, UNIT], F32, name="squares", bufs=3)
-            for t in range(PACK):
-                bank = dft_psum.tile([P, 2, UNIT], F32, name="dft_bank", tag="dft")
-                for part in range(2):
-                    for a in range(PASSES):
-                        nc.tensor.matmul_mx(
-                            out=bank[:, part, :],
-                            lhsT=dealt_words[part][:, a, 2 * P * t : 2 * P * (t + 1)].bitcast(FP4X4),
-                            lhsT_scale=dealt_scales[part][:, a, P * t : P * (t + 1)],
-                            rhs=frames[j0][:, a, :].bitcast(FP4X4),
-                            rhs_scale=planes(j0)[a],
-                            start=(a == 0),
-                            stop=(a == PASSES - 1),
-                        )
-                nc.scalar.activation(square[:, :, t, :], bank[:], ACT.Square, scale=root[:, t : t + 1])
+        def transform_by_frequency(j0, width):
+            square = keep.tile([P, 2, PACK, width], F32, name="squares%d" % j0)
+            per_bank = BANK // width
+            if per_bank == 1:
+                order = [(t, part) for part in range(2) for t in range(PACK)]
+            else:
+                order = [(t, part) for t in range(PACK) for part in range(2)]
+            for t, part in order:
+                if part % per_bank == 0:
+                    bank = next_bank(per_bank)
+                for a in range(PASSES):
+                    words, plane = frame_operand(j0, width, a)
+                    nc.tensor.matmul_mx(
+                        out=bank[:, part % per_bank, :],
+                        lhsT=dealt_words[part][:, a, 2 * P * t : 2 * P * (t + 1)].bitcast(FP4X4),
+                        lhsT_scale=dealt_scales[part][:, a, P * t : P * (t + 1)],
+                        rhs=words,
+                        rhs_scale=plane,
+                        start=(a == 0),
+                        stop=(a == PASSES - 1),
+                    )
+                if part % per_bank == per_bank - 1:
+                    nc.scalar.activation(
+                        square[:, part + 1 - per_bank : part + 1, t, :], bank[:], ACT.Square, scale=root[:, t : t + 1]
+                    )
             squares[j0] = square
 
-        def add_turned(target, j, t):
-            for part in range(2):
-                nc.tensor.matmul(
-                    target, lhsT=squares[j, part][:, t, :], rhs=identity[:], is_transpose=True,
-                    start=(part == 0), stop=(part == 1),
-                )
+        def add_by_frame(j0, width):
+            rows = keep.tile([P, PACK, width], BF16, name="rows%d" % j0)
+            for t in range(PACK):
+                bank = next_bank(1)
+                for c0 in range(0, width, P):
+                    for part in range(2):
+                        nc.tensor.matmul(
+                            bank[:, 0, c0 : c0 + P], lhsT=squares[j0 + c0, part][:, t, :], rhs=identity[:],
+                            is_transpose=True, start=(part == 0), stop=(part == 1),
+                        )
+                nc.scalar.activation(rows[:, t, :], bank[:, 0, 0:width], ACT.Copy, scale=gain[:, t : t + 1])
+            squares[j0] = rows
 
-        def power_on_vector(j0, power):
-            for i in range(UNIT // P):
-                bank = aux_psum.tile([P, PACK, P], F32, name="sum_bank", tag="aux")
-                for t in range(PACK):
-                    add_turned(bank[:, t, :], j0 + P * i, t)
-                nc.vector.tensor_tensor(
-                    power[:, PACK * P * i : PACK * P * (i + 1)].rearrange("p (j t) -> p j t", t=PACK),
-                    bank[:].rearrange("p t j -> p j t"),
-                    gain[:].unsqueeze(1).to_broadcast([P, P, PACK]),
-                    ALU.mult,
-                )
+        quantized = {}
 
-        def power_on_scalar(j0, power):
-            rows = work.tile([P, PACK, UNIT], BF16, name="rows")
-            for t0 in range(0, PACK, 2):
-                bank = aux_psum.tile([P, 2, UNIT], F32, name="sum_bank", tag="aux")
-                for e in range(2):
-                    for i in range(UNIT // P):
-                        add_turned(bank[:, e, P * i : P * (i + 1)], j0 + P * i, t0 + e)
-                for e in range(2):
-                    nc.scalar.activation(
-                        rows[:, t0 + e, :], bank[:, e, :], ACT.Copy, scale=gain[:, t0 + e : t0 + e + 1]
+        def quantize_power(road, j0, width):
+            piece = width // 2
+            power = work.tile([P, width * PACK], BF16, name="power", align_bytes=64)
+            codes = keep.tile([P, width], U32, name="codes%d" % j0, align_bytes=64)
+            scales = keep.tile([P, width], U8, name="scales%d" % j0, align_bytes=64)
+            if road == "frame":
+                for n0 in (0, piece):
+                    nc.vector.tensor_copy(
+                        power[:, PACK * n0 : PACK * (n0 + piece)].rearrange("p (c i t) -> p c t i", i=4, t=PACK),
+                        squares[j0][:, :, n0 : n0 + piece].rearrange("p t (c i) -> p c t i", i=4),
                     )
-            nc.vector.tensor_copy(
-                power[:].rearrange("p (c i t) -> p c t i", i=4, t=PACK),
-                rows[:].rearrange("p t (c i) -> p c t i", i=4),
-            )
-
-        def power_by_frequency(j0, power):
-            unsigned = work.tile([P, UNIT * PACK], BF16, name="unsigned", align_bytes=64)
-            nc.vector.tensor_tensor(
-                unsigned[:].rearrange("p (c i t) -> p c t i", i=4, t=PACK),
-                squares[j0][:, 0].rearrange("p t (c i) -> p c t i", i=4),
-                squares[j0][:, 1].rearrange("p t (c i) -> p c t i", i=4),
-                ALU.add,
-            )
-            nc.vector.tensor_tensor(
-                power[:].rearrange("p (r c) -> p r c", c=SIGN_COLS),
-                unsigned[:].rearrange("p (r c) -> p r c", c=SIGN_COLS),
-                signs[:].rearrange("p c t -> p (c t)").unsqueeze(1).to_broadcast(
-                    [P, UNIT * PACK // SIGN_COLS, SIGN_COLS]
-                ),
-                ALU.mult,
-            )
-
-        def power_codes(u):
-            power = work.tile([P, UNIT * PACK], BF16, name="power", align_bytes=64)
-            {"A": power_by_frequency, "B": power_on_vector, "S": power_on_scalar}[ROUTES[u]](UNIT * u, power)
-            codes = work.tile([P, UNIT], U32, name="codes", align_bytes=64, bufs=8)
-            scales = work.tile([P, UNIT], U8, name="scales", align_bytes=64, bufs=8)
-            nc.vector.quantize_mx(out=codes[:].bitcast(FP8X4), scales=scales[:], in_=power[:])
-            return codes, scales
+            else:
+                unsigned = work.tile([P, width * PACK], BF16, name="unsigned", align_bytes=64)
+                for n0 in (0, piece):
+                    nc.vector.tensor_tensor(
+                        unsigned[:, PACK * n0 : PACK * (n0 + piece)].rearrange("p (c i t) -> p c t i", i=4, t=PACK),
+                        squares[j0][:, 0, :, n0 : n0 + piece].rearrange("p t (c i) -> p c t i", i=4),
+                        squares[j0][:, 1, :, n0 : n0 + piece].rearrange("p t (c i) -> p c t i", i=4),
+                        ALU.add,
+                    )
+                for n0 in (0, piece):
+                    cols = slice(PACK * n0, PACK * (n0 + piece))
+                    nc.vector.tensor_tensor(
+                        power[:, cols].rearrange("p (r c) -> p r c", c=SIGN_COLS),
+                        unsigned[:, cols].rearrange("p (r c) -> p r c", c=SIGN_COLS),
+                        signs[:].rearrange("p c t -> p (c t)").unsqueeze(1).to_broadcast(
+                            [P, piece * PACK // SIGN_COLS, SIGN_COLS]
+                        ),
+                        ALU.mult,
+                    )
+            for n0 in (0, piece):
+                nc.vector.quantize_mx(
+                    out=codes[:, n0 : n0 + piece].bitcast(FP8X4),
+                    scales=scales[:, n0 : n0 + piece],
+                    in_=power[:, PACK * n0 : PACK * (n0 + piece)],
+                )
+            for u0 in range(0, width, UNIT):
+                quantized[j0 + u0] = codes[:, u0 : u0 + UNIT], scales[:, u0 : u0 + UNIT]
 
         def store(j0, result):
             nc.sync.dma_start(out[:, j0 : j0 + UNIT].rearrange("(h p) j -> p h j", p=P), result[:])
 
         def filter_direct(j0, codes, scales):
-            result = work.tile([P, N // P, UNIT], F32, name="result", bufs=3)
-            bank = aux_psum.tile([P, N // P, UNIT], F32, name="mel_bank", tag="aux")
+            result = work.tile([P, N // P, UNIT], F32, name="result", bufs=4)
+            bank = next_bank(N // P)
             for half in range(N // P):
                 nc.tensor.matmul_mx(
                     out=bank[:, half, :],
                     lhsT=fb_codes[:, 2 * P * half : 2 * P * (half + 1)].bitcast(FP4X4),
                     lhsT_scale=fb_scale[:, P * half : P * (half + 1)],
-                    rhs=codes[:].bitcast(FP8X4),
-                    rhs_scale=scales[:],
+                    rhs=codes.bitcast(FP8X4),
+                    rhs_scale=scales,
                     start=True,
                     stop=True,
                 )
@@ -262,7 +297,7 @@ def tile_list_meltab_gain_kernel(
 
         def filter_turned(j0, codes, scales):
             by_frame = work.tile([P, UNIT // P, N], F32, name="by_frame", bufs=3)
-            bank = aux_psum.tile([P, UNIT // P, N], F32, name="frame_bank", tag="aux")
+            bank = next_bank(UNIT // P)
             for i in range(UNIT // P):
                 cols = slice(P * i, P * (i + 1))
                 nc.tensor.matmul_mx(
@@ -276,26 +311,24 @@ def tile_list_meltab_gain_kernel(
                 )
             for i in range(UNIT // P):
                 nc.scalar.activation(by_frame[:, i, :], bank[:, i, :], ACT.Copy, scale=level_columns[j0 + P * i])
-            turned = aux_psum.tile([P, N // P, UNIT], F32, name="turned_bank", tag="aux")
+            turned = next_bank(N // P)
             for i in range(UNIT // P):
                 for half in range(N // P):
                     nc.tensor.transpose(
                         turned[:, half, P * i : P * (i + 1)], by_frame[:, i, P * half : P * (half + 1)], identity[:]
                     )
-            result = work.tile([P, N // P, UNIT], F32, name="turned_result", bufs=3)
+            result = work.tile([P, N // P, UNIT], F32, name="turned_result", bufs=4)
             nc.scalar.copy(result[:], turned[:])
             store(j0, result)
 
         for j0, width in SCALE_CHUNKS:
             gather_scales(j0, width)
         gather_words(0)
-        gain = staged.tile([P, PACK], F32, name="gain", offset=0)
-        nc.sync.dma_start(gain[:], gn.rearrange("(p t) -> p t", t=PACK))
-        levels = staged.tile([P, T], F32, name="levels", offset=2048)
+        levels = chain.tile([P, T], F32, name="levels", offset=0)
         nc.sync.dma_start(levels[:], ts)
-        fb_codes = early.tile([P, 2 * N], U8, name="fb_codes", offset=0, align_bytes=64)
+        fb_codes = chain.tile([P, 2 * N], U8, name="fb_codes", offset=17664, align_bytes=64)
         nc.sync.dma_start(fb_codes[:].bitcast(I32), fb_words[0].bitcast(I32))
-        fb_scale = staged.tile([P, N], U8, name="fb_scale", offset=256, align_bytes=64)
+        fb_scale = chain.tile([P, N], U8, name="fb_scale", offset=17408, align_bytes=64)
         nc.vector.memset(fb_scale[:].bitcast(I32), 0)
         for q in range(4):
             nc.sync.dma_start(
@@ -312,47 +345,30 @@ def tile_list_meltab_gain_kernel(
             )
             dealt_words.append(tile)
             tile = chain.tile(
-                [P, PASSES, F], U8, name="dealt_scales%d" % part, align_bytes=64, offset=3584 * part
+                [P, PASSES, F], U8, name="dealt_scales%d" % part, align_bytes=64, offset=16384 + 3840 * part
             )
             nc.vector.tensor_copy(
                 tile[:].rearrange("p a (t m) -> p a t m", t=PACK),
                 w_scales[part].rearrange("p a (m t) -> p a t m", t=PACK),
             )
             dealt_scales.append(tile)
-        negated = keep.tile([P, PACK], F32, name="negated")
-        nc.gpsimd.tensor_scalar(negated[:], gain[:], -1.0, TINY, ALU.mult, ALU.max)
-        size = keep.tile([P, PACK], F32, name="size")
-        nc.vector.tensor_tensor(size[:], negated[:], gain[:], ALU.max)
-        half = keep.tile([P, PACK], F32, name="half")
-        nc.gpsimd.memset(half[:], 0.5)
-        guess = keep.tile([P, PACK], F32, name="guess")
-        nc.gpsimd.tensor_tensor(guess[:], size[:], half[:], ALU.pow)
-        inverse = keep.tile([P, PACK], F32, name="inverse")
-        nc.vector.reciprocal(inverse[:], guess[:])
-        quotient = keep.tile([P, PACK], F32, name="quotient")
-        nc.gpsimd.tensor_tensor(quotient[:], size[:], inverse[:], ALU.mult)
-        doubled = keep.tile([P, PACK], F32, name="doubled")
-        nc.gpsimd.tensor_tensor(doubled[:], quotient[:], guess[:], ALU.add)
-        root = keep.tile([P, PACK], F32, name="root")
-        nc.gpsimd.tensor_tensor(root[:], doubled[:], half[:], ALU.mult)
-        signs = keep.tile([P, SIGN_COLS // PACK, PACK], BF16, name="signs")
-        nc.scalar.activation(
-            signs[:], gain[:].unsqueeze(1).to_broadcast([P, SIGN_COLS // PACK, PACK]), ACT.Sign
-        )
-
-        quantized = {}
-        transform_by_frame(0, 2 * UNIT)
-        for step in range(1, UNITS + 2):
-            if 2 <= step < UNITS:
-                if ROUTES[step] == "A":
-                    transform_by_frequency(UNIT * step)
-                else:
-                    transform_by_frame(UNIT * step, UNIT)
-            if step in (1, 3):
-                gather_words(CHUNK * (step + 3) // 2)
-            if step <= UNITS:
-                quantized[step - 1] = power_codes(step - 1)
-                if step % 2 == 1:
-                    gather_levels(UNIT * (step - 1))
-            if step >= 2:
-                (filter_turned if step - 2 in TURNED else filter_direct)(UNIT * (step - 2), *quantized[step - 2])
+        for j0 in range(2 * CHUNK, J, CHUNK):
+            gather_words(j0)
+        for j0 in range(0, J, CHUNK):
+            gather_levels(j0)
+        for step, b in ORDER:
+            road, j0, width = BLOCKS[b]
+            units = range(j0, j0 + width, UNIT)
+            if step == "transform":
+                (transform_by_frame if road == "frame" else transform_by_frequency)(j0, width)
+            elif step == "add":
+                add_by_frame(j0, width)
+            elif step == "quantize":
+                quantize_power(road, j0, width)
+            elif b in TURNED:
+                turn_levels(units)
+                for u0 in units:
+                    filter_turned(u0, *quantized[u0])
+            else:
+                for u0 in units:
+                    filter_direct(u0, *quantized[u0])

@@ -24,13 +24,14 @@ GROUP = 16
 CHUNK = 512
 UNIT = 256
 SCALE_CHUNKS = [(0, 512), (512, 1536)]
+WORD_CHUNKS = [(0, 512), (512, 512), (1024, 512), (1536, 512)]
 SHIFT = 16
 SHIFTED = P - SHIFT
 BANKS = 8
 BANK = 512
 BLOCKS = [("frame", 0, 512), ("frequency", 512, 512), ("frequency", 1024, 512), ("frequency", 1536, 256), ("frequency", 1792, 256)]
-TURNED = [0, 1]
-ORDER = [("transform", 0), ("transform", 1), ("add", 0), ("quantize", 1), ("quantize", 0), ("transform", 2), ("transform", 3), ("quantize", 2), ("filter", 1), ("transform", 4), ("filter", 0), ("quantize", 3), ("filter", 2), ("quantize", 4), ("filter", 3), ("filter", 4)]
+TURNED = [0, 1, 2, 3]
+ORDER = [("transform", 0), ("transform", 1), ("add", 0), ("quantize", 1), ("quantize", 0), ("transform", 2), ("levels", 2), ("transform", 3), ("filter", 2), ("filter", 3), ("quantize", 2), ("transform", 4), ("turn", 2), ("turn", 3), ("levels", 0), ("filter", 0), ("filter", 1), ("quantize", 3), ("filter", 4), ("filter", 5), ("turn", 0), ("turn", 1), ("quantize", 4), ("filter", 6), ("filter", 7)]
 SIGN_COLS = 128
 TINY = 2.0**-110
 
@@ -69,7 +70,8 @@ def tile_list_meltab_gain_kernel(
             w_words.append(tile)
 
         scale_table = keep.tile([P, T // 4], I32, name="scale_table", align_bytes=64)
-        nc.vector.memset(scale_table[:], 0)
+        nc.gpsimd.memset(scale_table[:, : T // 8], 0)
+        nc.vector.memset(scale_table[:, T // 8 :], 0)
         for r in range(4):
             (nc.sync, nc.scalar)[r % 2].dma_start(
                 scale_table[r:P:SHIFT, :], tab_scales[:, r:16:4, :].rearrange("a q t -> q a t").bitcast(I32)
@@ -79,13 +81,13 @@ def tile_list_meltab_gain_kernel(
         for j0, width in SCALE_CHUNKS:
             scale_pass1[j0] = keep.tile([P, width // 4], I32, name="scale_pass1_%d" % j0, align_bytes=64)
         blank = behind.tile([P, P], I32, name="blank", offset=4 * T - 2 * P, align_bytes=64)
-        nc.vector.memset(blank[:], 0)
+        nc.gpsimd.memset(blank[:], 0)
         nc.vector.tensor_copy(scale_pass1[0][:], blank[:])
         word_table = behind.tile([P, T], I32, name="word_table", offset=0, align_bytes=64)
         nc.sync.dma_start(word_table[:], tab_words[0].rearrange("p t b -> p (t b)").bitcast(I32))
 
         w_planes = behind.tile([P, 2 * PASSES * F], U8, name="w_planes", offset=4 * T, align_bytes=64)
-        nc.vector.memset(w_planes[:].bitcast(I32), 0)
+        nc.gpsimd.memset(w_planes[:].bitcast(I32), 0)
         for part, scales in enumerate((co_scales, si_scales)):
             for q in range(4):
                 nc.sync.dma_start(
@@ -99,7 +101,7 @@ def tile_list_meltab_gain_kernel(
             for part in range(2)
         ]
 
-        nc.vector.memset(scale_pass1[CHUNK][:], 0)
+        nc.gpsimd.memset(scale_pass1[CHUNK][:], 0)
         identity = keep.tile([P, P], F32, name="identity")
         make_identity(nc, identity[:])
 
@@ -131,14 +133,14 @@ def tile_list_meltab_gain_kernel(
 
         frames = {}
 
-        def gather_words(j0):
+        def gather_words(j0, width):
             if j0 == 0:
-                picked = chain.tile([P, CHUNK], U32, name="first_words", align_bytes=64, offset=16320)
+                picked = chain.tile([P, width], U32, name="first_words", align_bytes=64, offset=16320)
             else:
-                picked = chain.tile([P, CHUNK], U32, name="picked_words", align_bytes=64, offset=18176)
-            nc.vector.tensor_copy(picked[:], word_table[:].bitcast(U32).indirect(listed(j0, CHUNK)))
-            step = UNIT if j0 == 0 else CHUNK
-            for c0 in range(0, CHUNK, step):
+                picked = chain.tile([P, width], U32, name="picked_words", align_bytes=64, offset=18176)
+            nc.vector.tensor_copy(picked[:], word_table[:].bitcast(U32).indirect(listed(j0, width)))
+            step = UNIT if j0 == 0 else width
+            for c0 in range(0, width, step):
                 parted = keep.tile([P, PASSES, 2 * step], U8, name="frames%d" % (j0 + c0), align_bytes=64)
                 nc.vector.tensor_copy(
                     parted[:].bitcast(U16),
@@ -157,9 +159,9 @@ def tile_list_meltab_gain_kernel(
         level_columns = {}
 
         def gather_levels(j0):
-            picked = keep.tile([P, CHUNK], F32, name="picked_levels%d" % j0)
-            nc.vector.tensor_copy(picked[:], levels[:].indirect(listed(j0, CHUNK)))
-            for u0 in range(0, CHUNK, UNIT):
+            picked = keep.tile([P, 2 * CHUNK], F32, name="picked_levels%d" % j0)
+            nc.vector.tensor_copy(picked[:], levels[:].indirect(listed(j0, 2 * CHUNK)))
+            for u0 in range(0, 2 * CHUNK, UNIT):
                 picked_levels[j0 + u0] = picked[:, u0 : u0 + UNIT]
 
         def turn_levels(units):
@@ -274,29 +276,36 @@ def tile_list_meltab_gain_kernel(
             for u0 in range(0, width, UNIT):
                 quantized[j0 + u0] = codes[:, u0 : u0 + UNIT], scales[:, u0 : u0 + UNIT]
 
-        def store(j0, result):
-            nc.sync.dma_start(out[:, j0 : j0 + UNIT].rearrange("(h p) j -> p h j", p=P), result[:])
+        def store(j0, width, result):
+            nc.sync.dma_start(out[:, j0 : j0 + width].rearrange("(h p) j -> p h j", p=P), result)
 
         def filter_direct(j0, codes, scales):
-            result = work.tile([P, N // P, UNIT], F32, name="result", bufs=4)
-            bank = next_bank(N // P)
-            for half in range(N // P):
-                nc.tensor.matmul_mx(
-                    out=bank[:, half, :],
-                    lhsT=fb_codes[:, 2 * P * half : 2 * P * (half + 1)].bitcast(FP4X4),
-                    lhsT_scale=fb_scale[:, P * half : P * (half + 1)],
-                    rhs=codes.bitcast(FP8X4),
-                    rhs_scale=scales,
-                    start=True,
-                    stop=True,
+            width = P if j0 + UNIT == J else UNIT
+            for c0 in range(0, UNIT, width):
+                result = work.tile([P, N // P, width], F32, name="result", bufs=4)
+                bank = next_bank(N // P)
+                for half in range(N // P):
+                    nc.tensor.matmul_mx(
+                        out=bank[:, half, 0:width],
+                        lhsT=fb_codes[:, 2 * P * half : 2 * P * (half + 1)].bitcast(FP4X4),
+                        lhsT_scale=fb_scale[:, P * half : P * (half + 1)],
+                        rhs=codes[:, c0 : c0 + width].bitcast(FP8X4),
+                        rhs_scale=scales[:, c0 : c0 + width],
+                        start=True,
+                        stop=True,
+                    )
+                nc.vector.tensor_tensor(
+                    result[:],
+                    bank[:, :, 0:width],
+                    picked_levels[j0][:, c0 : c0 + width].unsqueeze(1).to_broadcast([P, N // P, width]),
+                    ALU.mult,
                 )
-            nc.vector.tensor_tensor(
-                result[:], bank[:], picked_levels[j0].unsqueeze(1).to_broadcast([P, N // P, UNIT]), ALU.mult
-            )
-            store(j0, result)
+                store(j0 + c0, width, result[:])
+
+        scaled = {}
 
         def filter_turned(j0, codes, scales):
-            by_frame = work.tile([P, UNIT // P, N], F32, name="by_frame", bufs=3)
+            by_frame = work.tile([P, UNIT // P, N], F32, name="by_frame", bufs=4)
             bank = next_bank(UNIT // P)
             for i in range(UNIT // P):
                 cols = slice(P * i, P * (i + 1))
@@ -311,6 +320,10 @@ def tile_list_meltab_gain_kernel(
                 )
             for i in range(UNIT // P):
                 nc.scalar.activation(by_frame[:, i, :], bank[:, i, :], ACT.Copy, scale=level_columns[j0 + P * i])
+            scaled[j0] = by_frame
+
+        def turn_back(j0):
+            by_frame = scaled[j0]
             turned = next_bank(N // P)
             for i in range(UNIT // P):
                 for half in range(N // P):
@@ -319,22 +332,22 @@ def tile_list_meltab_gain_kernel(
                     )
             result = work.tile([P, N // P, UNIT], F32, name="turned_result", bufs=4)
             nc.scalar.copy(result[:], turned[:])
-            store(j0, result)
+            store(j0, UNIT, result[:])
 
         for j0, width in SCALE_CHUNKS:
             gather_scales(j0, width)
-        gather_words(0)
+        gather_words(*WORD_CHUNKS[0])
         levels = chain.tile([P, T], F32, name="levels", offset=0)
         nc.sync.dma_start(levels[:], ts)
         fb_codes = chain.tile([P, 2 * N], U8, name="fb_codes", offset=17664, align_bytes=64)
         nc.sync.dma_start(fb_codes[:].bitcast(I32), fb_words[0].bitcast(I32))
         fb_scale = chain.tile([P, N], U8, name="fb_scale", offset=17408, align_bytes=64)
-        nc.vector.memset(fb_scale[:].bitcast(I32), 0)
+        nc.gpsimd.memset(fb_scale[:].bitcast(I32), 0)
         for q in range(4):
             nc.sync.dma_start(
                 fb_scale[32 * q : 32 * q + 4, :].bitcast(I32), fb_scales[0, 4 * q : 4 * q + 4, :].bitcast(I32)
             )
-        gather_words(CHUNK)
+        gather_words(*WORD_CHUNKS[1])
 
         dealt_words, dealt_scales = [], []
         for part in range(2):
@@ -344,31 +357,28 @@ def tile_list_meltab_gain_kernel(
                 w_words[part][:].bitcast(U16).rearrange("p a (m t) -> p a t m", t=PACK),
             )
             dealt_words.append(tile)
-            tile = chain.tile(
-                [P, PASSES, F], U8, name="dealt_scales%d" % part, align_bytes=64, offset=16384 + 3840 * part
-            )
+            tile = keep.tile([P, PASSES, F], U8, name="dealt_scales%d" % part, align_bytes=64)
             nc.vector.tensor_copy(
                 tile[:].rearrange("p a (t m) -> p a t m", t=PACK),
                 w_scales[part].rearrange("p a (m t) -> p a t m", t=PACK),
             )
             dealt_scales.append(tile)
-        for j0 in range(2 * CHUNK, J, CHUNK):
-            gather_words(j0)
-        for j0 in range(0, J, CHUNK):
+        for j0, width in WORD_CHUNKS[2:]:
+            gather_words(j0, width)
+        for j0 in range(0, J, 2 * CHUNK):
             gather_levels(j0)
         for step, b in ORDER:
-            road, j0, width = BLOCKS[b]
-            units = range(j0, j0 + width, UNIT)
-            if step == "transform":
-                (transform_by_frame if road == "frame" else transform_by_frequency)(j0, width)
-            elif step == "add":
-                add_by_frame(j0, width)
-            elif step == "quantize":
-                quantize_power(road, j0, width)
-            elif b in TURNED:
-                turn_levels(units)
-                for u0 in units:
-                    filter_turned(u0, *quantized[u0])
+            if step == "filter":
+                (filter_turned if b in TURNED else filter_direct)(UNIT * b, *quantized[UNIT * b])
+            elif step == "turn":
+                turn_back(UNIT * b)
+            elif step == "levels":
+                turn_levels([UNIT * b, UNIT * (b + 1)])
             else:
-                for u0 in units:
-                    filter_direct(u0, *quantized[u0])
+                road, j0, width = BLOCKS[b]
+                if step == "transform":
+                    (transform_by_frame if road == "frame" else transform_by_frequency)(j0, width)
+                elif step == "add":
+                    add_by_frame(j0, width)
+                else:
+                    quantize_power(road, j0, width)

@@ -30,8 +30,8 @@ SHIFTED = P - SHIFT
 BANKS = 8
 BANK = 512
 BLOCKS = [("frame", 0, 512), ("frequency", 512, 512), ("frequency", 1024, 512), ("frequency", 1536, 256), ("frequency", 1792, 256)]
-TURNED = [0, 1, 2, 3]
-ORDER = [("transform", 0), ("transform", 1), ("add", 0), ("quantize", 1), ("quantize", 0), ("transform", 2), ("levels", 2), ("transform", 3), ("filter", 2), ("filter", 3), ("quantize", 2), ("transform", 4), ("turn", 2), ("turn", 3), ("levels", 0), ("filter", 0), ("filter", 1), ("quantize", 3), ("filter", 4), ("filter", 5), ("turn", 0), ("turn", 1), ("quantize", 4), ("filter", 6), ("filter", 7)]
+TURNED = [0, 1, 4]
+ORDER = [("transform", 0), ("transform", 1), ("add", 0), ("quantize", 1), ("quantize", 0), ("transform", 2), ("filter", 2), ("filter", 3), ("transform", 3), ("levels", 0), ("filter", 0), ("filter", 1), ("quantize", 2), ("transform", 4), ("turn", 0), ("turn", 1), ("levels", 4), ("filter", 4), ("quantize", 3), ("filter", 5), ("turn", 4), ("quantize", 4), ("filter", 6), ("filter", 7)]
 SIGN_COLS = 128
 TINY = 2.0**-110
 
@@ -373,7 +373,7 @@ def tile_list_meltab_gain_kernel(
             elif step == "turn":
                 turn_back(UNIT * b)
             elif step == "levels":
-                turn_levels([UNIT * b, UNIT * (b + 1)])
+                turn_levels([UNIT * u for u in (b, b + 1) if u in TURNED])
             else:
                 road, j0, width = BLOCKS[b]
                 if step == "transform":

@@ -32,6 +32,7 @@ BANK = 512
 BLOCKS = [("frame", 0, 512), ("frequency", 512, 512), ("frequency", 1024, 512), ("frequency", 1536, 256), ("frequency", 1792, 256)]
 TURNED = [0, 1, 4]
 ORDER = [("transform", 0), ("transform", 1), ("add", 0), ("quantize", 1), ("quantize", 0), ("transform", 2), ("filter", 2), ("filter", 3), ("transform", 3), ("levels", 0), ("filter", 0), ("filter", 1), ("quantize", 2), ("transform", 4), ("turn", 0), ("turn", 1), ("levels", 4), ("filter", 4), ("quantize", 3), ("filter", 5), ("turn", 4), ("quantize", 4), ("filter", 6), ("filter", 7)]
+WARM_UPS = 4
 SIGN_COLS = 128
 TINY = 2.0**-110
 
@@ -166,13 +167,11 @@ def tile_list_meltab_gain_kernel(
 
         def turn_levels(units):
             tiles = [j0 + c0 for j0 in units for c0 in range(0, UNIT, P)]
-            bank = next_bank(BANK // P)
-            for i, j in enumerate(tiles):
-                nc.tensor.transpose(bank[:, i, :], picked_levels[j - j % UNIT][:, j % UNIT : j % UNIT + P], identity[:])
-            column = keep.tile([P, len(tiles)], F32, name="level_columns%d" % units[0])
-            nc.scalar.copy(column[:], bank[:, 0 : len(tiles), 0])
-            for i, j in enumerate(tiles):
-                level_columns[j] = column[:, i : i + 1]
+            for j in tiles:
+                column = keep.tile([P, 1], F32, name="level_column%d" % j)
+                with nc.allow_non_contiguous_dma(reason="a row of levels becomes a column"):
+                    nc.sync.dma_start(column[:], picked_levels[j - j % UNIT][0:1, j % UNIT : j % UNIT + P])
+                level_columns[j] = column[:]
 
         squares = {}
 
@@ -336,6 +335,17 @@ def tile_list_meltab_gain_kernel(
 
         for j0, width in SCALE_CHUNKS:
             gather_scales(j0, width)
+        unread = next_bank(1)
+        for n in range(WARM_UPS):
+            nc.tensor.matmul_mx(
+                out=unread[:, 0, :],
+                lhsT=w_words[0][:, 0, 0 : 2 * P].bitcast(FP4X4),
+                lhsT_scale=scale_pass0[CHUNK][:, 0:P],
+                rhs=w_words[0][:, 0, :].bitcast(FP4X4),
+                rhs_scale=scale_pass0[CHUNK][:, 0:F],
+                start=True,
+                stop=True,
+            )
         gather_words(*WORD_CHUNKS[0])
         levels = chain.tile([P, T], F32, name="levels", offset=0)
         nc.sync.dma_start(levels[:], ts)

@@ -23,16 +23,13 @@ PASSES = K // (P * PACK)
 GROUP = 16
 CHUNK = 512
 UNIT = 256
-SCALE_CHUNKS = [(0, 512), (512, 1536)]
 WORD_CHUNKS = [(0, 512), (512, 512), (1024, 512), (1536, 512)]
-SHIFT = 16
-SHIFTED = P - SHIFT
+LIVE = 96
 BANKS = 8
 BANK = 512
 BLOCKS = [("frame", 0, 512), ("frequency", 512, 512), ("frequency", 1024, 512), ("frequency", 1536, 256), ("frequency", 1792, 256)]
 TURNED = [0, 1, 4]
 ORDER = [("transform", 0), ("transform", 1), ("add", 0), ("quantize", 1), ("quantize", 0), ("transform", 2), ("filter", 2), ("filter", 3), ("transform", 3), ("levels", 0), ("filter", 0), ("filter", 1), ("quantize", 2), ("transform", 4), ("turn", 0), ("turn", 1), ("levels", 4), ("filter", 4), ("quantize", 3), ("filter", 5), ("turn", 4), ("quantize", 4), ("filter", 6), ("filter", 7)]
-WARM_UPS = 4
 SIGN_COLS = 128
 TINY = 2.0**-110
 
@@ -61,8 +58,12 @@ def tile_list_meltab_gain_kernel(
         def listed(j0, width):
             return offsets[:, j0 // GROUP : (j0 + width) // GROUP]
 
+        scale_table = behind.tile([P, T // 4], I32, name="scale_table", align_bytes=64, offset=2048)
+        nc.scalar.dma_start(scale_table[LIVE:P, :], tab_scales.rearrange("a q t -> (a q) t").bitcast(I32))
         gain = keep.tile([P, PACK], F32, name="gain")
         nc.scalar.dma_start(gain[:], gn.rearrange("(p t) -> p t", t=PACK))
+        word_table = keep.tile([P, T], I32, name="word_table", align_bytes=64)
+        nc.sync.dma_start(word_table[:], tab_words[0].rearrange("p t b -> p (t b)").bitcast(I32))
 
         w_words = []
         for part, words in enumerate((co_words, si_words)):
@@ -70,67 +71,54 @@ def tile_list_meltab_gain_kernel(
             nc.scalar.dma_start(tile[:].bitcast(I32), words.rearrange("a p b -> p a b").bitcast(I32))
             w_words.append(tile)
 
-        scale_table = keep.tile([P, T // 4], I32, name="scale_table", align_bytes=64)
-        nc.gpsimd.memset(scale_table[:, : T // 8], 0)
-        nc.vector.memset(scale_table[:, T // 8 :], 0)
-        for r in range(4):
-            (nc.sync, nc.scalar)[r % 2].dma_start(
-                scale_table[r:P:SHIFT, :], tab_scales[:, r:16:4, :].rearrange("a q t -> q a t").bitcast(I32)
-            )
+        w_scales = []
 
-        scale_pass1 = {}
-        for j0, width in SCALE_CHUNKS:
-            scale_pass1[j0] = keep.tile([P, width // 4], I32, name="scale_pass1_%d" % j0, align_bytes=64)
-        blank = behind.tile([P, P], I32, name="blank", offset=4 * T - 2 * P, align_bytes=64)
-        nc.gpsimd.memset(blank[:], 0)
-        nc.vector.tensor_copy(scale_pass1[0][:], blank[:])
-        word_table = behind.tile([P, T], I32, name="word_table", offset=0, align_bytes=64)
-        nc.sync.dma_start(word_table[:], tab_words[0].rearrange("p t b -> p (t b)").bitcast(I32))
-
-        w_planes = behind.tile([P, 2 * PASSES * F], U8, name="w_planes", offset=4 * T, align_bytes=64)
-        nc.gpsimd.memset(w_planes[:].bitcast(I32), 0)
-        for part, scales in enumerate((co_scales, si_scales)):
+        def load_planes(clearer, planes, scales, queues):
+            clearer.memset(planes[:].bitcast(I32), 0)
             for q in range(4):
-                nc.sync.dma_start(
-                    w_planes[32 * q : 32 * q + 4, PASSES * F * part : PASSES * F * (part + 1)]
-                    .bitcast(I32)
-                    .rearrange("r (a f) -> r a f", a=PASSES),
+                queues[q % len(queues)].dma_start(
+                    planes[32 * q : 32 * q + 4, :].bitcast(I32).rearrange("r (a f) -> r a f", a=PASSES),
                     scales[:, 4 * q : 4 * q + 4, :].rearrange("a r f -> r a f").bitcast(I32),
                 )
-        w_scales = [
-            w_planes[:, PASSES * F * part : PASSES * F * (part + 1)].rearrange("p (a f) -> p a f", a=PASSES)
-            for part in range(2)
-        ]
+            w_scales.append(planes[:].rearrange("p (a f) -> p a f", a=PASSES))
 
-        nc.gpsimd.memset(scale_pass1[CHUNK][:], 0)
+        co_planes = keep.tile([P, PASSES * F], U8, name="co_planes", align_bytes=64)
+        load_planes(nc.vector, co_planes, co_scales, [nc.scalar])
+        nc.vector.memset(scale_table[0:LIVE, :], 0)
+
+        frame_scales = []
+        for a in range(PASSES):
+            plane = keep.tile([P, J // 4], I32, name="frame_scales%d" % a, align_bytes=64)
+            nc.gpsimd.memset(plane[:], 0)
+            frame_scales.append(plane)
         identity = keep.tile([P, P], F32, name="identity")
         make_identity(nc, identity[:])
 
-        negated = keep.tile([P, PACK], F32, name="negated")
-        nc.vector.tensor_scalar(negated[:], gain[:], -1.0, TINY, ALU.mult, ALU.max)
-        size = keep.tile([P, PACK], F32, name="size")
-        nc.vector.tensor_tensor(size[:], negated[:], gain[:], ALU.max)
+        picked_scales = keep.tile([P, J], U8, name="picked_scales", align_bytes=64)
+        nc.vector.tensor_copy(picked_scales[:], scale_table[:].bitcast(U8).indirect(offsets[:]))
+        for a in range(PASSES):
+            for q in range(4):
+                first = LIVE + 16 * a + 4 * q
+                nc.sync.dma_start(
+                    frame_scales[a][32 * q : 32 * q + 4, :], picked_scales[first : first + 4, :].bitcast(I32)
+                )
+        si_planes = behind.tile([P, PASSES * F], U8, name="si_planes", align_bytes=64, offset=2112)
+        load_planes(nc.gpsimd, si_planes, si_scales, [nc.sync])
+
+        quarter = keep.tile([P, PACK], F32, name="quarter")
+        nc.scalar.activation(quarter[:], gain[:], ACT.Abs, scale=0.25)
+        floor = keep.tile([P, 1], F32, name="floor")
+        nc.gpsimd.memset(floor[:], TINY)
         half_guess = keep.tile([P, PACK], F32, name="half_guess")
-        nc.scalar.activation(half_guess[:], size[:], ACT.Sqrt, scale=0.25)
-        spread = gain[:].unsqueeze(1).to_broadcast([P, SIGN_COLS // PACK, PACK])
-        below = keep.tile([P, SIGN_COLS // PACK, PACK], F32, name="below")
-        nc.vector.tensor_scalar(below[:], spread, 0.0, None, ALU.is_lt)
+        nc.scalar.activation(half_guess[:], quarter[:], ACT.Sqrt, bias=floor[:])
         signs = keep.tile([P, SIGN_COLS // PACK, PACK], BF16, name="signs")
-        nc.vector.scalar_tensor_tensor(signs[:], spread, 0.0, below[:], ALU.is_gt, ALU.subtract)
+        nc.scalar.activation(signs[:], gain[:].unsqueeze(1).to_broadcast([P, SIGN_COLS // PACK, PACK]), ACT.Sign)
         inverse = keep.tile([P, PACK], F32, name="inverse")
         nc.vector.reciprocal(inverse[:], half_guess[:])
         half_quotient = keep.tile([P, PACK], F32, name="half_quotient")
-        nc.vector.scalar_tensor_tensor(half_quotient[:], size[:], 0.25, inverse[:], ALU.mult, ALU.mult)
+        nc.vector.tensor_tensor(half_quotient[:], quarter[:], inverse[:], ALU.mult)
         root = keep.tile([P, PACK], F32, name="root")
         nc.vector.tensor_tensor(root[:], half_quotient[:], half_guess[:], ALU.add)
-
-        scale_pass0 = {}
-
-        def gather_scales(j0, width):
-            picked = keep.tile([P, width], U8, name="picked_scales%d" % j0, align_bytes=64)
-            nc.vector.tensor_copy(picked[:], scale_table[:].bitcast(U8).indirect(listed(j0, width)))
-            nc.scalar.dma_start(scale_pass1[j0][0:SHIFTED, :], picked[SHIFT:P, :].bitcast(I32))
-            scale_pass0[j0] = picked
 
         frames = {}
 
@@ -152,9 +140,7 @@ def tile_list_meltab_gain_kernel(
         def frame_operand(j0, width, a):
             first = max(j for j in frames if j <= j0)
             words = frames[first][:, a, 2 * (j0 - first) : 2 * (j0 - first + width)].bitcast(FP4X4)
-            first = max(j for j in scale_pass0 if j <= j0)
-            plane = (scale_pass0[first][:], scale_pass1[first][:].bitcast(U8))[a]
-            return words, plane[:, j0 - first : j0 - first + width]
+            return words, frame_scales[a][:].bitcast(U8)[:, j0 : j0 + width]
 
         picked_levels = {}
         level_columns = {}
@@ -333,19 +319,19 @@ def tile_list_meltab_gain_kernel(
             nc.scalar.copy(result[:], turned[:])
             store(j0, UNIT, result[:])
 
-        for j0, width in SCALE_CHUNKS:
-            gather_scales(j0, width)
-        unread = next_bank(1)
-        for n in range(WARM_UPS):
-            nc.tensor.matmul_mx(
-                out=unread[:, 0, :],
-                lhsT=w_words[0][:, 0, 0 : 2 * P].bitcast(FP4X4),
-                lhsT_scale=scale_pass0[CHUNK][:, 0:P],
-                rhs=w_words[0][:, 0, :].bitcast(FP4X4),
-                rhs_scale=scale_pass0[CHUNK][:, 0:F],
-                start=True,
-                stop=True,
+        dealt_words, dealt_scales = [], []
+
+        def deal_words(part):
+            tile = behind.tile(
+                [P, PASSES, 2 * F], U8, name="dealt_words%d" % part, align_bytes=64, offset=(64, 3136)[part]
             )
+            nc.vector.tensor_copy(
+                tile[:].bitcast(U16).rearrange("p a (t m) -> p a t m", t=PACK),
+                w_words[part][:].bitcast(U16).rearrange("p a (m t) -> p a t m", t=PACK),
+            )
+            dealt_words.append(tile)
+
+        deal_words(0)
         gather_words(*WORD_CHUNKS[0])
         levels = chain.tile([P, T], F32, name="levels", offset=0)
         nc.sync.dma_start(levels[:], ts)
@@ -359,14 +345,8 @@ def tile_list_meltab_gain_kernel(
             )
         gather_words(*WORD_CHUNKS[1])
 
-        dealt_words, dealt_scales = [], []
+        deal_words(1)
         for part in range(2):
-            tile = keep.tile([P, PASSES, 2 * F], U8, name="dealt_words%d" % part, align_bytes=64)
-            nc.vector.tensor_copy(
-                tile[:].bitcast(U16).rearrange("p a (t m) -> p a t m", t=PACK),
-                w_words[part][:].bitcast(U16).rearrange("p a (m t) -> p a t m", t=PACK),
-            )
-            dealt_words.append(tile)
             tile = keep.tile([P, PASSES, F], U8, name="dealt_scales%d" % part, align_bytes=64)
             nc.vector.tensor_copy(
                 tile[:].rearrange("p a (t m) -> p a t m", t=PACK),

@@ -28,8 +28,8 @@ LIVE = 96
 BANKS = 8
 BANK = 512
 BLOCKS = [("frame", 0, 512), ("frequency", 512, 512), ("frequency", 1024, 512), ("frequency", 1536, 256), ("frequency", 1792, 256)]
-TURNED = [0, 1, 4]
-ORDER = [("transform", 0), ("transform", 1), ("add", 0), ("quantize", 1), ("quantize", 0), ("transform", 2), ("filter", 2), ("filter", 3), ("transform", 3), ("levels", 0), ("filter", 0), ("filter", 1), ("quantize", 2), ("transform", 4), ("turn", 0), ("turn", 1), ("levels", 4), ("filter", 4), ("quantize", 3), ("filter", 5), ("turn", 4), ("quantize", 4), ("filter", 6), ("filter", 7)]
+TURNED = [0, 2, 3, 4]
+ORDER = [("transform", 0), ("transform", 1), ("transform", 2), ("add", 0), ("quantize", 1), ("quantize", 2), ("quantize", 0), ("levels", 2), ("filter", 2), ("filter", 3), ("transform", 3), ("levels", 4), ("filter", 5), ("filter", 4), ("quantize", 3), ("transform", 4), ("turn", 2), ("turn", 3), ("levels", 0), ("filter", 1), ("filter", 0), ("turn", 4), ("quantize", 4), ("filter", 6), ("turn", 0), ("filter", 7)]
 SIGN_COLS = 128
 TINY = 2.0**-110
 
@@ -115,10 +115,12 @@ def tile_list_meltab_gain_kernel(
         nc.scalar.activation(signs[:], gain[:].unsqueeze(1).to_broadcast([P, SIGN_COLS // PACK, PACK]), ACT.Sign)
         inverse = keep.tile([P, PACK], F32, name="inverse")
         nc.vector.reciprocal(inverse[:], half_guess[:])
-        half_quotient = keep.tile([P, PACK], F32, name="half_quotient")
-        nc.vector.tensor_tensor(half_quotient[:], quarter[:], inverse[:], ALU.mult)
         root = keep.tile([P, PACK], F32, name="root")
-        nc.vector.tensor_tensor(root[:], half_quotient[:], half_guess[:], ALU.add)
+        for t in range(PACK):
+            column = slice(t, t + 1)
+            nc.scalar.activation(
+                root[:, column], inverse[:, column], ACT.Identity, bias=half_guess[:, column], scale=quarter[:, column]
+            )
 
         frames = {}
 

@@ -324,10 +324,8 @@ def tile_list_meltab_gain_kernel(
         dealt_words, dealt_scales = [], []
 
         def deal_words(part):
-            tile = behind.tile(
-                [P, PASSES, 2 * F], U8, name="dealt_words%d" % part, align_bytes=64, offset=(64, 3136)[part]
-            )
-            nc.vector.tensor_copy(
+            tile = keep.tile([P, PASSES, 2 * F], U8, name="dealt_words%d" % part, align_bytes=64)
+            nc.scalar.copy(
                 tile[:].bitcast(U16).rearrange("p a (t m) -> p a t m", t=PACK),
                 w_words[part][:].bitcast(U16).rearrange("p a (m t) -> p a t m", t=PACK),
             )

@@ -24,6 +24,7 @@ GROUP = 16
 CHUNK = 512
 UNIT = 256
 WORD_CHUNKS = [(0, 512), (512, 512), (1024, 512), (1536, 512)]
+WARM_UPS = 6
 LIVE = 96
 BANKS = 8
 BANK = 512
@@ -357,6 +358,17 @@ def tile_list_meltab_gain_kernel(
             gather_words(j0, width)
         for j0 in range(0, J, 2 * CHUNK):
             gather_levels(j0)
+        idle = next_bank(1)
+        for i in range(WARM_UPS):
+            nc.tensor.matmul_mx(
+                out=idle[:, 0, :],
+                lhsT=dealt_words[0][:, 0, 0 : 2 * P].bitcast(FP4X4),
+                lhsT_scale=w_scales[0][:, 0, 0:P],
+                rhs=w_words[0][:, 0, :].bitcast(FP4X4),
+                rhs_scale=w_scales[0][:, 0, :],
+                start=True,
+                stop=True,
+            )
         for step, b in ORDER:
             if step == "filter":
                 (filter_turned if b in TURNED else filter_direct)(UNIT * b, *quantized[UNIT * b])

@@ -62,29 +62,43 @@ def tile_list_meltab_gain_kernel(
         scale_table = behind.tile([P, T // 4], I32, name="scale_table", align_bytes=64, offset=2048)
         nc.scalar.dma_start(scale_table[LIVE:P, :], tab_scales.rearrange("a q t -> (a q) t").bitcast(I32))
         gain = keep.tile([P, PACK], F32, name="gain")
-        nc.scalar.dma_start(gain[:], gn.rearrange("(p t) -> p t", t=PACK))
-        word_table = keep.tile([P, T], I32, name="word_table", align_bytes=64)
-        nc.sync.dma_start(word_table[:], tab_words[0].rearrange("p t b -> p (t b)").bitcast(I32))
+        nc.sync.dma_start(gain[:], gn.rearrange("(p t) -> p t", t=PACK))
+        quarter = keep.tile([P, PACK], F32, name="quarter")
+        nc.scalar.activation(quarter[:], gain[:], ACT.Abs, scale=0.25)
+        floor = keep.tile([P, 1], F32, name="floor")
+        nc.vector.memset(floor[:], TINY)
+        half_guess = keep.tile([P, PACK], F32, name="half_guess")
+        nc.scalar.activation(half_guess[:], quarter[:], ACT.Sqrt, bias=floor[:])
+        signs = keep.tile([P, SIGN_COLS // PACK, PACK], BF16, name="signs")
+        nc.scalar.activation(signs[:], gain[:].unsqueeze(1).to_broadcast([P, SIGN_COLS // PACK, PACK]), ACT.Sign)
+        inverse = keep.tile([P, PACK], F32, name="inverse")
+        nc.vector.reciprocal(inverse[:], half_guess[:])
+
 
         w_words = []
         for part, words in enumerate((co_words, si_words)):
             tile = keep.tile([P, PASSES, 2 * F], U8, name="w_words%d" % part, align_bytes=64)
-            nc.scalar.dma_start(tile[:].bitcast(I32), words.rearrange("a p b -> p a b").bitcast(I32))
+            nc.sync.dma_start(tile[:].bitcast(I32), words.rearrange("a p b -> p a b").bitcast(I32))
             w_words.append(tile)
 
         w_scales = []
 
+        word_table = keep.tile([P, T], I32, name="word_table", align_bytes=64)
+        nc.sync.dma_start(word_table[:], tab_words[0].rearrange("p t b -> p (t b)").bitcast(I32))
+
         def load_planes(clearer, planes, scales, queues):
             clearer.memset(planes[:].bitcast(I32), 0)
             for q in range(4):
-                queues[q % len(queues)].dma_start(
+                queues[q].dma_start(
                     planes[32 * q : 32 * q + 4, :].bitcast(I32).rearrange("r (a f) -> r a f", a=PASSES),
                     scales[:, 4 * q : 4 * q + 4, :].rearrange("a r f -> r a f").bitcast(I32),
                 )
             w_scales.append(planes[:].rearrange("p (a f) -> p a f", a=PASSES))
 
         co_planes = keep.tile([P, PASSES * F], U8, name="co_planes", align_bytes=64)
-        load_planes(nc.vector, co_planes, co_scales, [nc.scalar])
+        load_planes(nc.vector, co_planes, co_scales, [nc.scalar] * 4)
+        si_planes = keep.tile([P, PASSES * F], U8, name="si_planes", align_bytes=64)
+        load_planes(nc.vector, si_planes, si_scales, [nc.scalar] * 4)
         nc.vector.memset(scale_table[0:LIVE, :], 0)
 
         frame_scales = []
@@ -95,33 +109,22 @@ def tile_list_meltab_gain_kernel(
         identity = keep.tile([P, P], F32, name="identity")
         make_identity(nc, identity[:])
 
-        picked_scales = keep.tile([P, J], U8, name="picked_scales", align_bytes=64)
+        picked_scales = behind.tile([P, J], U8, name="picked_scales", align_bytes=64, offset=0)
         nc.vector.tensor_copy(picked_scales[:], scale_table[:].bitcast(U8).indirect(offsets[:]))
-        for a in range(PASSES):
+        for a in reversed(range(PASSES)):
             for q in range(4):
                 first = LIVE + 16 * a + 4 * q
                 nc.sync.dma_start(
                     frame_scales[a][32 * q : 32 * q + 4, :], picked_scales[first : first + 4, :].bitcast(I32)
                 )
-        si_planes = behind.tile([P, PASSES * F], U8, name="si_planes", align_bytes=64, offset=2112)
-        load_planes(nc.gpsimd, si_planes, si_scales, [nc.sync])
-
-        quarter = keep.tile([P, PACK], F32, name="quarter")
-        nc.scalar.activation(quarter[:], gain[:], ACT.Abs, scale=0.25)
-        floor = keep.tile([P, 1], F32, name="floor")
-        nc.gpsimd.memset(floor[:], TINY)
-        half_guess = keep.tile([P, PACK], F32, name="half_guess")
-        nc.scalar.activation(half_guess[:], quarter[:], ACT.Sqrt, bias=floor[:])
-        signs = keep.tile([P, SIGN_COLS // PACK, PACK], BF16, name="signs")
-        nc.scalar.activation(signs[:], gain[:].unsqueeze(1).to_broadcast([P, SIGN_COLS // PACK, PACK]), ACT.Sign)
-        inverse = keep.tile([P, PACK], F32, name="inverse")
-        nc.vector.reciprocal(inverse[:], half_guess[:])
-        root = keep.tile([P, PACK], F32, name="root")
+        root = behind.tile([P, PACK], F32, name="root", offset=0)
         for t in range(PACK):
             column = slice(t, t + 1)
             nc.scalar.activation(
                 root[:, column], inverse[:, column], ACT.Identity, bias=half_guess[:, column], scale=quarter[:, column]
             )
+        levels = behind.tile([P, T], F32, name="levels", offset=2048 + T - 64)
+        nc.sync.dma_start(levels[:], ts)
 
         frames = {}
 
@@ -334,12 +337,10 @@ def tile_list_meltab_gain_kernel(
 
         deal_words(0)
         gather_words(*WORD_CHUNKS[0])
-        levels = chain.tile([P, T], F32, name="levels", offset=0)
-        nc.sync.dma_start(levels[:], ts)
         fb_codes = chain.tile([P, 2 * N], U8, name="fb_codes", offset=17664, align_bytes=64)
         nc.sync.dma_start(fb_codes[:].bitcast(I32), fb_words[0].bitcast(I32))
         fb_scale = chain.tile([P, N], U8, name="fb_scale", offset=17408, align_bytes=64)
-        nc.gpsimd.memset(fb_scale[:].bitcast(I32), 0)
+        nc.vector.memset(fb_scale[:].bitcast(I32), 0)
         for q in range(4):
             nc.sync.dma_start(
                 fb_scale[32 * q : 32 * q + 4, :].bitcast(I32), fb_scales[0, 4 * q : 4 * q + 4, :].bitcast(I32)
@@ -348,7 +349,7 @@ def tile_list_meltab_gain_kernel(
 
         deal_words(1)
         for part in range(2):
-            tile = keep.tile([P, PASSES, F], U8, name="dealt_scales%d" % part, align_bytes=64)
+            tile = behind.tile([P, PASSES, F], U8, name="dealt_scales%d" % part, align_bytes=64, offset=2048 + 1024 * part)
             nc.vector.tensor_copy(
                 tile[:].rearrange("p a (t m) -> p a t m", t=PACK),
                 w_scales[part].rearrange("p a (m t) -> p a t m", t=PACK),

@@ -20,19 +20,26 @@ ACT = mybir.ActivationFunctionType
 P = 128
 PACK = 4
 PASSES = K // (P * PACK)
+QUADS = 4
 GROUP = 16
 CHUNK = 512
 UNIT = 256
-WORD_CHUNKS = [(0, 512), (512, 512), (1024, 512), (1536, 512)]
-WARM_UPS = 6
 LIVE = 96
 BANKS = 8
 BANK = 512
-BLOCKS = [("frame", 0, 512), ("frequency", 512, 512), ("frequency", 1024, 512), ("frequency", 1536, 256), ("frequency", 1792, 256)]
-TURNED = [0, 2, 3, 4]
-ORDER = [("transform", 0), ("transform", 1), ("transform", 2), ("add", 0), ("quantize", 1), ("quantize", 2), ("quantize", 0), ("levels", 2), ("filter", 2), ("filter", 3), ("transform", 3), ("levels", 4), ("filter", 5), ("filter", 4), ("quantize", 3), ("transform", 4), ("turn", 2), ("turn", 3), ("levels", 0), ("filter", 1), ("filter", 0), ("turn", 4), ("quantize", 4), ("filter", 6), ("turn", 0), ("filter", 7)]
 SIGN_COLS = 128
 TINY = 2.0**-110
+WARM_UPS = 6
+
+PICKED_SCALES_AT = 0
+SCALE_TABLE_AT = J
+LEVELS_AT = SCALE_TABLE_AT + T - 64
+WORDS = 4 * CHUNK
+FIRST_AT = 2 * WORDS - 64
+PICKED_WORDS_AT = (FIRST_AT, FIRST_AT + 64 - WORDS, FIRST_AT + WORDS - 64, 64)
+FB_SCALE_AT = 64 + WORDS
+FB_CODES_AT = FB_SCALE_AT + N
+SI_DEALT_AT = FIRST_AT - PASSES * F
 
 
 def tile_list_meltab_gain_kernel(
@@ -59,8 +66,9 @@ def tile_list_meltab_gain_kernel(
         def listed(j0, width):
             return offsets[:, j0 // GROUP : (j0 + width) // GROUP]
 
-        scale_table = behind.tile([P, T // 4], I32, name="scale_table", align_bytes=64, offset=2048)
+        scale_table = behind.tile([P, T // 4], I32, name="scale_table", align_bytes=64, offset=SCALE_TABLE_AT)
         nc.scalar.dma_start(scale_table[LIVE:P, :], tab_scales.rearrange("a q t -> (a q) t").bitcast(I32))
+
         gain = keep.tile([P, PACK], F32, name="gain")
         nc.sync.dma_start(gain[:], gn.rearrange("(p t) -> p t", t=PACK))
         quarter = keep.tile([P, PACK], F32, name="quarter")
@@ -74,31 +82,25 @@ def tile_list_meltab_gain_kernel(
         inverse = keep.tile([P, PACK], F32, name="inverse")
         nc.vector.reciprocal(inverse[:], half_guess[:])
 
-
         w_words = []
         for part, words in enumerate((co_words, si_words)):
             tile = keep.tile([P, PASSES, 2 * F], U8, name="w_words%d" % part, align_bytes=64)
             nc.sync.dma_start(tile[:].bitcast(I32), words.rearrange("a p b -> p a b").bitcast(I32))
             w_words.append(tile)
 
-        w_scales = []
-
         word_table = keep.tile([P, T], I32, name="word_table", align_bytes=64)
         nc.sync.dma_start(word_table[:], tab_words[0].rearrange("p t b -> p (t b)").bitcast(I32))
 
-        def load_planes(clearer, planes, scales, queues):
-            clearer.memset(planes[:].bitcast(I32), 0)
-            for q in range(4):
-                queues[q].dma_start(
+        w_scales = []
+        for name, scales in (("co_planes", co_scales), ("si_planes", si_scales)):
+            planes = keep.tile([P, PASSES * F], U8, name=name, align_bytes=64)
+            nc.vector.memset(planes[:].bitcast(I32), 0)
+            for q in range(QUADS):
+                nc.scalar.dma_start(
                     planes[32 * q : 32 * q + 4, :].bitcast(I32).rearrange("r (a f) -> r a f", a=PASSES),
                     scales[:, 4 * q : 4 * q + 4, :].rearrange("a r f -> r a f").bitcast(I32),
                 )
             w_scales.append(planes[:].rearrange("p (a f) -> p a f", a=PASSES))
-
-        co_planes = keep.tile([P, PASSES * F], U8, name="co_planes", align_bytes=64)
-        load_planes(nc.vector, co_planes, co_scales, [nc.scalar] * 4)
-        si_planes = keep.tile([P, PASSES * F], U8, name="si_planes", align_bytes=64)
-        load_planes(nc.vector, si_planes, si_scales, [nc.scalar] * 4)
         nc.vector.memset(scale_table[0:LIVE, :], 0)
 
         frame_scales = []
@@ -109,39 +111,43 @@ def tile_list_meltab_gain_kernel(
         identity = keep.tile([P, P], F32, name="identity")
         make_identity(nc, identity[:])
 
-        picked_scales = behind.tile([P, J], U8, name="picked_scales", align_bytes=64, offset=0)
+        picked_scales = behind.tile([P, J], U8, name="picked_scales", align_bytes=64, offset=PICKED_SCALES_AT)
         nc.vector.tensor_copy(picked_scales[:], scale_table[:].bitcast(U8).indirect(offsets[:]))
         for a in reversed(range(PASSES)):
-            for q in range(4):
+            for q in range(QUADS):
                 first = LIVE + 16 * a + 4 * q
                 nc.sync.dma_start(
                     frame_scales[a][32 * q : 32 * q + 4, :], picked_scales[first : first + 4, :].bitcast(I32)
                 )
-        root = behind.tile([P, PACK], F32, name="root", offset=0)
+
+        root = behind.tile([P, PACK], F32, name="root", offset=PICKED_SCALES_AT)
         for t in range(PACK):
             column = slice(t, t + 1)
             nc.scalar.activation(
                 root[:, column], inverse[:, column], ACT.Identity, bias=half_guess[:, column], scale=quarter[:, column]
             )
-        levels = behind.tile([P, T], F32, name="levels", offset=2048 + T - 64)
+        levels = behind.tile([P, T], F32, name="levels", offset=LEVELS_AT)
         nc.sync.dma_start(levels[:], ts)
 
         frames = {}
 
-        def gather_words(j0, width):
-            if j0 == 0:
-                picked = chain.tile([P, width], U32, name="first_words", align_bytes=64, offset=16320)
-            else:
-                picked = chain.tile([P, width], U32, name="picked_words", align_bytes=64, offset=18176)
-            nc.vector.tensor_copy(picked[:], word_table[:].bitcast(U32).indirect(listed(j0, width)))
-            step = UNIT if j0 == 0 else width
-            for c0 in range(0, width, step):
-                parted = keep.tile([P, PASSES, 2 * step], U8, name="frames%d" % (j0 + c0), align_bytes=64)
-                nc.vector.tensor_copy(
-                    parted[:].bitcast(U16),
-                    picked[:, c0 : c0 + step].bitcast(U16).rearrange("p (n a) -> p a n", a=PASSES),
-                )
-                frames[j0 + c0] = parted
+        picked_words = {}
+
+        def gather_words(j0):
+            picked = chain.tile(
+                [P, CHUNK], U32, name="picked_words%d" % j0, align_bytes=64, offset=PICKED_WORDS_AT[j0 // CHUNK]
+            )
+            nc.vector.tensor_copy(picked[:], word_table[:].bitcast(U32).indirect(listed(j0, CHUNK)))
+            picked_words[j0] = picked
+
+        def part_words(j0, width):
+            c0 = j0 % CHUNK
+            parted = keep.tile([P, PASSES, 2 * width], U8, name="frames%d" % j0, align_bytes=64)
+            nc.vector.tensor_copy(
+                parted[:].bitcast(U16),
+                picked_words[j0 - c0][:, c0 : c0 + width].bitcast(U16).rearrange("p (n a) -> p a n", a=PASSES),
+            )
+            frames[j0] = parted
 
         def frame_operand(j0, width, a):
             first = max(j for j in frames if j <= j0)
@@ -151,18 +157,18 @@ def tile_list_meltab_gain_kernel(
         picked_levels = {}
         level_columns = {}
 
-        def gather_levels(j0):
-            picked = keep.tile([P, 2 * CHUNK], F32, name="picked_levels%d" % j0)
-            nc.vector.tensor_copy(picked[:], levels[:].indirect(listed(j0, 2 * CHUNK)))
-            for u0 in range(0, 2 * CHUNK, UNIT):
+        def gather_levels(j0, width):
+            picked = keep.tile([P, width], F32, name="picked_levels%d" % j0)
+            nc.vector.tensor_copy(picked[:], levels[:].indirect(listed(j0, width)))
+            for u0 in range(0, width, UNIT):
                 picked_levels[j0 + u0] = picked[:, u0 : u0 + UNIT]
 
-        def turn_levels(units):
-            tiles = [j0 + c0 for j0 in units for c0 in range(0, UNIT, P)]
-            for j in tiles:
+        def turn_levels(unit):
+            for c0 in range(0, UNIT, P):
+                j = UNIT * unit + c0
                 column = keep.tile([P, 1], F32, name="level_column%d" % j)
                 with nc.allow_non_contiguous_dma(reason="a row of levels becomes a column"):
-                    nc.sync.dma_start(column[:], picked_levels[j - j % UNIT][0:1, j % UNIT : j % UNIT + P])
+                    nc.sync.dma_start(column[:], picked_levels[UNIT * unit][0:1, c0 : c0 + P])
                 level_columns[j] = column[:]
 
         squares = {}
@@ -224,22 +230,37 @@ def tile_list_meltab_gain_kernel(
                             is_transpose=True, start=(part == 0), stop=(part == 1),
                         )
                 nc.scalar.activation(rows[:, t, :], bank[:, 0, 0:width], ACT.Copy, scale=gain[:, t : t + 1])
-            squares[j0] = rows
+            return rows
 
         quantized = {}
 
-        def quantize_power(road, j0, width):
+        def quantize(fill, j0, width):
             piece = width // 2
             power = work.tile([P, width * PACK], BF16, name="power", align_bytes=64)
             codes = keep.tile([P, width], U32, name="codes%d" % j0, align_bytes=64)
             scales = keep.tile([P, width], U8, name="scales%d" % j0, align_bytes=64)
-            if road == "frame":
+            fill(power, piece)
+            for n0 in (0, piece):
+                nc.vector.quantize_mx(
+                    out=codes[:, n0 : n0 + piece].bitcast(FP8X4),
+                    scales=scales[:, n0 : n0 + piece],
+                    in_=power[:, PACK * n0 : PACK * (n0 + piece)],
+                )
+            for u0 in range(0, width, UNIT):
+                quantized[(j0 + u0) // UNIT] = codes[:, u0 : u0 + UNIT], scales[:, u0 : u0 + UNIT]
+
+        def quantize_by_frame(rows, j0, width):
+            def interleave(power, piece):
                 for n0 in (0, piece):
                     nc.vector.tensor_copy(
                         power[:, PACK * n0 : PACK * (n0 + piece)].rearrange("p (c i t) -> p c t i", i=4, t=PACK),
-                        squares[j0][:, :, n0 : n0 + piece].rearrange("p t (c i) -> p c t i", i=4),
+                        rows[:, :, n0 : n0 + piece].rearrange("p t (c i) -> p c t i", i=4),
                     )
-            else:
+
+            quantize(interleave, j0, width)
+
+        def quantize_by_frequency(j0, width):
+            def add_and_sign(power, piece):
                 unsigned = work.tile([P, width * PACK], BF16, name="unsigned", align_bytes=64)
                 for n0 in (0, piece):
                     nc.vector.tensor_tensor(
@@ -258,19 +279,15 @@ def tile_list_meltab_gain_kernel(
                         ),
                         ALU.mult,
                     )
-            for n0 in (0, piece):
-                nc.vector.quantize_mx(
-                    out=codes[:, n0 : n0 + piece].bitcast(FP8X4),
-                    scales=scales[:, n0 : n0 + piece],
-                    in_=power[:, PACK * n0 : PACK * (n0 + piece)],
-                )
-            for u0 in range(0, width, UNIT):
-                quantized[j0 + u0] = codes[:, u0 : u0 + UNIT], scales[:, u0 : u0 + UNIT]
+
+            quantize(add_and_sign, j0, width)
 
         def store(j0, width, result):
             nc.sync.dma_start(out[:, j0 : j0 + width].rearrange("(h p) j -> p h j", p=P), result)
 
-        def filter_direct(j0, codes, scales):
+        def filter_direct(unit):
+            j0 = UNIT * unit
+            codes, scales = quantized[unit]
             width = P if j0 + UNIT == J else UNIT
             for c0 in range(0, UNIT, width):
                 result = work.tile([P, N // P, width], F32, name="result", bufs=4)
@@ -295,7 +312,8 @@ def tile_list_meltab_gain_kernel(
 
         scaled = {}
 
-        def filter_turned(j0, codes, scales):
+        def filter_turned(unit):
+            codes, scales = quantized[unit]
             by_frame = work.tile([P, UNIT // P, N], F32, name="by_frame", bufs=4)
             bank = next_bank(UNIT // P)
             for i in range(UNIT // P):
@@ -310,11 +328,13 @@ def tile_list_meltab_gain_kernel(
                     stop=True,
                 )
             for i in range(UNIT // P):
-                nc.scalar.activation(by_frame[:, i, :], bank[:, i, :], ACT.Copy, scale=level_columns[j0 + P * i])
-            scaled[j0] = by_frame
+                nc.scalar.activation(
+                    by_frame[:, i, :], bank[:, i, :], ACT.Copy, scale=level_columns[UNIT * unit + P * i]
+                )
+            scaled[unit] = by_frame
 
-        def turn_back(j0):
-            by_frame = scaled[j0]
+        def turn_back(unit):
+            by_frame = scaled[unit]
             turned = next_bank(N // P)
             for i in range(UNIT // P):
                 for half in range(N // P):
@@ -323,7 +343,7 @@ def tile_list_meltab_gain_kernel(
                     )
             result = work.tile([P, N // P, UNIT], F32, name="turned_result", bufs=4)
             nc.scalar.copy(result[:], turned[:])
-            store(j0, UNIT, result[:])
+            store(UNIT * unit, UNIT, result[:])
 
         dealt_words, dealt_scales = [], []
 
@@ -335,30 +355,38 @@ def tile_list_meltab_gain_kernel(
             )
             dealt_words.append(tile)
 
-        deal_words(0)
-        gather_words(*WORD_CHUNKS[0])
-        fb_codes = chain.tile([P, 2 * N], U8, name="fb_codes", offset=17664, align_bytes=64)
-        nc.sync.dma_start(fb_codes[:].bitcast(I32), fb_words[0].bitcast(I32))
-        fb_scale = chain.tile([P, N], U8, name="fb_scale", offset=17408, align_bytes=64)
-        nc.vector.memset(fb_scale[:].bitcast(I32), 0)
-        for q in range(4):
-            nc.sync.dma_start(
-                fb_scale[32 * q : 32 * q + 4, :].bitcast(I32), fb_scales[0, 4 * q : 4 * q + 4, :].bitcast(I32)
-            )
-        gather_words(*WORD_CHUNKS[1])
-
-        deal_words(1)
-        for part in range(2):
-            tile = behind.tile([P, PASSES, F], U8, name="dealt_scales%d" % part, align_bytes=64, offset=2048 + 1024 * part)
+        def deal_scales(part, pool, offset):
+            tile = pool.tile([P, PASSES, F], U8, name="dealt_scales%d" % part, align_bytes=64, offset=offset)
             nc.vector.tensor_copy(
                 tile[:].rearrange("p a (t m) -> p a t m", t=PACK),
                 w_scales[part].rearrange("p a (m t) -> p a t m", t=PACK),
             )
             dealt_scales.append(tile)
-        for j0, width in WORD_CHUNKS[2:]:
-            gather_words(j0, width)
-        for j0 in range(0, J, 2 * CHUNK):
-            gather_levels(j0)
+
+        deal_words(0)
+        gather_words(0)
+        part_words(0, UNIT)
+        gather_words(CHUNK)
+        part_words(UNIT, UNIT)
+        part_words(CHUNK, CHUNK)
+        deal_words(1)
+        deal_scales(0, behind, SCALE_TABLE_AT)
+        deal_scales(1, chain, SI_DEALT_AT)
+        gather_words(2 * CHUNK)
+        gather_words(3 * CHUNK)
+        part_words(2 * CHUNK, CHUNK)
+        part_words(3 * CHUNK, CHUNK)
+        fb_codes = chain.tile([P, 2 * N], U8, name="fb_codes", offset=FB_CODES_AT, align_bytes=64)
+        nc.sync.dma_start(fb_codes[:].bitcast(I32), fb_words[0].bitcast(I32))
+        fb_scale = chain.tile([P, N], U8, name="fb_scale", offset=FB_SCALE_AT, align_bytes=64)
+        nc.vector.memset(fb_scale[:].bitcast(I32), 0)
+        for q in range(QUADS):
+            nc.sync.dma_start(
+                fb_scale[32 * q : 32 * q + 4, :].bitcast(I32), fb_scales[0, 4 * q : 4 * q + 4, :].bitcast(I32)
+            )
+        for j0 in range(0, J, J // 2):
+            gather_levels(j0, J // 2)
+
         idle = next_bank(1)
         for i in range(WARM_UPS):
             nc.tensor.matmul_mx(
@@ -370,18 +398,30 @@ def tile_list_meltab_gain_kernel(
                 start=True,
                 stop=True,
             )
-        for step, b in ORDER:
-            if step == "filter":
-                (filter_turned if b in TURNED else filter_direct)(UNIT * b, *quantized[UNIT * b])
-            elif step == "turn":
-                turn_back(UNIT * b)
-            elif step == "levels":
-                turn_levels([UNIT * u for u in (b, b + 1) if u in TURNED])
-            else:
-                road, j0, width = BLOCKS[b]
-                if step == "transform":
-                    (transform_by_frame if road == "frame" else transform_by_frequency)(j0, width)
-                elif step == "add":
-                    add_by_frame(j0, width)
-                else:
-                    quantize_power(road, j0, width)
+
+        transform_by_frame(0, CHUNK)
+        for j0 in (CHUNK, 2 * CHUNK):
+            transform_by_frequency(j0, CHUNK)
+        first_rows = add_by_frame(0, CHUNK)
+        for j0 in (CHUNK, 2 * CHUNK):
+            quantize_by_frequency(j0, CHUNK)
+        quantize_by_frame(first_rows, 0, CHUNK)
+
+        for unit in (2, 3, 4, 5, 0):
+            turn_levels(unit)
+        transform_by_frequency(6 * UNIT, UNIT)
+        filter_turned(2)
+        filter_turned(3)
+        turn_back(2)
+        quantize_by_frequency(6 * UNIT, UNIT)
+        transform_by_frequency(7 * UNIT, UNIT)
+        for unit in (4, 5):
+            filter_turned(unit)
+            turn_back(unit - 1)
+        filter_direct(1)
+        filter_turned(0)
+        turn_back(5)
+        quantize_by_frequency(7 * UNIT, UNIT)
+        filter_direct(6)
+        turn_back(0)
+        filter_direct(7)

@@ -83,20 +83,20 @@ def tile_list_meltab_gain_kernel(
         nc.vector.reciprocal(inverse[:], half_guess[:])
 
         w_words = []
-        for part, words in enumerate((co_words, si_words)):
+        for part, (words, queue) in enumerate(((co_words, nc.sync), (si_words, nc.scalar))):
             tile = keep.tile([P, PASSES, 2 * F], U8, name="w_words%d" % part, align_bytes=64)
-            nc.sync.dma_start(tile[:].bitcast(I32), words.rearrange("a p b -> p a b").bitcast(I32))
+            queue.dma_start(tile[:].bitcast(I32), words.rearrange("a p b -> p a b").bitcast(I32))
             w_words.append(tile)
 
         word_table = keep.tile([P, T], I32, name="word_table", align_bytes=64)
         nc.sync.dma_start(word_table[:], tab_words[0].rearrange("p t b -> p (t b)").bitcast(I32))
 
         w_scales = []
-        for name, scales in (("co_planes", co_scales), ("si_planes", si_scales)):
+        for name, scales, queue in (("co_planes", co_scales, nc.scalar), ("si_planes", si_scales, nc.sync)):
             planes = keep.tile([P, PASSES * F], U8, name=name, align_bytes=64)
             nc.vector.memset(planes[:].bitcast(I32), 0)
             for q in range(QUADS):
-                nc.scalar.dma_start(
+                queue.dma_start(
                     planes[32 * q : 32 * q + 4, :].bitcast(I32).rearrange("r (a f) -> r a f", a=PASSES),
                     scales[:, 4 * q : 4 * q + 4, :].rearrange("a r f -> r a f").bitcast(I32),
                 )

@@ -83,10 +83,13 @@ def tile_list_meltab_gain_kernel(
         nc.vector.reciprocal(inverse[:], half_guess[:])
 
         w_words = []
-        for part, (words, queue) in enumerate(((co_words, nc.sync), (si_words, nc.scalar))):
-            tile = keep.tile([P, PASSES, 2 * F], U8, name="w_words%d" % part, align_bytes=64)
+
+        def load_words(name, words, queue):
+            tile = keep.tile([P, PASSES, 2 * F], U8, name=name, align_bytes=64)
             queue.dma_start(tile[:].bitcast(I32), words.rearrange("a p b -> p a b").bitcast(I32))
             w_words.append(tile)
+
+        load_words("co_w", co_words, nc.sync)
 
         word_table = keep.tile([P, T], I32, name="word_table", align_bytes=64)
         nc.sync.dma_start(word_table[:], tab_words[0].rearrange("p t b -> p (t b)").bitcast(I32))
@@ -101,6 +104,7 @@ def tile_list_meltab_gain_kernel(
                     scales[:, 4 * q : 4 * q + 4, :].rearrange("a r f -> r a f").bitcast(I32),
                 )
             w_scales.append(planes[:].rearrange("p (a f) -> p a f", a=PASSES))
+        load_words("si_w", si_words, nc.scalar)
         nc.vector.memset(scale_table[0:LIVE, :], 0)
 
         frame_scales = []
@@ -355,9 +359,8 @@ def tile_list_meltab_gain_kernel(
             )
             dealt_words.append(tile)
 
-        def deal_scales(part, pool, offset):
-            tile = pool.tile([P, PASSES, F], U8, name="dealt_scales%d" % part, align_bytes=64, offset=offset)
-            nc.vector.tensor_copy(
+        def deal_scales(tile, part, engine):
+            engine.tensor_copy(
                 tile[:].rearrange("p a (t m) -> p a t m", t=PACK),
                 w_scales[part].rearrange("p a (m t) -> p a t m", t=PACK),
             )
@@ -370,8 +373,10 @@ def tile_list_meltab_gain_kernel(
         part_words(UNIT, UNIT)
         part_words(CHUNK, CHUNK)
         deal_words(1)
-        deal_scales(0, behind, SCALE_TABLE_AT)
-        deal_scales(1, chain, SI_DEALT_AT)
+        co_dealt = keep.tile([P, PASSES, F], U8, name="co_dealt", align_bytes=64)
+        deal_scales(co_dealt, 0, nc.gpsimd)
+        si_dealt = chain.tile([P, PASSES, F], U8, name="si_dealt", align_bytes=64, offset=SI_DEALT_AT)
+        deal_scales(si_dealt, 1, nc.vector)
         gather_words(2 * CHUNK)
         gather_words(3 * CHUNK)
         part_words(2 * CHUNK, CHUNK)

@@ -28,7 +28,7 @@ LIVE = 96
 BANKS = 8
 BANK = 512
 SIGN_COLS = 128
-TINY = 2.0**-110
+TINY = 2.0**-112
 WARM_UPS = 6
 
 PICKED_SCALES_AT = 0
@@ -37,6 +37,7 @@ LEVELS_AT = SCALE_TABLE_AT + T - 64
 WORDS = 4 * CHUNK
 FIRST_AT = 2 * WORDS - 64
 PICKED_WORDS_AT = (FIRST_AT, FIRST_AT + 64 - WORDS, FIRST_AT + WORDS - 64, 64)
+INVERSE_AT = FIRST_AT + 64
 FB_SCALE_AT = 64 + WORDS
 FB_CODES_AT = FB_SCALE_AT + N
 SI_DEALT_AT = FIRST_AT - PASSES * F
@@ -69,44 +70,48 @@ def tile_list_meltab_gain_kernel(
         scale_table = behind.tile([P, T // 4], I32, name="scale_table", align_bytes=64, offset=SCALE_TABLE_AT)
         nc.scalar.dma_start(scale_table[LIVE:P, :], tab_scales.rearrange("a q t -> (a q) t").bitcast(I32))
 
-        gain = keep.tile([P, PACK], F32, name="gain")
-        nc.sync.dma_start(gain[:], gn.rearrange("(p t) -> p t", t=PACK))
-        quarter = keep.tile([P, PACK], F32, name="quarter")
-        nc.scalar.activation(quarter[:], gain[:], ACT.Abs, scale=0.25)
-        floor = keep.tile([P, 1], F32, name="floor")
-        nc.vector.memset(floor[:], TINY)
-        half_guess = keep.tile([P, PACK], F32, name="half_guess")
-        nc.scalar.activation(half_guess[:], quarter[:], ACT.Sqrt, bias=floor[:])
-        signs = keep.tile([P, SIGN_COLS // PACK, PACK], BF16, name="signs")
-        nc.scalar.activation(signs[:], gain[:].unsqueeze(1).to_broadcast([P, SIGN_COLS // PACK, PACK]), ACT.Sign)
-        inverse = keep.tile([P, PACK], F32, name="inverse")
-        nc.vector.reciprocal(inverse[:], half_guess[:])
+        w_words, w_scales = [], []
 
-        w_words = []
-
-        def load_words(name, words, queue):
-            tile = keep.tile([P, PASSES, 2 * F], U8, name=name, align_bytes=64)
-            queue.dma_start(tile[:].bitcast(I32), words.rearrange("a p b -> p a b").bitcast(I32))
+        def load_words(tile, words):
+            nc.sync.dma_start(tile[:].bitcast(I32), words.rearrange("a p b -> p a b").bitcast(I32))
             w_words.append(tile)
 
-        load_words("co_w", co_words, nc.sync)
-
-        word_table = keep.tile([P, T], I32, name="word_table", align_bytes=64)
-        nc.sync.dma_start(word_table[:], tab_words[0].rearrange("p t b -> p (t b)").bitcast(I32))
-
-        w_scales = []
-        for name, scales, queue in (("co_planes", co_scales, nc.scalar), ("si_planes", si_scales, nc.sync)):
-            planes = keep.tile([P, PASSES * F], U8, name=name, align_bytes=64)
-            nc.vector.memset(planes[:].bitcast(I32), 0)
+        def load_planes(planes, scales, clearing, queues):
+            clearing.memset(planes[:].bitcast(I32), 0)
             for q in range(QUADS):
-                queue.dma_start(
+                queues[q].dma_start(
                     planes[32 * q : 32 * q + 4, :].bitcast(I32).rearrange("r (a f) -> r a f", a=PASSES),
                     scales[:, 4 * q : 4 * q + 4, :].rearrange("a r f -> r a f").bitcast(I32),
                 )
             w_scales.append(planes[:].rearrange("p (a f) -> p a f", a=PASSES))
-        load_words("si_w", si_words, nc.scalar)
-        nc.vector.memset(scale_table[0:LIVE, :], 0)
 
+        co_tile = keep.tile([P, PASSES, 2 * F], U8, name="co_tile", align_bytes=64)
+        load_words(co_tile, co_words)
+        co_planes = keep.tile([P, PASSES * F], U8, name="co_planes", align_bytes=64)
+        load_planes(co_planes, co_scales, nc.gpsimd, (nc.scalar, nc.sync, nc.scalar, nc.sync))
+        word_table = keep.tile([P, T], I32, name="word_table", align_bytes=64)
+        nc.sync.dma_start(word_table[:], tab_words[0].rearrange("p t b -> p (t b)").bitcast(I32))
+
+        si_tile = keep.tile([P, PASSES, 2 * F], U8, name="si_tile", align_bytes=64)
+        load_words(si_tile, si_words)
+        si_planes = keep.tile([P, PASSES * F], U8, name="si_planes", align_bytes=64)
+        load_planes(si_planes, si_scales, nc.vector, (nc.sync,) * QUADS)
+        gain = keep.tile([P, PACK], F32, name="gain")
+        nc.scalar.dma_start(gain[:], gn.rearrange("(p t) -> p t", t=PACK))
+        tiny = keep.tile([P, 1], F32, name="tiny")
+        nc.vector.memset(tiny[:], TINY)
+        tiny_root = keep.tile([P, 1], F32, name="tiny_root")
+        nc.scalar.activation(tiny_root[:], tiny[:], ACT.Sqrt)
+        floor = keep.tile([P, 1], F32, name="floor")
+        nc.scalar.activation(floor[:], tiny_root[:], ACT.Square)
+        quarter = keep.tile([P, PACK], F32, name="quarter")
+        nc.scalar.activation(quarter[:], gain[:], ACT.Abs, scale=0.25)
+        half_guess = keep.tile([P, PACK], F32, name="half_guess")
+        nc.scalar.activation(half_guess[:], quarter[:], ACT.Sqrt, bias=floor[:])
+        signs = keep.tile([P, SIGN_COLS // PACK, PACK], BF16, name="signs")
+        nc.scalar.activation(signs[:], gain[:].unsqueeze(1).to_broadcast([P, SIGN_COLS // PACK, PACK]), ACT.Sign)
+
+        nc.vector.memset(scale_table[0:LIVE, :], 0)
         frame_scales = []
         for a in range(PASSES):
             plane = keep.tile([P, J // 4], I32, name="frame_scales%d" % a, align_bytes=64)
@@ -114,6 +119,25 @@ def tile_list_meltab_gain_kernel(
             frame_scales.append(plane)
         identity = keep.tile([P, P], F32, name="identity")
         make_identity(nc, identity[:])
+
+        dealt_words, dealt_scales = [], []
+
+        def deal_words(part):
+            tile = keep.tile([P, PASSES, 2 * F], U8, name="dealt_words%d" % part, align_bytes=64)
+            nc.scalar.copy(
+                tile[:].bitcast(U16).rearrange("p a (t m) -> p a t m", t=PACK),
+                w_words[part][:].bitcast(U16).rearrange("p a (m t) -> p a t m", t=PACK),
+            )
+            dealt_words.append(tile)
+
+        def deal_scales(tile, part, engine):
+            engine.tensor_copy(
+                tile[:].rearrange("p a (t m) -> p a t m", t=PACK),
+                w_scales[part].rearrange("p a (m t) -> p a t m", t=PACK),
+            )
+            dealt_scales.append(tile)
+
+        deal_words(0)
 
         picked_scales = behind.tile([P, J], U8, name="picked_scales", align_bytes=64, offset=PICKED_SCALES_AT)
         nc.vector.tensor_copy(picked_scales[:], scale_table[:].bitcast(U8).indirect(offsets[:]))
@@ -124,12 +148,6 @@ def tile_list_meltab_gain_kernel(
                     frame_scales[a][32 * q : 32 * q + 4, :], picked_scales[first : first + 4, :].bitcast(I32)
                 )
 
-        root = behind.tile([P, PACK], F32, name="root", offset=PICKED_SCALES_AT)
-        for t in range(PACK):
-            column = slice(t, t + 1)
-            nc.scalar.activation(
-                root[:, column], inverse[:, column], ACT.Identity, bias=half_guess[:, column], scale=quarter[:, column]
-            )
         levels = behind.tile([P, T], F32, name="levels", offset=LEVELS_AT)
         nc.sync.dma_start(levels[:], ts)
 
@@ -349,31 +367,21 @@ def tile_list_meltab_gain_kernel(
             nc.scalar.copy(result[:], turned[:])
             store(UNIT * unit, UNIT, result[:])
 
-        dealt_words, dealt_scales = [], []
-
-        def deal_words(part):
-            tile = keep.tile([P, PASSES, 2 * F], U8, name="dealt_words%d" % part, align_bytes=64)
-            nc.scalar.copy(
-                tile[:].bitcast(U16).rearrange("p a (t m) -> p a t m", t=PACK),
-                w_words[part][:].bitcast(U16).rearrange("p a (m t) -> p a t m", t=PACK),
-            )
-            dealt_words.append(tile)
-
-        def deal_scales(tile, part, engine):
-            engine.tensor_copy(
-                tile[:].rearrange("p a (t m) -> p a t m", t=PACK),
-                w_scales[part].rearrange("p a (m t) -> p a t m", t=PACK),
-            )
-            dealt_scales.append(tile)
-
-        deal_words(0)
+        deal_words(1)
         gather_words(0)
         part_words(0, UNIT)
         gather_words(CHUNK)
+        inverse = chain.tile([P, PACK], F32, name="inverse", offset=INVERSE_AT)
+        nc.vector.reciprocal(inverse[:], half_guess[:])
+        root = keep.tile([P, PACK], F32, name="root")
+        for t in range(PACK):
+            column = slice(t, t + 1)
+            nc.scalar.activation(
+                root[:, column], inverse[:, column], ACT.Identity, bias=half_guess[:, column], scale=quarter[:, column]
+            )
         part_words(UNIT, UNIT)
         part_words(CHUNK, CHUNK)
-        deal_words(1)
-        co_dealt = keep.tile([P, PASSES, F], U8, name="co_dealt", align_bytes=64)
+        co_dealt = behind.tile([P, PASSES, F], U8, name="co_dealt", align_bytes=64, offset=SCALE_TABLE_AT)
         deal_scales(co_dealt, 0, nc.gpsimd)
         si_dealt = chain.tile([P, PASSES, F], U8, name="si_dealt", align_bytes=64, offset=SI_DEALT_AT)
         deal_scales(si_dealt, 1, nc.vector)
@@ -398,8 +406,8 @@ def tile_list_meltab_gain_kernel(
                 out=idle[:, 0, :],
                 lhsT=dealt_words[0][:, 0, 0 : 2 * P].bitcast(FP4X4),
                 lhsT_scale=w_scales[0][:, 0, 0:P],
-                rhs=w_words[0][:, 0, :].bitcast(FP4X4),
-                rhs_scale=w_scales[0][:, 0, :],
+                rhs=w_words[2 * i // WARM_UPS][:, 0, :].bitcast(FP4X4),
+                rhs_scale=w_scales[2 * i // WARM_UPS][:, 0, :],
                 start=True,
                 stop=True,
             )

@@ -41,6 +41,8 @@ INVERSE_AT = FIRST_AT + 64
 FB_SCALE_AT = 64 + WORDS
 FB_CODES_AT = FB_SCALE_AT + N
 SI_DEALT_AT = FIRST_AT - PASSES * F
+LATE_LEVELS_AT = 0
+POWER_AT = {5 * UNIT: 2 * J - 64, 0: 2 * J + 2 * PACK * UNIT - 128}
 
 
 def tile_list_meltab_gain_kernel(
@@ -51,6 +53,7 @@ def tile_list_meltab_gain_kernel(
         keep = ctx.enter_context(tc.tile_pool(name="keep", bufs=1))
         chain = ctx.enter_context(tc.tile_pool(name="chain", bufs=1))
         behind = ctx.enter_context(tc.tile_pool(name="behind", bufs=1))
+        late = ctx.enter_context(tc.tile_pool(name="late", bufs=1))
         work = ctx.enter_context(tc.tile_pool(name="work", bufs=2))
         psum = ctx.enter_context(tc.psum_pool(name="psum", bufs=1))
         taken = []
@@ -179,8 +182,7 @@ def tile_list_meltab_gain_kernel(
         picked_levels = {}
         level_columns = {}
 
-        def gather_levels(j0, width):
-            picked = keep.tile([P, width], F32, name="picked_levels%d" % j0)
+        def gather_levels(picked, j0, width):
             nc.vector.tensor_copy(picked[:], levels[:].indirect(listed(j0, width)))
             for u0 in range(0, width, UNIT):
                 picked_levels[j0 + u0] = picked[:, u0 : u0 + UNIT]
@@ -258,7 +260,10 @@ def tile_list_meltab_gain_kernel(
 
         def quantize(fill, j0, width):
             piece = width // 2
-            power = work.tile([P, width * PACK], BF16, name="power", align_bytes=64)
+            if j0 in POWER_AT:
+                power = late.tile([P, width * PACK], BF16, name="power%d" % j0, align_bytes=64, offset=POWER_AT[j0])
+            else:
+                power = work.tile([P, width * PACK], BF16, name="power", align_bytes=64)
             codes = keep.tile([P, width], U32, name="codes%d" % j0, align_bytes=64)
             scales = keep.tile([P, width], U8, name="scales%d" % j0, align_bytes=64)
             fill(power, piece)
@@ -274,9 +279,10 @@ def tile_list_meltab_gain_kernel(
         def quantize_by_frame(rows, j0, width):
             def interleave(power, piece):
                 for n0 in (0, piece):
-                    nc.vector.tensor_copy(
-                        power[:, PACK * n0 : PACK * (n0 + piece)].rearrange("p (c i t) -> p c t i", i=4, t=PACK),
-                        rows[:, :, n0 : n0 + piece].rearrange("p t (c i) -> p c t i", i=4),
+                    nc.gpsimd.tensor_scalar(
+                        power[:, PACK * n0 : PACK * (n0 + piece)].rearrange("p (c t) -> p c t", t=PACK),
+                        rows[:, :, n0 : n0 + piece].rearrange("p t c -> p c t"),
+                        1.0, 0.0, ALU.mult, ALU.add,
                     )
 
             quantize(interleave, j0, width)
@@ -397,8 +403,8 @@ def tile_list_meltab_gain_kernel(
             nc.sync.dma_start(
                 fb_scale[32 * q : 32 * q + 4, :].bitcast(I32), fb_scales[0, 4 * q : 4 * q + 4, :].bitcast(I32)
             )
-        for j0 in range(0, J, J // 2):
-            gather_levels(j0, J // 2)
+        early_levels = keep.tile([P, J // 2], F32, name="early_levels")
+        gather_levels(early_levels, 0, J // 2)
 
         idle = next_bank(1)
         for i in range(WARM_UPS):
@@ -413,28 +419,28 @@ def tile_list_meltab_gain_kernel(
             )
 
         transform_by_frame(0, CHUNK)
-        for j0 in (CHUNK, 2 * CHUNK):
-            transform_by_frequency(j0, CHUNK)
-        first_rows = add_by_frame(0, CHUNK)
-        for j0 in (CHUNK, 2 * CHUNK):
-            quantize_by_frequency(j0, CHUNK)
-        quantize_by_frame(first_rows, 0, CHUNK)
-
-        for unit in (2, 3, 4, 5, 0):
+        for unit in (2, 3, 0, 1):
             turn_levels(unit)
-        transform_by_frequency(6 * UNIT, UNIT)
+        for unit in (2, 3, 4, 5):
+            transform_by_frequency(unit * UNIT, UNIT)
+            quantize_by_frequency(unit * UNIT, UNIT)
+        rows = add_by_frame(0, CHUNK)
+        late_levels = late.tile([P, J // 2], F32, name="late_levels", align_bytes=64, offset=LATE_LEVELS_AT)
+        gather_levels(late_levels, J // 2, J // 2)
         filter_turned(2)
-        filter_turned(3)
+        filter_direct(4)
+        filter_direct(5)
+        quantize_by_frame(rows, 0, CHUNK)
+        transform_by_frequency(6 * UNIT, UNIT)
         turn_back(2)
-        quantize_by_frequency(6 * UNIT, UNIT)
         transform_by_frequency(7 * UNIT, UNIT)
-        for unit in (4, 5):
-            filter_turned(unit)
-            turn_back(unit - 1)
-        filter_direct(1)
+        quantize_by_frequency(6 * UNIT, UNIT)
+        filter_turned(3)
         filter_turned(0)
-        turn_back(5)
-        quantize_by_frequency(7 * UNIT, UNIT)
-        filter_direct(6)
+        turn_back(3)
+        filter_turned(1)
         turn_back(0)
+        filter_direct(6)
+        turn_back(1)
+        quantize_by_frequency(7 * UNIT, UNIT)
         filter_direct(7)

from contextlib import ExitStack

import concourse.mybir as mybir
from concourse.masks import make_identity

K, F, N, T, J = 1024, 512, 256, 4096, 2048
FLOPS = 2 * J * (2 * K * F + F * N)

F32 = mybir.dt.float32
BF16 = mybir.dt.bfloat16
I32 = mybir.dt.int32
U32 = mybir.dt.uint32
U16 = mybir.dt.uint16
U8 = mybir.dt.uint8
FP8X4 = mybir.dt.float8_e4m3fn_x4
FP4X4 = mybir.dt.float4_e2m1fn_x4
ALU = mybir.AluOpType
ACT = mybir.ActivationFunctionType

P = 128
PACK = 4
PASSES = K // (P * PACK)
QUADS = 4
GROUP = 16
CHUNK = 512
UNIT = 256
LIVE = 96
BANKS = 8
BANK = 512
SIGN_COLS = 128
TINY = 2.0**-112
WARM_UPS = 6

PICKED_SCALES_AT = 0
SCALE_TABLE_AT = J
LEVELS_AT = SCALE_TABLE_AT + T - 64
WORDS = 4 * CHUNK
FIRST_AT = 2 * WORDS - 64
PICKED_WORDS_AT = (FIRST_AT, FIRST_AT + 64 - WORDS, FIRST_AT + WORDS - 64, 64)
INVERSE_AT = FIRST_AT + 64
FB_SCALE_AT = 64 + WORDS
FB_CODES_AT = FB_SCALE_AT + N
SI_DEALT_AT = FIRST_AT - PASSES * F
LATE_LEVELS_AT = 0
POWER_AT = {5 * UNIT: 2 * J - 64, 0: 2 * J + 2 * PACK * UNIT - 128}


def tile_list_meltab_gain_kernel(
    tc, tab_words, tab_scales, co_words, co_scales, si_words, si_scales, gn, fb_words, fb_scales, ts, offs, out
):
    nc = tc.nc
    with ExitStack() as ctx:
        keep = ctx.enter_context(tc.tile_pool(name="keep", bufs=1))
        chain = ctx.enter_context(tc.tile_pool(name="chain", bufs=1))
        behind = ctx.enter_context(tc.tile_pool(name="behind", bufs=1))
        late = ctx.enter_context(tc.tile_pool(name="late", bufs=1))
        work = ctx.enter_context(tc.tile_pool(name="work", bufs=2))
        psum = ctx.enter_context(tc.psum_pool(name="psum", bufs=1))
        taken = []

        def next_bank(rows):
            taken.append(rows)
            return psum.tile(
                [P, rows, BANK // rows], F32, name="bank%d" % len(taken), offset=4 * BANK * (len(taken) % BANKS)
            )

        offsets = keep.tile([P, J // GROUP], U16, name="offsets")
        nc.sync.dma_start(offsets[:], offs)

        def listed(j0, width):
            return offsets[:, j0 // GROUP : (j0 + width) // GROUP]

        scale_table = behind.tile([P, T // 4], I32, name="scale_table", align_bytes=64, offset=SCALE_TABLE_AT)
        nc.scalar.dma_start(scale_table[LIVE:P, :], tab_scales.rearrange("a q t -> (a q) t").bitcast(I32))

        w_words, w_scales = [], []

        def load_words(tile, words):
            nc.sync.dma_start(tile[:].bitcast(I32), words.rearrange("a p b -> p a b").bitcast(I32))
            w_words.append(tile)

        def load_planes(planes, scales, clearing, queues):
            clearing.memset(planes[:].bitcast(I32), 0)
            for q in range(QUADS):
                queues[q].dma_start(
                    planes[32 * q : 32 * q + 4, :].bitcast(I32).rearrange("r (a f) -> r a f", a=PASSES),
                    scales[:, 4 * q : 4 * q + 4, :].rearrange("a r f -> r a f").bitcast(I32),
                )
            w_scales.append(planes[:].rearrange("p (a f) -> p a f", a=PASSES))

        co_tile = keep.tile([P, PASSES, 2 * F], U8, name="co_tile", align_bytes=64)
        load_words(co_tile, co_words)
        co_planes = keep.tile([P, PASSES * F], U8, name="co_planes", align_bytes=64)
        load_planes(co_planes, co_scales, nc.gpsimd, (nc.scalar, nc.sync, nc.scalar, nc.sync))
        word_table = keep.tile([P, T], I32, name="word_table", align_bytes=64)
        nc.sync.dma_start(word_table[:], tab_words[0].rearrange("p t b -> p (t b)").bitcast(I32))

        si_tile = keep.tile([P, PASSES, 2 * F], U8, name="si_tile", align_bytes=64)
        load_words(si_tile, si_words)
        si_planes = keep.tile([P, PASSES * F], U8, name="si_planes", align_bytes=64)
        load_planes(si_planes, si_scales, nc.vector, (nc.sync,) * QUADS)
        gain = keep.tile([P, PACK], F32, name="gain")
        nc.scalar.dma_start(gain[:], gn.rearrange("(p t) -> p t", t=PACK))
        tiny = keep.tile([P, 1], F32, name="tiny")
        nc.vector.memset(tiny[:], TINY)
        tiny_root = keep.tile([P, 1], F32, name="tiny_root")
        nc.scalar.activation(tiny_root[:], tiny[:], ACT.Sqrt)
        floor = keep.tile([P, 1], F32, name="floor")
        nc.scalar.activation(floor[:], tiny_root[:], ACT.Square)
        quarter = keep.tile([P, PACK], F32, name="quarter")
        nc.scalar.activation(quarter[:], gain[:], ACT.Abs, scale=0.25)
        half_guess = keep.tile([P, PACK], F32, name="half_guess")
        nc.scalar.activation(half_guess[:], quarter[:], ACT.Sqrt, bias=floor[:])
        signs = keep.tile([P, SIGN_COLS // PACK, PACK], BF16, name="signs")
        nc.scalar.activation(signs[:], gain[:].unsqueeze(1).to_broadcast([P, SIGN_COLS // PACK, PACK]), ACT.Sign)

        nc.vector.memset(scale_table[0:LIVE, :], 0)
        frame_scales = []
        for a in range(PASSES):
            plane = keep.tile([P, J // 4], I32, name="frame_scales%d" % a, align_bytes=64)
            nc.gpsimd.memset(plane[:], 0)
            frame_scales.append(plane)
        identity = keep.tile([P, P], F32, name="identity")
        make_identity(nc, identity[:])

        dealt_words, dealt_scales = [], []

        def deal_words(part):
            tile = keep.tile([P, PASSES, 2 * F], U8, name="dealt_words%d" % part, align_bytes=64)
            nc.scalar.copy(
                tile[:].bitcast(U16).rearrange("p a (t m) -> p a t m", t=PACK),
                w_words[part][:].bitcast(U16).rearrange("p a (m t) -> p a t m", t=PACK),
            )
            dealt_words.append(tile)

        def deal_scales(tile, part, engine):
            engine.tensor_copy(
                tile[:].rearrange("p a (t m) -> p a t m", t=PACK),
                w_scales[part].rearrange("p a (m t) -> p a t m", t=PACK),
            )
            dealt_scales.append(tile)

        deal_words(0)

        picked_scales = behind.tile([P, J], U8, name="picked_scales", align_bytes=64, offset=PICKED_SCALES_AT)
        nc.vector.tensor_copy(picked_scales[:], scale_table[:].bitcast(U8).indirect(offsets[:]))
        for a in reversed(range(PASSES)):
            for q in range(QUADS):
                first = LIVE + 16 * a + 4 * q
                nc.sync.dma_start(
                    frame_scales[a][32 * q : 32 * q + 4, :], picked_scales[first : first + 4, :].bitcast(I32)
                )

        levels = behind.tile([P, T], F32, name="levels", offset=LEVELS_AT)
        nc.sync.dma_start(levels[:], ts)

        frames = {}

        picked_words = {}

        def gather_words(j0):
            picked = chain.tile(
                [P, CHUNK], U32, name="picked_words%d" % j0, align_bytes=64, offset=PICKED_WORDS_AT[j0 // CHUNK]
            )
            nc.vector.tensor_copy(picked[:], word_table[:].bitcast(U32).indirect(listed(j0, CHUNK)))
            picked_words[j0] = picked

        def part_words(j0, width):
            c0 = j0 % CHUNK
            parted = keep.tile([P, PASSES, 2 * width], U8, name="frames%d" % j0, align_bytes=64)
            nc.vector.tensor_copy(
                parted[:].bitcast(U16),
                picked_words[j0 - c0][:, c0 : c0 + width].bitcast(U16).rearrange("p (n a) -> p a n", a=PASSES),
            )
            frames[j0] = parted

        def frame_operand(j0, width, a):
            first = max(j for j in frames if j <= j0)
            words = frames[first][:, a, 2 * (j0 - first) : 2 * (j0 - first + width)].bitcast(FP4X4)
            return words, frame_scales[a][:].bitcast(U8)[:, j0 : j0 + width]

        picked_levels = {}
        level_columns = {}

        def gather_levels(picked, j0, width):
            nc.vector.tensor_copy(picked[:], levels[:].indirect(listed(j0, width)))
            for u0 in range(0, width, UNIT):
                picked_levels[j0 + u0] = picked[:, u0 : u0 + UNIT]

        def turn_levels(unit):
            for c0 in range(0, UNIT, P):
                j = UNIT * unit + c0
                column = keep.tile([P, 1], F32, name="level_column%d" % j)
                with nc.allow_non_contiguous_dma(reason="a row of levels becomes a column"):
                    nc.sync.dma_start(column[:], picked_levels[UNIT * unit][0:1, c0 : c0 + P])
                level_columns[j] = column[:]

        squares = {}

        def transform_by_frame(j0, width):
            for part in range(2):
                for j in range(j0, j0 + width, P):
                    bank = next_bank(1)
                    for a in range(PASSES):
                        words, plane = frame_operand(j, P, a)
                        nc.tensor.matmul_mx(
                            out=bank[:, 0, :],
                            lhsT=words,
                            lhsT_scale=plane,
                            rhs=w_words[part][:, a, :].bitcast(FP4X4),
                            rhs_scale=w_scales[part][:, a, :],
                            start=(a == 0),
                            stop=(a == PASSES - 1),
                        )
                    square = keep.tile([P, PACK, P], F32, name="square%d_%d" % (j, part))
                    nc.scalar.activation(square[:], bank[:, 0, :].rearrange("p (m t) -> p t m", t=PACK), ACT.Square)
                    squares[j, part] = square

        def transform_by_frequency(j0, width):
            square = keep.tile([P, 2, PACK, width], F32, name="squares%d" % j0)
            per_bank = BANK // width
            if per_bank == 1:
                order = [(t, part) for part in range(2) for t in range(PACK)]
            else:
                order = [(t, part) for t in range(PACK) for part in range(2)]
            for t, part in order:
                if part % per_bank == 0:
                    bank = next_bank(per_bank)
                for a in range(PASSES):
                    words, plane = frame_operand(j0, width, a)
                    nc.tensor.matmul_mx(
                        out=bank[:, part % per_bank, :],
                        lhsT=dealt_words[part][:, a, 2 * P * t : 2 * P * (t + 1)].bitcast(FP4X4),
                        lhsT_scale=dealt_scales[part][:, a, P * t : P * (t + 1)],
                        rhs=words,
                        rhs_scale=plane,
                        start=(a == 0),
                        stop=(a == PASSES - 1),
                    )
                if part % per_bank == per_bank - 1:
                    nc.scalar.activation(
                        square[:, part + 1 - per_bank : part + 1, t, :], bank[:], ACT.Square, scale=root[:, t : t + 1]
                    )
            squares[j0] = square

        def add_by_frame(j0, width):
            rows = keep.tile([P, PACK, width], BF16, name="rows%d" % j0)
            for t in range(PACK):
                bank = next_bank(1)
                for c0 in range(0, width, P):
                    for part in range(2):
                        nc.tensor.matmul(
                            bank[:, 0, c0 : c0 + P], lhsT=squares[j0 + c0, part][:, t, :], rhs=identity[:],
                            is_transpose=True, start=(part == 0), stop=(part == 1),
                        )
                nc.scalar.activation(rows[:, t, :], bank[:, 0, 0:width], ACT.Copy, scale=gain[:, t : t + 1])
            return rows

        quantized = {}

        def quantize(fill, j0, width):
            piece = width // 2
            if j0 in POWER_AT:
                power = late.tile([P, width * PACK], BF16, name="power%d" % j0, align_bytes=64, offset=POWER_AT[j0])
            else:
                power = work.tile([P, width * PACK], BF16, name="power", align_bytes=64)
            codes = keep.tile([P, width], U32, name="codes%d" % j0, align_bytes=64)
            scales = keep.tile([P, width], U8, name="scales%d" % j0, align_bytes=64)
            fill(power, piece)
            for n0 in (0, piece):
                nc.vector.quantize_mx(
                    out=codes[:, n0 : n0 + piece].bitcast(FP8X4),
                    scales=scales[:, n0 : n0 + piece],
                    in_=power[:, PACK * n0 : PACK * (n0 + piece)],
                )
            for u0 in range(0, width, UNIT):
                quantized[(j0 + u0) // UNIT] = codes[:, u0 : u0 + UNIT], scales[:, u0 : u0 + UNIT]

        def quantize_by_frame(rows, j0, width):
            def interleave(power, piece):
                for n0 in (0, piece):
                    nc.gpsimd.tensor_scalar(
                        power[:, PACK * n0 : PACK * (n0 + piece)].rearrange("p (c t) -> p c t", t=PACK),
                        rows[:, :, n0 : n0 + piece].rearrange("p t c -> p c t"),
                        1.0, 0.0, ALU.mult, ALU.add,
                    )

            quantize(interleave, j0, width)

        def quantize_by_frequency(j0, width):
            def add_and_sign(power, piece):
                unsigned = work.tile([P, width * PACK], BF16, name="unsigned", align_bytes=64)
                for n0 in (0, piece):
                    nc.vector.tensor_tensor(
                        unsigned[:, PACK * n0 : PACK * (n0 + piece)].rearrange("p (c i t) -> p c t i", i=4, t=PACK),
                        squares[j0][:, 0, :, n0 : n0 + piece].rearrange("p t (c i) -> p c t i", i=4),
                        squares[j0][:, 1, :, n0 : n0 + piece].rearrange("p t (c i) -> p c t i", i=4),
                        ALU.add,
                    )
                for n0 in (0, piece):
                    cols = slice(PACK * n0, PACK * (n0 + piece))
                    nc.vector.tensor_tensor(
                        power[:, cols].rearrange("p (r c) -> p r c", c=SIGN_COLS),
                        unsigned[:, cols].rearrange("p (r c) -> p r c", c=SIGN_COLS),
                        signs[:].rearrange("p c t -> p (c t)").unsqueeze(1).to_broadcast(
                            [P, piece * PACK // SIGN_COLS, SIGN_COLS]
                        ),
                        ALU.mult,
                    )

            quantize(add_and_sign, j0, width)

        def store(j0, width, result):
            nc.sync.dma_start(out[:, j0 : j0 + width].rearrange("(h p) j -> p h j", p=P), result)

        def filter_direct(unit):
            j0 = UNIT * unit
            codes, scales = quantized[unit]
            width = P if j0 + UNIT == J else UNIT
            for c0 in range(0, UNIT, width):
                result = work.tile([P, N // P, width], F32, name="result", bufs=4)
                bank = next_bank(N // P)
                for half in range(N // P):
                    nc.tensor.matmul_mx(
                        out=bank[:, half, 0:width],
                        lhsT=fb_codes[:, 2 * P * half : 2 * P * (half + 1)].bitcast(FP4X4),
                        lhsT_scale=fb_scale[:, P * half : P * (half + 1)],
                        rhs=codes[:, c0 : c0 + width].bitcast(FP8X4),
                        rhs_scale=scales[:, c0 : c0 + width],
                        start=True,
                        stop=True,
                    )
                nc.vector.tensor_tensor(
                    result[:],
                    bank[:, :, 0:width],
                    picked_levels[j0][:, c0 : c0 + width].unsqueeze(1).to_broadcast([P, N // P, width]),
                    ALU.mult,
                )
                store(j0 + c0, width, result[:])

        scaled = {}

        def filter_turned(unit):
            codes, scales = quantized[unit]
            by_frame = work.tile([P, UNIT // P, N], F32, name="by_frame", bufs=4)
            bank = next_bank(UNIT // P)
            for i in range(UNIT // P):
                cols = slice(P * i, P * (i + 1))
                nc.tensor.matmul_mx(
                    out=bank[:, i, :],
                    lhsT=codes[:, cols].bitcast(FP8X4),
                    lhsT_scale=scales[:, cols],
                    rhs=fb_codes[:].bitcast(FP4X4),
                    rhs_scale=fb_scale[:],
                    start=True,
                    stop=True,
                )
            for i in range(UNIT // P):
                nc.scalar.activation(
                    by_frame[:, i, :], bank[:, i, :], ACT.Copy, scale=level_columns[UNIT * unit + P * i]
                )
            scaled[unit] = by_frame

        def turn_back(unit):
            by_frame = scaled[unit]
            turned = next_bank(N // P)
            for i in range(UNIT // P):
                for half in range(N // P):
                    nc.tensor.transpose(
                        turned[:, half, P * i : P * (i + 1)], by_frame[:, i, P * half : P * (half + 1)], identity[:]
                    )
            result = work.tile([P, N // P, UNIT], F32, name="turned_result", bufs=4)
            nc.scalar.copy(result[:], turned[:])
            store(UNIT * unit, UNIT, result[:])

        deal_words(1)
        gather_words(0)
        part_words(0, UNIT)
        gather_words(CHUNK)
        inverse = chain.tile([P, PACK], F32, name="inverse", offset=INVERSE_AT)
        nc.vector.reciprocal(inverse[:], half_guess[:])
        root = keep.tile([P, PACK], F32, name="root")
        for t in range(PACK):
            column = slice(t, t + 1)
            nc.scalar.activation(
                root[:, column], inverse[:, column], ACT.Identity, bias=half_guess[:, column], scale=quarter[:, column]
            )
        part_words(UNIT, UNIT)
        part_words(CHUNK, CHUNK)
        co_dealt = behind.tile([P, PASSES, F], U8, name="co_dealt", align_bytes=64, offset=SCALE_TABLE_AT)
        deal_scales(co_dealt, 0, nc.gpsimd)
        si_dealt = chain.tile([P, PASSES, F], U8, name="si_dealt", align_bytes=64, offset=SI_DEALT_AT)
        deal_scales(si_dealt, 1, nc.vector)
        gather_words(2 * CHUNK)
        gather_words(3 * CHUNK)
        part_words(2 * CHUNK, CHUNK)
        part_words(3 * CHUNK, CHUNK)
        fb_codes = chain.tile([P, 2 * N], U8, name="fb_codes", offset=FB_CODES_AT, align_bytes=64)
        nc.sync.dma_start(fb_codes[:].bitcast(I32), fb_words[0].bitcast(I32))
        fb_scale = chain.tile([P, N], U8, name="fb_scale", offset=FB_SCALE_AT, align_bytes=64)
        nc.vector.memset(fb_scale[:].bitcast(I32), 0)
        for q in range(QUADS):
            nc.sync.dma_start(
                fb_scale[32 * q : 32 * q + 4, :].bitcast(I32), fb_scales[0, 4 * q : 4 * q + 4, :].bitcast(I32)
            )
        early_levels = keep.tile([P, J // 2], F32, name="early_levels")
        gather_levels(early_levels, 0, J // 2)

        idle = next_bank(1)
        for i in range(WARM_UPS):
            nc.tensor.matmul_mx(
                out=idle[:, 0, :],
                lhsT=dealt_words[0][:, 0, 0 : 2 * P].bitcast(FP4X4),
                lhsT_scale=w_scales[0][:, 0, 0:P],
                rhs=w_words[2 * i // WARM_UPS][:, 0, :].bitcast(FP4X4),
                rhs_scale=w_scales[2 * i // WARM_UPS][:, 0, :],
                start=True,
                stop=True,
            )

        transform_by_frame(0, CHUNK)
        for unit in (2, 3, 0, 1):
            turn_levels(unit)
        for unit in (2, 3, 4, 5):
            transform_by_frequency(unit * UNIT, UNIT)
            quantize_by_frequency(unit * UNIT, UNIT)
        rows = add_by_frame(0, CHUNK)
        late_levels = late.tile([P, J // 2], F32, name="late_levels", align_bytes=64, offset=LATE_LEVELS_AT)
        gather_levels(late_levels, J // 2, J // 2)
        filter_turned(2)
        filter_direct(4)
        filter_direct(5)
        quantize_by_frame(rows, 0, CHUNK)
        transform_by_frequency(6 * UNIT, UNIT)
        turn_back(2)
        transform_by_frequency(7 * UNIT, UNIT)
        quantize_by_frequency(6 * UNIT, UNIT)
        filter_turned(3)
        filter_turned(0)
        turn_back(3)
        filter_turned(1)
        turn_back(0)
        filter_direct(6)
        turn_back(1)
        quantize_by_frequency(7 * UNIT, UNIT)
        filter_direct(7)
